import numpy as np
import ml_dtypes


def mxq(x, axis, fmt="e4m3"):
    dtype, down = {"e4m3": (ml_dtypes.float8_e4m3fn, 7), "e5m2": (ml_dtypes.float8_e5m2, 14)}[fmt]
    v = np.moveaxis(np.asarray(x, np.float32).astype(ml_dtypes.bfloat16).astype(np.float64), axis, -1)
    blocks = v.reshape(v.shape[:-1] + (-1, 32))
    amax = np.abs(blocks).max(-1, keepdims=True)
    byte = np.maximum(np.where(amax > 0, np.frexp(amax)[1] - 1 + 127, 0) - down, 1)
    scale = np.exp2(byte - 127.0)
    codes = (blocks / scale).astype(np.float32).astype(dtype).astype(np.float64)
    return np.moveaxis((codes * scale).reshape(v.shape), -1, axis)


WIDE = False


def mx_kscale(k):
    if not WIDE:
        return np.ones(k)
    levels = np.array([10, -10, 5, -5, 0])
    if k % 512:
        return np.exp2(np.random.permutation(np.resize(levels, k // 32))).repeat(32)
    a = np.empty((k // 512, 16))
    for p in range(k // 512):
        a[p, :8] = np.random.permutation(np.resize(levels, 8))
        for g in range(8):
            far = levels[np.abs(levels - a[p, g]) >= 10]
            a[p, g + 8] = far[np.random.randint(len(far))]
    return np.exp2(a.ravel()).repeat(32)


def f64(x):
    return np.asarray(x).astype(np.float64)


def striped(idx):
    return np.tile(idx.reshape(-1, 16).T, (8, 1)).astype(np.uint16)


def unstriped(offs):
    return offs[:16].T.reshape(-1).astype(np.int64)


E2M1 = np.array([0.0, 0.5, 1.0, 1.5, 2.0, 3.0, 4.0, 6.0, -0.0, -0.5, -1.0, -1.5, -2.0, -3.0, -4.0, -6.0])


def pack_fp4(w):
    k, n = w.shape
    w = f64(np.asarray(w, np.float32).astype(ml_dtypes.bfloat16)).reshape(k // 32, 32, n)
    amax = np.abs(w).max(1)
    mant, ex = np.frexp(amax / 6.0)
    byte = np.clip(np.where(amax > 0, np.where(mant > 0.5, ex, ex - 1) + 127, 1), 1, 254)
    scaled = (w * np.exp2(127.0 - byte)[:, None, :]).reshape(k, n).astype(np.float32)
    c = np.ascontiguousarray(scaled.reshape(k // 512, 128, 4, n).transpose(0, 1, 3, 2)).astype(ml_dtypes.float4_e2m1fn).view(np.uint8) & 0xF
    words = (c[..., 0::2] | (c[..., 1::2] << 4)).reshape(k // 512, 128, 2 * n)
    return np.ascontiguousarray(words), np.ascontiguousarray(byte.astype(np.uint8).reshape(k // 512, 16, n))


def unpack_fp4(words, scales):
    g, _, n = scales.shape
    words = np.ascontiguousarray(words).reshape(g, 128, n, 2)
    nib = np.empty((g, 128, n, 4), np.uint8)
    nib[..., 0::2] = words & 0xF
    nib[..., 1::2] = words >> 4
    vals = E2M1[nib] * np.repeat(np.exp2(scales.astype(np.float64) - 127.0), 8, axis=1)[..., None]
    return vals.transpose(0, 1, 3, 2).reshape(g * 512, n)


def gelu(v):
    return 0.5 * v * (1.0 + np.tanh(np.sqrt(2.0 / np.pi) * (v + 0.044715 * v**3)))


K, T, S, V, H, N = 1024, 1024, 512, 256, 512, 256


def setup_inputs():
    n = np.random.standard_normal
    s = mx_kscale(K)[:, None]
    u = mx_kscale(H)
    packed_xT = pack_fp4(n((K, T)) * s)
    return {
        "x_words": packed_xT[0],
        "x_scales": packed_xT[1],
        "w1": (n((K, H)) / np.sqrt(2 * K) / s * u).astype(np.float32),
        "w2": (n((K, H)) / np.sqrt(2 * K) / s * u).astype(np.float32),
        "w3": (n((H, N)) / np.sqrt(H) / u[:, None]).astype(np.float32),
        "offs": striped(np.random.permutation(T)[:S]),
        "cen": striped(np.random.permutation(S)[:V]),
        "pos1": striped(np.random.permutation(S)[:V]),
        "pos2": striped(np.random.permutation(S)[:V]),
        "pos3": striped(np.random.permutation(S)[:V]),
        "pos4": striped(np.random.permutation(S)[:V]),
    }


def reference(x_words, x_scales, w1, w2, w3, offs, cen, pos1, pos2, pos3, pos4):
    xq = unpack_fp4(x_words, x_scales)[:, unstriped(offs)]
    y = mxq(f64(w1), 0, "e4m3").T @ xq
    yc = y[:, unstriped(cen)]
    e = mxq(f64(w2), 0, "e4m3").T @ xq
    z = np.maximum(np.maximum(np.maximum(gelu(yc + e[:, unstriped(pos1)]), gelu(yc + e[:, unstriped(pos2)])), gelu(yc + e[:, unstriped(pos3)])), gelu(yc + e[:, unstriped(pos4)]))
    return mxq(f64(w3), 0, "e4m3").T @ mxq(z, 0, "e4m3")

@@ -1,0 +1,215 @@
+from contextlib import ExitStack
+
+import concourse.mybir as mybir
+from concourse.masks import make_identity
+
+K, T, S, V, H, N = 1024, 1024, 512, 256, 512, 256
+D = 4
+FLOPS = 2 * (2 * K * H * S + H * N * V)
+
+F32 = mybir.dt.float32
+BF16 = mybir.dt.bfloat16
+I32 = mybir.dt.int32
+U32 = mybir.dt.uint32
+U16 = mybir.dt.uint16
+U8 = mybir.dt.uint8
+FP8X4 = mybir.dt.float8_e4m3fn_x4
+FP4X4 = mybir.dt.float4_e2m1fn_x4
+GELU = mybir.ActivationFunctionType.Gelu_apprx_tanh
+MAX = mybir.AluOpType.max
+
+P = 128
+PACK = 4
+K_PASS = P * PACK
+PASSES = K // K_PASS
+CHUNK = 256
+
+
+def tile_picked_edgecv_gelu_p_kernel(
+    tc, x_words, x_scales, w1, w2, w3, offs, cen, pos1, pos2, pos3, pos4, out
+):
+    nc = tc.nc
+    with ExitStack() as ctx:
+        sb = ctx.enter_context(tc.tile_pool(name="sb", bufs=1))
+        ps = ctx.enter_context(tc.psum_pool(name="ps", bufs=1))
+
+        def load_list(src, name):
+            t = sb.tile(list(src.shape), U16, name=name)
+            nc.sync.dma_start(t[:], src)
+            return t
+
+        def load_weights(w, g, c, name):
+            raw = sb.tile([P, PACK, CHUNK], F32, name=name)
+            rows = w[g * K_PASS : (g + 1) * K_PASS, c * CHUNK : (c + 1) * CHUNK]
+            nc.sync.dma_start(raw[:], rows.rearrange("(p j) c -> p j c", j=PACK))
+            return raw
+
+        def cast(raw, name, on_vector):
+            grouped = sb.tile([P, CHUNK * PACK], BF16, name=name, align_bytes=64)
+            dst = grouped[:].rearrange("p (c i j) -> p c j i", i=4, j=PACK)
+            src = raw[:].rearrange("p j (c i) -> p c j i", i=4)
+            if on_vector:
+                nc.vector.tensor_copy(dst, src)
+            else:
+                nc.scalar.copy(dst, src)
+            return grouped
+
+        def quantize(grouped, name):
+            width = grouped.shape[1] // PACK
+            codes = sb.tile([P, width], U32, name=name + "_codes", align_bytes=64)
+            scales = sb.tile([P, width], U8, name=name + "_scales", align_bytes=64)
+            nc.vector.quantize_mx(out=codes[:].bitcast(FP8X4), scales=scales[:], in_=grouped[:])
+            return codes, scales
+
+        xs = sb.tile([P, PASSES, T], U8, name="xs")
+        nc.vector.memset(xs[:].rearrange("p g c -> p (g c)").bitcast(I32), 0)
+        warm = sb.tile([P, 1], F32, name="warm")
+        nc.vector.memset(warm[:], 0.0)
+        warm_out = sb.tile([P, 1], F32, name="warm_out")
+        nc.scalar.activation(warm_out[:], warm[:], GELU)
+        ident = sb.tile([P, P], F32, name="ident")
+        make_identity(nc, ident[:])
+
+        offs_t = load_list(offs, "offs_t")
+        xw = []
+        for g in range(PASSES):
+            t = sb.tile([P, T], U16, name="xw%d" % g)
+            nc.sync.dma_start(t[:].bitcast(I32), x_words[g].bitcast(I32))
+            xw.append(t)
+            if g == 0:
+                for q in range(4):
+                    nc.sync.dma_start(
+                        xs[32 * q : 32 * q + 4, :, :].bitcast(I32),
+                        x_scales[:, 4 * q : 4 * q + 4, :].rearrange("g r c -> r g c").bitcast(I32),
+                    )
+        raw = {}
+        for g in range(PASSES):
+            raw["e", 0, g] = load_weights(w2, g, 0, "raw_e0%d" % g)
+        pos_t = [load_list(src, "pos%d_t" % d) for d, src in enumerate((pos1, pos2, pos3, pos4))]
+        for g in range(PASSES):
+            raw["y", 0, g] = load_weights(w1, g, 0, "raw_y0%d" % g)
+        cen_t = load_list(cen, "cen_t")
+        for g in range(PASSES):
+            raw["y", 1, g] = load_weights(w1, g, 1, "raw_y1%d" % g)
+        for g in range(PASSES):
+            raw["e", 1, g] = load_weights(w2, g, 1, "raw_e1%d" % g)
+        raw3 = load_weights(w3, 0, 0, "raw3")
+
+        xw_p, xs_p = [], []
+        for g in range(PASSES):
+            words = sb.tile([P, S], U16, name="xw_p%d" % g, align_bytes=64)
+            nc.vector.tensor_copy(words[:], xw[g][:].indirect(offs_t[:]))
+            xw_p.append(words)
+            scales = sb.tile([P, S], U8, name="xs_p%d" % g, align_bytes=64)
+            nc.vector.tensor_copy(scales[:], xs[:, g, :].indirect(offs_t[:]))
+            xs_p.append(scales)
+
+        rows = {}
+
+        def first_product(kind, c, vector_casts):
+            quant = []
+            for g in range(PASSES):
+                name = "%s%d%d" % (kind, c, g)
+                grouped = cast(raw[kind, c, g], "grp_" + name, g in vector_casts)
+                quant.append(quantize(grouped, name))
+            for tt in range(2):
+                acc = ps.tile([P, S], F32, name="acc", tag="acc", bufs=3)
+                cols = slice(tt * P, (tt + 1) * P)
+                for g in range(PASSES):
+                    codes, scales = quant[g]
+                    nc.tensor.matmul_mx(
+                        out=acc[:],
+                        lhsT=codes[:, cols].bitcast(FP8X4),
+                        lhsT_scale=scales[:, cols],
+                        rhs=xw_p[g][:].bitcast(FP4X4),
+                        rhs_scale=xs_p[g][:],
+                        start=(g == 0),
+                        stop=(g == PASSES - 1),
+                    )
+                row = sb.tile([P, S], F32, name="row_%s%d" % (kind, 2 * c + tt))
+                nc.scalar.copy(row[:], acc[:])
+                rows[kind, 2 * c + tt] = row
+
+        got = {}
+
+        def gather(kind, t, d, lst):
+            g_t = sb.tile([P, V], F32, name="got_%s%d%d" % (kind, t, d))
+            nc.vector.tensor_copy(g_t[:], rows[kind, t][:].indirect(lst[:]))
+            got[kind, t, d] = g_t
+
+        z_all = sb.tile([P, 2, 2, 4, 64], BF16, name="z_all")
+        acts = {}
+
+        def edges(t, pair):
+            bank = ps.tile([P, 2, 2, P], F32, name="bank", tag="bank", bufs=4)
+            for dd in range(2):
+                for half in range(2):
+                    vs = slice(half * P, (half + 1) * P)
+                    nc.tensor.matmul(bank[:, half, dd, :], got["y", t, 0][:, vs], ident[:], start=True, stop=False, is_transpose=True)
+                    nc.tensor.matmul(bank[:, half, dd, :], got["e", t, 2 * pair + dd][:, vs], ident[:], start=False, stop=True, is_transpose=True)
+            act = sb.tile([P, 4 * P], BF16, name="act%d%d" % (t, pair))
+            nc.scalar.activation(
+                act[:].rearrange("p (u q b) -> p u q b", u=2, b=2),
+                bank[:].rearrange("p h d (q u b) -> p u (h d q) b", u=2, b=2),
+                GELU,
+            )
+            acts[t, pair] = act
+
+        def largest(t):
+            m = sb.tile([P, 4, 2, 64], BF16, name="m%d" % t)
+            nc.vector.tensor_tensor(m[:].rearrange("p a d c -> p (a d c)"), acts[t, 0][:], acts[t, 1][:], MAX)
+            nc.vector.tensor_tensor(
+                z_all[:].rearrange("p u h t c -> p (u h) t c")[:, :, t, :], m[:, :, 0, :], m[:, :, 1, :], MAX
+            )
+
+        first_product("e", 0, ())
+        first_product("y", 0, (0,))
+        for t in range(2):
+            for d in range(D):
+                gather("e", t, d, pos_t[d])
+        for t in range(2):
+            gather("y", t, 0, cen_t)
+        first_product("y", 1, ())
+        for pair in range(2):
+            edges(0, pair)
+        first_product("e", 1, ())
+        for pair in range(2):
+            edges(1, pair)
+        for t in range(2, 4):
+            gather("y", t, 0, cen_t)
+        largest(0)
+        w3_codes, w3_scales = quantize(cast(raw3, "grp3", False), "w3")
+        for t in range(2, 4):
+            for pair in range(2):
+                for dd in range(2):
+                    gather("e", t, 2 * pair + dd, pos_t[2 * pair + dd])
+                edges(t, pair)
+            largest(t - 1)
+        largest(3)
+
+        zt = ps.tile([P, 2, V], F32, name="zt")
+        z_words = z_all[:].rearrange("p u h t c -> p u h (t c)").bitcast(F32)
+        for half in range(2):
+            for u in range(2):
+                nc.tensor.transpose(zt[:, u, half * P : (half + 1) * P], z_words[:, u, half, :], ident[:])
+        zg = sb.tile([P, V * PACK], BF16, name="zg", align_bytes=64)
+        nc.scalar.copy(zg[:].bitcast(F32).rearrange("p (v u) -> p v u", u=2), zt[:].rearrange("p u v -> p v u"))
+        z_codes, z_scales = quantize(zg, "z")
+        for mt in range(N // P):
+            acc = ps.tile([P, S], F32, name="acc", tag="acc", bufs=3)
+            cols = slice(mt * P, (mt + 1) * P)
+            nc.tensor.matmul_mx(
+                out=acc[:, 0:V],
+                lhsT=w3_codes[:, cols].bitcast(FP8X4),
+                lhsT_scale=w3_scales[:, cols],
+                rhs=z_codes[:].bitcast(FP8X4),
+                rhs_scale=z_scales[:],
+                start=True,
+                stop=True,
+            )
+            res = sb.tile([P, V], F32, name="res%d" % mt)
+            if mt == 0:
+                nc.vector.tensor_copy(res[:], acc[:, 0:V])
+            else:
+                nc.scalar.copy(res[:], acc[:, 0:V])
+            nc.sync.dma_start(out[cols, :], res[:])

@@ -39,13 +39,13 @@ def tile_picked_edgecv_gelu_p_kernel(
             return t
 
         def load_weights(w, g, c, name):
-            raw = sb.tile([P, PACK, CHUNK], F32, name=name)
+            raw = sb.tile([P, PACK, CHUNK], F32, name=name, tag=name, align_bytes=64)
             rows = w[g * K_PASS : (g + 1) * K_PASS, c * CHUNK : (c + 1) * CHUNK]
             nc.sync.dma_start(raw[:], rows.rearrange("(p j) c -> p j c", j=PACK))
             return raw
 
         def cast(raw, name, on_vector):
-            grouped = sb.tile([P, CHUNK * PACK], BF16, name=name, align_bytes=64)
+            grouped = sb.tile([P, CHUNK * PACK], BF16, name=name, tag=name, align_bytes=64)
             dst = grouped[:].rearrange("p (c i j) -> p c j i", i=4, j=PACK)
             src = raw[:].rearrange("p j (c i) -> p c j i", i=4)
             if on_vector:
@@ -62,7 +62,7 @@ def tile_picked_edgecv_gelu_p_kernel(
             return codes, scales
 
         xs = sb.tile([P, PASSES, T], U8, name="xs")
-        nc.vector.memset(xs[:].rearrange("p g c -> p (g c)").bitcast(I32), 0)
+        nc.gpsimd.memset(xs[:].rearrange("p g c -> p (g c)").bitcast(I32), 0)
         warm = sb.tile([P, 1], F32, name="warm")
         nc.vector.memset(warm[:], 0.0)
         warm_out = sb.tile([P, 1], F32, name="warm_out")
@@ -71,24 +71,21 @@ def tile_picked_edgecv_gelu_p_kernel(
         make_identity(nc, ident[:])
 
         offs_t = load_list(offs, "offs_t")
-        xw = []
-        for g in range(PASSES):
-            t = sb.tile([P, T], U16, name="xw%d" % g)
-            nc.sync.dma_start(t[:].bitcast(I32), x_words[g].bitcast(I32))
-            xw.append(t)
-            if g == 0:
-                for q in range(4):
-                    nc.sync.dma_start(
-                        xs[32 * q : 32 * q + 4, :, :].bitcast(I32),
-                        x_scales[:, 4 * q : 4 * q + 4, :].rearrange("g r c -> r g c").bitcast(I32),
-                    )
+        xw = [sb.tile([P, T], U16, name="xw%d" % g) for g in range(PASSES)]
         raw = {}
-        for g in range(PASSES):
-            raw["e", 0, g] = load_weights(w2, g, 0, "raw_e0%d" % g)
-        pos_t = [load_list(src, "pos%d_t" % d) for d, src in enumerate((pos1, pos2, pos3, pos4))]
+        nc.sync.dma_start(xw[0][:].bitcast(I32), x_words[0].bitcast(I32))
+        for q in range(4):
+            nc.sync.dma_start(
+                xs[32 * q : 32 * q + 4, :, :].bitcast(I32),
+                x_scales[:, 4 * q : 4 * q + 4, :].rearrange("g r c -> r g c").bitcast(I32),
+            )
+        raw["e", 0, 0] = load_weights(w2, 0, 0, "raw_e00")
+        nc.sync.dma_start(xw[1][:].bitcast(I32), x_words[1].bitcast(I32))
+        raw["e", 0, 1] = load_weights(w2, 1, 0, "raw_e01")
+        cen_t = load_list(cen, "cen_t")
         for g in range(PASSES):
             raw["y", 0, g] = load_weights(w1, g, 0, "raw_y0%d" % g)
-        cen_t = load_list(cen, "cen_t")
+        pos_t = [load_list(src, "pos%d_t" % d) for d, src in enumerate((pos1, pos2, pos3, pos4))]
         for g in range(PASSES):
             raw["y", 1, g] = load_weights(w1, g, 1, "raw_y1%d" % g)
         for g in range(PASSES):
@@ -104,53 +101,71 @@ def tile_picked_edgecv_gelu_p_kernel(
             nc.vector.tensor_copy(scales[:], xs[:, g, :].indirect(offs_t[:]))
             xs_p.append(scales)
 
-        rows = {}
+        quant, accs, rows, got, banks, acts = {}, {}, {}, {}, {}, {}
 
-        def first_product(kind, c, vector_casts):
-            quant = []
+        grouped = {}
+
+        def round_weights(kind, c, g, on_vector=False):
+            grouped[kind, c, g] = cast(raw[kind, c, g], "grp_%s%d%d" % (kind, c, g), on_vector)
+
+        def quantize_weights(kind, c, g):
+            quant[kind, c, g] = quantize(grouped[kind, c, g], "%s%d%d" % (kind, c, g))
+
+        def product(kind, t, tag):
+            acc = ps.tile([P, S], F32, name="acc", tag=tag)
+            cols = slice((t % 2) * P, (t % 2 + 1) * P)
             for g in range(PASSES):
-                name = "%s%d%d" % (kind, c, g)
-                grouped = cast(raw[kind, c, g], "grp_" + name, g in vector_casts)
-                quant.append(quantize(grouped, name))
-            for tt in range(2):
-                acc = ps.tile([P, S], F32, name="acc", tag="acc", bufs=3)
-                cols = slice(tt * P, (tt + 1) * P)
-                for g in range(PASSES):
-                    codes, scales = quant[g]
-                    nc.tensor.matmul_mx(
-                        out=acc[:],
-                        lhsT=codes[:, cols].bitcast(FP8X4),
-                        lhsT_scale=scales[:, cols],
-                        rhs=xw_p[g][:].bitcast(FP4X4),
-                        rhs_scale=xs_p[g][:],
-                        start=(g == 0),
-                        stop=(g == PASSES - 1),
-                    )
-                row = sb.tile([P, S], F32, name="row_%s%d" % (kind, 2 * c + tt))
-                nc.scalar.copy(row[:], acc[:])
-                rows[kind, 2 * c + tt] = row
+                codes, scales = quant[kind, t // 2, g]
+                nc.tensor.matmul_mx(
+                    out=acc[:],
+                    lhsT=codes[:, cols].bitcast(FP8X4),
+                    lhsT_scale=scales[:, cols],
+                    rhs=xw_p[g][:].bitcast(FP4X4),
+                    rhs_scale=xs_p[g][:],
+                    start=(g == 0),
+                    stop=(g == PASSES - 1),
+                )
+            accs[kind, t] = acc
 
-        got = {}
+        def evacuate(kind, t, on_vector=False, reuse=None):
+            name = "row_%s%d" % (kind, t)
+            row = sb.tile([P, S], F32, name=name, tag=reuse or name, align_bytes=64)
+            if on_vector:
+                nc.vector.tensor_copy(row[:], accs[kind, t][:])
+            else:
+                nc.scalar.copy(row[:], accs[kind, t][:])
+            rows[kind, t] = row
 
-        def gather(kind, t, d, lst):
-            g_t = sb.tile([P, V], F32, name="got_%s%d%d" % (kind, t, d))
-            nc.vector.tensor_copy(g_t[:], rows[kind, t][:].indirect(lst[:]))
-            got[kind, t, d] = g_t
+        def gather_centres(t, reuse=None):
+            name = "got_y%d" % t
+            g_t = sb.tile([P, V], F32, name=name, tag=reuse or name, align_bytes=64)
+            nc.vector.tensor_copy(g_t[:], rows["y", t][:].indirect(cen_t[:]))
+            got["y", t, 0] = g_t[:]
+
+        def gather_neighbours(t, ds, reuse=None):
+            name = "got_e%d%d" % (t, ds[0])
+            g_t = sb.tile([P, len(ds), V], F32, name=name, tag=reuse or name, align_bytes=64)
+            for i, d in enumerate(ds):
+                nc.vector.tensor_copy(g_t[:, i, :], rows["e", t][:].indirect(pos_t[d][:]))
+                got["e", t, d] = g_t[:, i, :]
 
         z_all = sb.tile([P, 2, 2, 4, 64], BF16, name="z_all")
-        acts = {}
 
-        def edges(t, pair):
+        def edge_sums(t, pair):
             bank = ps.tile([P, 2, 2, P], F32, name="bank", tag="bank", bufs=4)
             for dd in range(2):
                 for half in range(2):
                     vs = slice(half * P, (half + 1) * P)
                     nc.tensor.matmul(bank[:, half, dd, :], got["y", t, 0][:, vs], ident[:], start=True, stop=False, is_transpose=True)
                     nc.tensor.matmul(bank[:, half, dd, :], got["e", t, 2 * pair + dd][:, vs], ident[:], start=False, stop=True, is_transpose=True)
-            act = sb.tile([P, 4 * P], BF16, name="act%d%d" % (t, pair))
+            banks[t, pair] = bank
+
+        def gelu(t, pair, reuse=None):
+            name = "act%d%d" % (t, pair)
+            act = sb.tile([P, 4 * P], BF16, name=name, tag=reuse or name, align_bytes=64)
             nc.scalar.activation(
                 act[:].rearrange("p (u q b) -> p u q b", u=2, b=2),
-                bank[:].rearrange("p h d (q u b) -> p u (h d q) b", u=2, b=2),
+                banks[t, pair][:].rearrange("p h d (q u b) -> p u (h d q) b", u=2, b=2),
                 GELU,
             )
             acts[t, pair] = act
@@ -162,41 +177,104 @@ def tile_picked_edgecv_gelu_p_kernel(
                 z_all[:].rearrange("p u h t c -> p (u h) t c")[:, :, t, :], m[:, :, 0, :], m[:, :, 1, :], MAX
             )
 
-        first_product("e", 0, ())
-        first_product("y", 0, (0,))
-        for t in range(2):
-            for d in range(D):
-                gather("e", t, d, pos_t[d])
-        for t in range(2):
-            gather("y", t, 0, cen_t)
-        first_product("y", 1, ())
+        for g in range(PASSES):
+            round_weights("e", 0, g)
+            quantize_weights("e", 0, g)
+        product("e", 0, "acc0")
+        round_weights("y", 0, 0)
+        quantize_weights("y", 0, 0)
+        evacuate("e", 0, True, reuse="grp_y00")
+        round_weights("y", 0, 1)
+        quantize_weights("y", 0, 1)
+        gather_neighbours(0, (0, 1, 2, 3), "grp_y01")
+        product("y", 0, "acc1")
+        product("y", 1, "acc2")
+        product("e", 1, "acc0")
+        round_weights("y", 1, 0)
+        round_weights("y", 1, 1)
+        evacuate("y", 0, reuse="raw_y11")
+        evacuate("y", 1)
+        evacuate("e", 1, reuse="raw_y10")
+        quantize_weights("y", 1, 0)
+        quantize_weights("y", 1, 1)
+        gather_centres(0)
+        gather_centres(1)
+        product("y", 2, "acc1")
+        product("y", 3, "acc2")
+        round_weights("e", 1, 0)
+        round_weights("e", 1, 1)
         for pair in range(2):
-            edges(0, pair)
-        first_product("e", 1, ())
+            edge_sums(0, pair)
+        gather_neighbours(1, (0, 1))
+        quantize_weights("e", 1, 0)
+        quantize_weights("e", 1, 1)
+        gather_neighbours(1, (2, 3), "grp_e11")
+        evacuate("y", 2)
+        evacuate("y", 3)
+        product("e", 2, "acc0")
+        product("e", 3, "acc1")
         for pair in range(2):
-            edges(1, pair)
+            edge_sums(1, pair)
         for t in range(2, 4):
-            gather("y", t, 0, cen_t)
+            gather_centres(t)
+        for pair in range(2):
+            gelu(0, pair)
+        evacuate("e", 2)
+        for pair in range(2):
+            gelu(1, pair)
+        evacuate("e", 3)
+        w3_grouped = cast(raw3, "grp3", False)
+        gather_neighbours(2, (0, 1))
+        edge_sums(2, 0)
+        gelu(2, 0)
         largest(0)
-        w3_codes, w3_scales = quantize(cast(raw3, "grp3", False), "w3")
-        for t in range(2, 4):
-            for pair in range(2):
-                for dd in range(2):
-                    gather("e", t, 2 * pair + dd, pos_t[2 * pair + dd])
-                edges(t, pair)
-            largest(t - 1)
-        largest(3)
+        gather_neighbours(2, (2, 3), "act00")
+        edge_sums(2, 1)
+        gelu(2, 1)
+        largest(1)
+        w3_codes, w3_scales = quantize(w3_grouped, "w3")
+        gather_neighbours(3, (0, 1), "grp3")
+        edge_sums(3, 0)
+        gelu(3, 0)
+        largest(2)
+        last = []
+        for d in (2, 3):
+            gather_neighbours(3, (d,), "act2%d" % (d - 2))
+            bank = ps.tile([P, 2, P], F32, name="bank", tag="bank", bufs=4)
+            for half in range(2):
+                vs = slice(half * P, (half + 1) * P)
+                nc.tensor.matmul(bank[:, half, :], got["y", 3, 0][:, vs], ident[:], start=(half == 0), stop=False, is_transpose=True)
+            for half in range(2):
+                vs = slice(half * P, (half + 1) * P)
+                nc.tensor.matmul(bank[:, half, :], got["e", 3, d][:, vs], ident[:], start=False, stop=(half == 1), is_transpose=True)
+            act = sb.tile([P, 4, 64], BF16, name="act_last%d" % d)
+            nc.scalar.activation(
+                act[:].rearrange("p (u h) (q b) -> p u (h q) b", u=2, b=2),
+                bank[:].rearrange("p h (q u b) -> p u (h q) b", u=2, b=2),
+                GELU,
+            )
+            last.append(act)
+        a01 = acts[3, 0][:].rearrange("p (a d c) -> p a d c", d=2, c=64)
+        m01 = sb.tile([P, 4, 64], BF16, name="m01")
+        nc.vector.tensor_tensor(m01[:], a01[:, :, 0, :], a01[:, :, 1, :], MAX)
+        m012 = sb.tile([P, 4, 64], BF16, name="m012")
+        nc.vector.tensor_tensor(m012[:], m01[:], last[0][:], MAX)
+        nc.vector.tensor_tensor(z_all[:].rearrange("p u h t c -> p (u h) t c")[:, :, 3, :], m012[:], last[1][:], MAX)
 
-        zt = ps.tile([P, 2, V], F32, name="zt")
         z_words = z_all[:].rearrange("p u h t c -> p u h (t c)").bitcast(F32)
-        for half in range(2):
-            for u in range(2):
-                nc.tensor.transpose(zt[:, u, half * P : (half + 1) * P], z_words[:, u, half, :], ident[:])
         zg = sb.tile([P, V * PACK], BF16, name="zg", align_bytes=64)
-        nc.scalar.copy(zg[:].bitcast(F32).rearrange("p (v u) -> p v u", u=2), zt[:].rearrange("p u v -> p v u"))
+        for half in range(2):
+            zt = ps.tile([P, 2, P], F32, name="zt", tag=("zt", "acc2")[half])
+            for u in range(2):
+                nc.tensor.transpose(zt[:, u, :], z_words[:, u, half, :], ident[:])
+            dst = zg[:, half * 512 : (half + 1) * 512].bitcast(F32).rearrange("p (v u) -> p v u", u=2)
+            if half == 0:
+                nc.scalar.copy(dst, zt[:].rearrange("p u v -> p v u"))
+            else:
+                nc.vector.tensor_copy(dst, zt[:].rearrange("p u v -> p v u"))
         z_codes, z_scales = quantize(zg, "z")
         for mt in range(N // P):
-            acc = ps.tile([P, S], F32, name="acc", tag="acc", bufs=3)
+            acc = ps.tile([P, S], F32, name="acc", tag="acc%d" % mt)
             cols = slice(mt * P, (mt + 1) * P)
             nc.tensor.matmul_mx(
                 out=acc[:, 0:V],

@@ -23,6 +23,7 @@ PACK = 4
 K_PASS = P * PACK
 PASSES = K // K_PASS
 CHUNK = 256
+ROW = 4 * S
 
 
 def tile_picked_edgecv_gelu_p_kernel(
@@ -31,6 +32,7 @@ def tile_picked_edgecv_gelu_p_kernel(
     nc = tc.nc
     with ExitStack() as ctx:
         sb = ctx.enter_context(tc.tile_pool(name="sb", bufs=1))
+        shared = ctx.enter_context(tc.tile_pool(name="shared", bufs=1))
         ps = ctx.enter_context(tc.psum_pool(name="ps", bufs=1))
 
         def load_list(src, name):
@@ -38,8 +40,11 @@ def tile_picked_edgecv_gelu_p_kernel(
             nc.sync.dma_start(t[:], src)
             return t
 
-        def load_weights(w, g, c, name):
-            raw = sb.tile([P, PACK, CHUNK], F32, name=name, tag=name, align_bytes=64)
+        def load_weights(w, g, c, name, offset=None):
+            if offset is None:
+                raw = sb.tile([P, PACK, CHUNK], F32, name=name, tag=name, align_bytes=64)
+            else:
+                raw = shared.tile([P, PACK, CHUNK], F32, name=name, offset=offset)
             rows = w[g * K_PASS : (g + 1) * K_PASS, c * CHUNK : (c + 1) * CHUNK]
             nc.sync.dma_start(raw[:], rows.rearrange("(p j) c -> p j c", j=PACK))
             return raw
@@ -67,30 +72,34 @@ def tile_picked_edgecv_gelu_p_kernel(
         nc.vector.memset(warm[:], 0.0)
         warm_out = sb.tile([P, 1], F32, name="warm_out")
         nc.scalar.activation(warm_out[:], warm[:], GELU)
-        ident = sb.tile([P, P], F32, name="ident")
-        make_identity(nc, ident[:])
 
-        offs_t = load_list(offs, "offs_t")
         xw = [sb.tile([P, T], U16, name="xw%d" % g) for g in range(PASSES)]
-        raw = {}
+        raw, pos_t = {}, {}
+        offs_t = load_list(offs, "offs_t")
         nc.sync.dma_start(xw[0][:].bitcast(I32), x_words[0].bitcast(I32))
+        cen_t = load_list(cen, "cen_t")
+        pos_t[0] = load_list(pos1, "pos0_t")
+        nc.sync.dma_start(xw[1][:].bitcast(I32), x_words[1].bitcast(I32))
+        raw["e", 0, 0] = load_weights(w2, 0, 0, "raw_e00")
         for q in range(4):
             nc.sync.dma_start(
                 xs[32 * q : 32 * q + 4, :, :].bitcast(I32),
                 x_scales[:, 4 * q : 4 * q + 4, :].rearrange("g r c -> r g c").bitcast(I32),
             )
-        raw["e", 0, 0] = load_weights(w2, 0, 0, "raw_e00")
-        nc.sync.dma_start(xw[1][:].bitcast(I32), x_words[1].bitcast(I32))
         raw["e", 0, 1] = load_weights(w2, 1, 0, "raw_e01")
-        cen_t = load_list(cen, "cen_t")
-        for g in range(PASSES):
-            raw["y", 0, g] = load_weights(w1, g, 0, "raw_y0%d" % g)
-        pos_t = [load_list(src, "pos%d_t" % d) for d, src in enumerate((pos1, pos2, pos3, pos4))]
-        for g in range(PASSES):
-            raw["y", 1, g] = load_weights(w1, g, 1, "raw_y1%d" % g)
-        for g in range(PASSES):
-            raw["e", 1, g] = load_weights(w2, g, 1, "raw_e1%d" % g)
+        raw["y", 0, 0] = load_weights(w1, 0, 0, "raw_y00")
+        raw["y", 0, 1] = load_weights(w1, 1, 0, "raw_y01")
+        raw["y", 1, 0] = load_weights(w1, 0, 1, "raw_y10")
+        pos_t[1] = load_list(pos2, "pos1_t")
+        pos_t[2] = load_list(pos3, "pos2_t")
+        pos_t[3] = load_list(pos4, "pos3_t")
+        raw["y", 1, 1] = load_weights(w1, 1, 1, "raw_y11", ROW // 2)
+        raw["e", 1, 0] = load_weights(w2, 0, 1, "raw_e10")
+        raw["e", 1, 1] = load_weights(w2, 1, 1, "raw_e11", 3 * ROW + ROW // 2)
         raw3 = load_weights(w3, 0, 0, "raw3")
+
+        ident = sb.tile([P, P], F32, name="ident")
+        make_identity(nc, ident[:])
 
         xw_p, xs_p = [], []
         for g in range(PASSES):
@@ -101,7 +110,7 @@ def tile_picked_edgecv_gelu_p_kernel(
             nc.vector.tensor_copy(scales[:], xs[:, g, :].indirect(offs_t[:]))
             xs_p.append(scales)
 
-        quant, accs, rows, got, banks, acts = {}, {}, {}, {}, {}, {}
+        quant, accs, rows, got, banks = {}, {}, {}, {}, {}
 
         grouped = {}
 
@@ -127,9 +136,12 @@ def tile_picked_edgecv_gelu_p_kernel(
                 )
             accs[kind, t] = acc
 
-        def evacuate(kind, t, on_vector=False, reuse=None):
+        def evacuate(kind, t, on_vector=False, reuse=None, offset=None):
             name = "row_%s%d" % (kind, t)
-            row = sb.tile([P, S], F32, name=name, tag=reuse or name, align_bytes=64)
+            if offset is None:
+                row = sb.tile([P, S], F32, name=name, tag=reuse or name, align_bytes=64)
+            else:
+                row = shared.tile([P, S], F32, name=name, offset=offset)
             if on_vector:
                 nc.vector.tensor_copy(row[:], accs[kind, t][:])
             else:
@@ -149,145 +161,175 @@ def tile_picked_edgecv_gelu_p_kernel(
                 nc.vector.tensor_copy(g_t[:, i, :], rows["e", t][:].indirect(pos_t[d][:]))
                 got["e", t, d] = g_t[:, i, :]
 
-        z_all = sb.tile([P, 2, 2, 4, 64], BF16, name="z_all")
+        z_all = sb.tile([P, 2 * H], BF16, name="z_all")
 
-        def edge_sums(t, pair):
-            bank = ps.tile([P, 2, 2, P], F32, name="bank", tag="bank", bufs=4)
-            for dd in range(2):
-                for half in range(2):
-                    vs = slice(half * P, (half + 1) * P)
-                    nc.tensor.matmul(bank[:, half, dd, :], got["y", t, 0][:, vs], ident[:], start=True, stop=False, is_transpose=True)
-                    nc.tensor.matmul(bank[:, half, dd, :], got["e", t, 2 * pair + dd][:, vs], ident[:], start=False, stop=True, is_transpose=True)
+        slots = [(half, dd) for dd in range(2) for half in range(2)]
+
+        def turn(bank, half, dd, src, first, last):
+            nc.tensor.matmul(
+                bank[:, half, dd, :], src[:, half * P : (half + 1) * P], ident[:], start=first, stop=last, is_transpose=True
+            )
+
+        def add_neighbours(t, pair, tag):
+            bank = ps.tile([P, 2, 2, P], F32, name="bank", tag=tag)
             banks[t, pair] = bank
+            for i, (half, dd) in enumerate(slots):
+                turn(bank, half, dd, got["e", t, 2 * pair + dd], i == 0, False)
 
-        def gelu(t, pair, reuse=None):
-            name = "act%d%d" % (t, pair)
-            act = sb.tile([P, 4 * P], BF16, name=name, tag=reuse or name, align_bytes=64)
+        def add_centres(t, pair):
+            for i, (half, dd) in enumerate(slots):
+                turn(banks[t, pair], half, dd, got["y", t, 0], False, i == 3)
+
+        def edge_sums(t, pair, tag):
+            bank = ps.tile([P, 2, 2, P], F32, name="bank", tag=tag)
+            banks[t, pair] = bank
+            for i, (half, dd) in enumerate(slots):
+                turn(bank, half, dd, got["y", t, 0], i == 0, False)
+            for i, (half, dd) in enumerate(slots):
+                turn(bank, half, dd, got["e", t, 2 * pair + dd], False, i == 3)
+
+        def gelu(t, pair, act):
             nc.scalar.activation(
-                act[:].rearrange("p (u q b) -> p u q b", u=2, b=2),
+                act.rearrange("p (u q b) -> p u q b", u=2, b=2),
                 banks[t, pair][:].rearrange("p h d (q u b) -> p u (h d q) b", u=2, b=2),
                 GELU,
             )
-            acts[t, pair] = act
 
-        def largest(t):
-            m = sb.tile([P, 4, 2, 64], BF16, name="m%d" % t)
-            nc.vector.tensor_tensor(m[:].rearrange("p a d c -> p (a d c)"), acts[t, 0][:], acts[t, 1][:], MAX)
-            nc.vector.tensor_tensor(
-                z_all[:].rearrange("p u h t c -> p (u h) t c")[:, :, t, :], m[:, :, 0, :], m[:, :, 1, :], MAX
-            )
+        z_blocks = z_all[:].rearrange("p (h u t c) -> p u h t c", h=2, u=2, t=4)
 
         for g in range(PASSES):
             round_weights("e", 0, g)
             quantize_weights("e", 0, g)
-        product("e", 0, "acc0")
+        product("e", 0, "bank0")
         round_weights("y", 0, 0)
         quantize_weights("y", 0, 0)
         evacuate("e", 0, True, reuse="grp_y00")
         round_weights("y", 0, 1)
         quantize_weights("y", 0, 1)
         gather_neighbours(0, (0, 1, 2, 3), "grp_y01")
-        product("y", 0, "acc1")
-        product("y", 1, "acc2")
-        product("e", 1, "acc0")
+        product("y", 0, "bank1")
+        product("y", 1, "bank2")
+        product("e", 1, "bank0")
+        for pair in range(2):
+            add_neighbours(0, pair, "bank%d" % (3 + pair))
         round_weights("y", 1, 0)
         round_weights("y", 1, 1)
-        evacuate("y", 0, reuse="raw_y11")
-        evacuate("y", 1)
-        evacuate("e", 1, reuse="raw_y10")
+        evacuate("y", 0, offset=0)
+        evacuate("y", 1, offset=ROW)
+        evacuate("e", 1, offset=2 * ROW)
         quantize_weights("y", 1, 0)
         quantize_weights("y", 1, 1)
         gather_centres(0)
         gather_centres(1)
-        product("y", 2, "acc1")
-        product("y", 3, "acc2")
+        product("y", 2, "bank1")
+        product("y", 3, "bank2")
         round_weights("e", 1, 0)
         round_weights("e", 1, 1)
         for pair in range(2):
-            edge_sums(0, pair)
+            add_centres(0, pair)
         gather_neighbours(1, (0, 1))
         quantize_weights("e", 1, 0)
         quantize_weights("e", 1, 1)
         gather_neighbours(1, (2, 3), "grp_e11")
-        evacuate("y", 2)
-        evacuate("y", 3)
-        product("e", 2, "acc0")
-        product("e", 3, "acc1")
+        evacuate("y", 2, offset=3 * ROW)
+        evacuate("y", 3, offset=4 * ROW)
+        product("e", 2, "bank0")
+        product("e", 3, "bank5")
         for pair in range(2):
-            edge_sums(1, pair)
+            edge_sums(1, pair, "bank%d" % (2 - pair))
         for t in range(2, 4):
             gather_centres(t)
-        for pair in range(2):
-            gelu(0, pair)
+        acts01 = shared.tile([P, 2, 2, 4 * P], BF16, name="acts01", offset=5 * ROW)
+        gelu(0, 0, acts01[:, 0, 0, :])
+        gelu(0, 1, acts01[:, 1, 0, :])
         evacuate("e", 2)
-        for pair in range(2):
-            gelu(1, pair)
         evacuate("e", 3)
-        w3_grouped = cast(raw3, "grp3", False)
         gather_neighbours(2, (0, 1))
-        edge_sums(2, 0)
-        gelu(2, 0)
-        largest(0)
-        gather_neighbours(2, (2, 3), "act00")
-        edge_sums(2, 1)
-        gelu(2, 1)
-        largest(1)
+        gather_neighbours(2, (2, 3))
+        gelu(1, 0, acts01[:, 0, 1, :])
+        gelu(1, 1, acts01[:, 1, 1, :])
+        m01 = sb.tile([P, 2, 2, 2, 2, 64], BF16, name="m01")
+        nc.vector.tensor_tensor(
+            m01[:].rearrange("p t u h d c -> p (t u h d c)"),
+            acts01[:, 0, :, :].rearrange("p t c -> p (t c)"),
+            acts01[:, 1, :, :].rearrange("p t c -> p (t c)"),
+            MAX,
+        )
+        acts2 = [sb.tile([P, 4 * P], BF16, name="acts2%d" % pair, tag=("raw3", "acts21")[pair], align_bytes=64) for pair in range(2)]
+        for pair in range(2):
+            edge_sums(2, pair, "bank%d" % (3 + pair))
+            gelu(2, pair, acts2[pair][:])
+        gather_neighbours(3, (0,))
+        for t in range(2):
+            nc.vector.tensor_tensor(z_blocks[:, :, :, t, :], m01[:, t, :, :, 0, :], m01[:, t, :, :, 1, :], MAX)
+        gather_neighbours(3, (1,))
+        w3_grouped = cast(raw3, "grp3", False)
+        edge_sums(3, 0, "bank6")
+        acts3 = sb.tile([P, 4, 2, 64], BF16, name="acts3")
+        gelu(3, 0, acts3[:].rearrange("p a d c -> p (a d c)"))
         w3_codes, w3_scales = quantize(w3_grouped, "w3")
-        gather_neighbours(3, (0, 1), "grp3")
-        edge_sums(3, 0)
-        gelu(3, 0)
-        largest(2)
-        last = []
-        for d in (2, 3):
-            gather_neighbours(3, (d,), "act2%d" % (d - 2))
-            bank = ps.tile([P, 2, P], F32, name="bank", tag="bank", bufs=4)
-            for half in range(2):
-                vs = slice(half * P, (half + 1) * P)
-                nc.tensor.matmul(bank[:, half, :], got["y", 3, 0][:, vs], ident[:], start=(half == 0), stop=False, is_transpose=True)
-            for half in range(2):
-                vs = slice(half * P, (half + 1) * P)
-                nc.tensor.matmul(bank[:, half, :], got["e", 3, d][:, vs], ident[:], start=False, stop=(half == 1), is_transpose=True)
-            act = sb.tile([P, 4, 64], BF16, name="act_last%d" % d)
-            nc.scalar.activation(
-                act[:].rearrange("p (u h) (q b) -> p u (h q) b", u=2, b=2),
-                bank[:].rearrange("p h (q u b) -> p u (h q) b", u=2, b=2),
-                GELU,
-            )
-            last.append(act)
-        a01 = acts[3, 0][:].rearrange("p (a d c) -> p a d c", d=2, c=64)
-        m01 = sb.tile([P, 4, 64], BF16, name="m01")
-        nc.vector.tensor_tensor(m01[:], a01[:, :, 0, :], a01[:, :, 1, :], MAX)
-        m012 = sb.tile([P, 4, 64], BF16, name="m012")
-        nc.vector.tensor_tensor(m012[:], m01[:], last[0][:], MAX)
-        nc.vector.tensor_tensor(z_all[:].rearrange("p u h t c -> p (u h) t c")[:, :, 3, :], m012[:], last[1][:], MAX)
-
-        z_words = z_all[:].rearrange("p u h t c -> p u h (t c)").bitcast(F32)
-        zg = sb.tile([P, V * PACK], BF16, name="zg", align_bytes=64)
+        m2 = sb.tile([P, 2, 2, 2, 64], BF16, name="m2")
+        nc.vector.tensor_tensor(m2[:].rearrange("p u h d c -> p (u h d c)"), acts2[0][:], acts2[1][:], MAX)
+        gather_neighbours(3, (2,), "grp3")
+        nc.vector.tensor_tensor(z_blocks[:, :, :, 2, :], m2[:, :, :, 0, :], m2[:, :, :, 1, :], MAX)
+        bank = ps.tile([P, 2, P], F32, name="bank", tag="bank7")
         for half in range(2):
-            zt = ps.tile([P, 2, P], F32, name="zt", tag=("zt", "acc2")[half])
-            for u in range(2):
-                nc.tensor.transpose(zt[:, u, :], z_words[:, u, half, :], ident[:])
-            dst = zg[:, half * 512 : (half + 1) * 512].bitcast(F32).rearrange("p (v u) -> p v u", u=2)
-            if half == 0:
-                nc.scalar.copy(dst, zt[:].rearrange("p u v -> p v u"))
-            else:
-                nc.vector.tensor_copy(dst, zt[:].rearrange("p u v -> p v u"))
-        z_codes, z_scales = quantize(zg, "z")
-        for mt in range(N // P):
-            acc = ps.tile([P, S], F32, name="acc", tag="acc%d" % mt)
-            cols = slice(mt * P, (mt + 1) * P)
-            nc.tensor.matmul_mx(
-                out=acc[:, 0:V],
-                lhsT=w3_codes[:, cols].bitcast(FP8X4),
-                lhsT_scale=w3_scales[:, cols],
-                rhs=z_codes[:].bitcast(FP8X4),
-                rhs_scale=z_scales[:],
-                start=True,
-                stop=True,
+            vs = slice(half * P, (half + 1) * P)
+            nc.tensor.matmul(bank[:, half, :], got["y", 3, 0][:, vs], ident[:], start=(half == 0), stop=False, is_transpose=True)
+        for half in range(2):
+            vs = slice(half * P, (half + 1) * P)
+            nc.tensor.matmul(bank[:, half, :], got["e", 3, 2][:, vs], ident[:], start=False, stop=(half == 1), is_transpose=True)
+        third = sb.tile([P, 4, 64], BF16, name="third")
+        nc.scalar.activation(
+            third[:].rearrange("p (u h) (q b) -> p u (h q) b", u=2, b=2),
+            bank[:].rearrange("p h (q u b) -> p u (h q) b", u=2, b=2),
+            GELU,
+        )
+        m3a = sb.tile([P, 4, 64], BF16, name="m3a")
+        nc.vector.tensor_tensor(m3a[:], acts3[:, :, 0, :], acts3[:, :, 1, :], MAX)
+        fourth = []
+        for half in range(2):
+            g_t = sb.tile([P, P], F32, name="got_last%d" % half, tag=("raw3", "acts21")[half], align_bytes=64)
+            nc.vector.tensor_copy(g_t[:], rows["e", 3][:].indirect(pos_t[3][:, 8 * half : 8 * half + 8]))
+            bank = ps.tile([P, P], F32, name="bank", tag=("bank0", "bank5")[half])
+            nc.tensor.matmul(bank[:], got["y", 3, 0][:, half * P : (half + 1) * P], ident[:], start=True, stop=False, is_transpose=True)
+            nc.tensor.matmul(bank[:], g_t[:], ident[:], start=False, stop=True, is_transpose=True)
+            act = sb.tile([P, 2, 64], BF16, name="fourth%d" % half)
+            nc.scalar.activation(
+                act[:].rearrange("p u (q b) -> p u q b", b=2), bank[:].rearrange("p (q u b) -> p u q b", u=2, b=2), GELU
             )
-            res = sb.tile([P, V], F32, name="res%d" % mt)
-            if mt == 0:
-                nc.vector.tensor_copy(res[:], acc[:, 0:V])
-            else:
-                nc.scalar.copy(res[:], acc[:, 0:V])
-            nc.sync.dma_start(out[cols, :], res[:])
+            fourth.append(act)
+        m3b = sb.tile([P, 2, 2, 64], BF16, name="m3b")
+        nc.vector.tensor_tensor(m3b[:].rearrange("p u h c -> p (u h) c"), m3a[:], third[:], MAX)
+
+        z_words = z_all[:].bitcast(F32).rearrange("p (h u w) -> p h u w", h=2, u=2)
+        out_rows = out.rearrange("(m p) v -> p m v", p=P)
+        zgs = []
+        for half in range(2):
+            nc.vector.tensor_tensor(z_blocks[:, :, half, 3, :], m3b[:, :, half, :], fourth[half][:], MAX)
+            zt = ps.tile([P, 2, P], F32, name="zt", tag="bank%d" % (1 + half))
+            for u in range(2):
+                nc.tensor.transpose(zt[:, u, :], z_words[:, half, u, :], ident[:])
+            zg = sb.tile([P, P * PACK], BF16, name="zg%d" % half, align_bytes=64)
+            nc.scalar.copy(zg[:].bitcast(F32).rearrange("p (v u) -> p v u", u=2), zt[:].rearrange("p u v -> p v u"))
+            zgs.append(zg)
+        for half in range(2):
+            z_codes, z_scales = quantize(zgs[half], "z%d" % half)
+            res = sb.tile([P, 2, P], F32, name="res%d" % half)
+            for mt in range(N // P):
+                acc = ps.tile([P, P], F32, name="acc_out", tag=(("bank3", "bank4"), ("bank6", "bank7"))[half][mt])
+                cols = slice(mt * P, (mt + 1) * P)
+                nc.tensor.matmul_mx(
+                    out=acc[:],
+                    lhsT=w3_codes[:, cols].bitcast(FP8X4),
+                    lhsT_scale=w3_scales[:, cols],
+                    rhs=z_codes[:].bitcast(FP8X4),
+                    rhs_scale=z_scales[:],
+                    start=True,
+                    stop=True,
+                )
+                if mt == 0:
+                    nc.vector.tensor_copy(res[:, mt, :], acc[:])
+                else:
+                    nc.scalar.copy(res[:, mt, :], acc[:])
+            nc.sync.dma_start(out_rows[:, :, half * P : (half + 1) * P], res[:])

@@ -4,7 +4,6 @@ import concourse.mybir as mybir
 from concourse.masks import make_identity
 
 K, T, S, V, H, N = 1024, 1024, 512, 256, 512, 256
-D = 4
 FLOPS = 2 * (2 * K * H * S + H * N * V)
 
 F32 = mybir.dt.float32
@@ -22,7 +21,10 @@ P = 128
 PACK = 4
 K_PASS = P * PACK
 PASSES = K // K_PASS
-CHUNK = 256
+QUADRANT = 32
+CHUNK = 2 * P
+TILES = H // P
+RUN = P // 2
 ROW = 4 * S
 
 
@@ -35,301 +37,290 @@ def tile_picked_edgecv_gelu_p_kernel(
         shared = ctx.enter_context(tc.tile_pool(name="shared", bufs=1))
         ps = ctx.enter_context(tc.psum_pool(name="ps", bufs=1))
 
-        def load_list(src, name):
-            t = sb.tile(list(src.shape), U16, name=name)
-            nc.sync.dma_start(t[:], src)
-            return t
-
-        def load_weights(w, g, c, name, offset=None):
+        def place(shape, dtype, name, tag=None, offset=None):
             if offset is None:
-                raw = sb.tile([P, PACK, CHUNK], F32, name=name, tag=name, align_bytes=64)
-            else:
-                raw = shared.tile([P, PACK, CHUNK], F32, name=name, offset=offset)
-            rows = w[g * K_PASS : (g + 1) * K_PASS, c * CHUNK : (c + 1) * CHUNK]
-            nc.sync.dma_start(raw[:], rows.rearrange("(p j) c -> p j c", j=PACK))
-            return raw
+                return sb.tile(shape, dtype, name=name, tag=tag or name, align_bytes=64)
+            return shared.tile(shape, dtype, name=name, offset=offset, align_bytes=64)
 
-        def cast(raw, name, on_vector):
-            grouped = sb.tile([P, CHUNK * PACK], BF16, name=name, tag=name, align_bytes=64)
-            dst = grouped[:].rearrange("p (c i j) -> p c j i", i=4, j=PACK)
-            src = raw[:].rearrange("p j (c i) -> p c j i", i=4)
-            if on_vector:
-                nc.vector.tensor_copy(dst, src)
-            else:
-                nc.scalar.copy(dst, src)
-            return grouped
+        def bank(shape, number):
+            return ps.tile(shape, F32, name="bank", tag="bank%d" % number)
 
-        def quantize(grouped, name):
-            width = grouped.shape[1] // PACK
-            codes = sb.tile([P, width], U32, name=name + "_codes", align_bytes=64)
-            scales = sb.tile([P, width], U8, name=name + "_scales", align_bytes=64)
-            nc.vector.quantize_mx(out=codes[:].bitcast(FP8X4), scales=scales[:], in_=grouped[:])
-            return codes, scales
 
-        xs = sb.tile([P, PASSES, T], U8, name="xs")
-        nc.gpsimd.memset(xs[:].rearrange("p g c -> p (g c)").bitcast(I32), 0)
-        warm = sb.tile([P, 1], F32, name="warm")
-        nc.vector.memset(warm[:], 0.0)
+        def load_list(src, name):
+            lst = sb.tile(list(src.shape), U16, name=name)
+            nc.sync.dma_start(lst[:], src)
+            return lst
+
+        raw = {}
+
+        def load_weights(kind, chunk, g, offset=None):
+            w = {"y": w1, "e": w2, "out": w3}[kind]
+            tile = place([P, PACK, CHUNK], F32, "raw_%s%d%d" % (kind, chunk, g), offset=offset)
+            rows = w[g * K_PASS : (g + 1) * K_PASS, chunk * CHUNK : (chunk + 1) * CHUNK]
+            nc.sync.dma_start(tile[:], rows.rearrange("(p j) c -> p j c", j=PACK))
+            raw[kind, chunk, g] = tile
+
+        x_scale_rows = sb.tile([P, PASSES, T], U8, name="x_scale_rows")
+        nc.gpsimd.memset(x_scale_rows[:].rearrange("p g c -> p (g c)").bitcast(I32), 0)
+
+        warm_in = sb.tile([P, 1], F32, name="warm_in")
+        nc.vector.memset(warm_in[:], 0.0)
         warm_out = sb.tile([P, 1], F32, name="warm_out")
-        nc.scalar.activation(warm_out[:], warm[:], GELU)
+        nc.scalar.activation(warm_out[:], warm_in[:], GELU)
 
-        xw = [sb.tile([P, T], U16, name="xw%d" % g) for g in range(PASSES)]
-        raw, pos_t = {}, {}
-        offs_t = load_list(offs, "offs_t")
-        nc.sync.dma_start(xw[0][:].bitcast(I32), x_words[0].bitcast(I32))
-        cen_t = load_list(cen, "cen_t")
-        pos_t[0] = load_list(pos1, "pos0_t")
-        nc.sync.dma_start(xw[1][:].bitcast(I32), x_words[1].bitcast(I32))
-        raw["e", 0, 0] = load_weights(w2, 0, 0, "raw_e00")
-        for q in range(4):
+        x_word_rows = [sb.tile([P, T], U16, name="x_word_rows%d" % g) for g in range(PASSES)]
+        nc.sync.dma_start(x_word_rows[0][:].bitcast(I32), x_words[0].bitcast(I32))
+        offs_list = load_list(offs, "offs_list")
+        cen_list = load_list(cen, "cen_list")
+        pos_lists = [load_list(pos1, "pos1_list")]
+        nc.sync.dma_start(x_word_rows[1][:].bitcast(I32), x_words[1].bitcast(I32))
+        load_weights("e", 0, 0)
+        for q in range(P // QUADRANT):
             nc.sync.dma_start(
-                xs[32 * q : 32 * q + 4, :, :].bitcast(I32),
+                x_scale_rows[QUADRANT * q : QUADRANT * q + 4, :, :].bitcast(I32),
                 x_scales[:, 4 * q : 4 * q + 4, :].rearrange("g r c -> r g c").bitcast(I32),
             )
-        raw["e", 0, 1] = load_weights(w2, 1, 0, "raw_e01")
-        raw["y", 0, 0] = load_weights(w1, 0, 0, "raw_y00")
-        raw["y", 0, 1] = load_weights(w1, 1, 0, "raw_y01")
-        raw["y", 1, 0] = load_weights(w1, 0, 1, "raw_y10")
-        pos_t[1] = load_list(pos2, "pos1_t")
-        pos_t[2] = load_list(pos3, "pos2_t")
-        pos_t[3] = load_list(pos4, "pos3_t")
-        raw["y", 1, 1] = load_weights(w1, 1, 1, "raw_y11", ROW // 2)
-        raw["e", 1, 0] = load_weights(w2, 0, 1, "raw_e10")
-        raw["e", 1, 1] = load_weights(w2, 1, 1, "raw_e11", 3 * ROW + ROW // 2)
-        raw3 = load_weights(w3, 0, 0, "raw3")
+        load_weights("e", 0, 1)
+        load_weights("y", 0, 0)
+        load_weights("y", 0, 1)
+        load_weights("y", 1, 0)
+        pos_lists.extend(load_list(src, "pos%d_list" % (d + 2)) for d, src in enumerate((pos2, pos3, pos4)))
+        load_weights("y", 1, 1, offset=ROW // 2)
+        load_weights("e", 1, 0)
+        load_weights("e", 1, 1, offset=3 * ROW + ROW // 2)
+        load_weights("out", 0, 0)
 
         ident = sb.tile([P, P], F32, name="ident")
         make_identity(nc, ident[:])
 
-        xw_p, xs_p = [], []
+
+        x_codes, x_planes = [], []
         for g in range(PASSES):
-            words = sb.tile([P, S], U16, name="xw_p%d" % g, align_bytes=64)
-            nc.vector.tensor_copy(words[:], xw[g][:].indirect(offs_t[:]))
-            xw_p.append(words)
-            scales = sb.tile([P, S], U8, name="xs_p%d" % g, align_bytes=64)
-            nc.vector.tensor_copy(scales[:], xs[:, g, :].indirect(offs_t[:]))
-            xs_p.append(scales)
+            words = sb.tile([P, S], U16, name="x_codes%d" % g, align_bytes=64)
+            nc.vector.tensor_copy(words[:], x_word_rows[g][:].indirect(offs_list[:]))
+            x_codes.append(words)
+            plane = sb.tile([P, S], U8, name="x_plane%d" % g, align_bytes=64)
+            nc.vector.tensor_copy(plane[:], x_scale_rows[:, g, :].indirect(offs_list[:]))
+            x_planes.append(plane)
 
-        quant, accs, rows, got, banks = {}, {}, {}, {}, {}
 
-        grouped = {}
+        rounded, quantised, sums, rows, centres, neighbours, edges = {}, {}, {}, {}, {}, {}, {}
 
-        def round_weights(kind, c, g, on_vector=False):
-            grouped[kind, c, g] = cast(raw[kind, c, g], "grp_%s%d%d" % (kind, c, g), on_vector)
+        def round_weights(kind, chunk, g, offset=None):
+            tile = place([P, CHUNK * PACK], BF16, "rounded_%s%d%d" % (kind, chunk, g), offset=offset)
+            nc.scalar.copy(
+                tile[:].rearrange("p (c i j) -> p c j i", i=4, j=PACK),
+                raw[kind, chunk, g][:].rearrange("p j (c i) -> p c j i", i=4),
+            )
+            rounded[kind, chunk, g] = tile
 
-        def quantize_weights(kind, c, g):
-            quant[kind, c, g] = quantize(grouped[kind, c, g], "%s%d%d" % (kind, c, g))
+        def quantise(values, name, tag=None):
+            width = values.shape[1] // PACK
+            codes = place([P, width], U32, name + "_codes", tag=tag)
+            plane = place([P, width], U8, name + "_plane")
+            nc.vector.quantize_mx(out=codes[:].bitcast(FP8X4), scales=plane[:], in_=values[:])
+            return codes, plane
 
-        def product(kind, t, tag):
-            acc = ps.tile([P, S], F32, name="acc", tag=tag)
+        def quantise_weights(kind, chunk, g, tag=None):
+            quantised[kind, chunk, g] = quantise(rounded[kind, chunk, g], "%s%d%d" % (kind, chunk, g), tag)
+
+        def product(kind, t, number):
+            acc = bank([P, S], number)
             cols = slice((t % 2) * P, (t % 2 + 1) * P)
             for g in range(PASSES):
-                codes, scales = quant[kind, t // 2, g]
+                codes, plane = quantised[kind, t // 2, g]
                 nc.tensor.matmul_mx(
                     out=acc[:],
                     lhsT=codes[:, cols].bitcast(FP8X4),
-                    lhsT_scale=scales[:, cols],
-                    rhs=xw_p[g][:].bitcast(FP4X4),
-                    rhs_scale=xs_p[g][:],
+                    lhsT_scale=plane[:, cols],
+                    rhs=x_codes[g][:].bitcast(FP4X4),
+                    rhs_scale=x_planes[g][:],
                     start=(g == 0),
                     stop=(g == PASSES - 1),
                 )
-            accs[kind, t] = acc
+            sums[kind, t] = acc
 
-        def evacuate(kind, t, on_vector=False, reuse=None, offset=None):
-            name = "row_%s%d" % (kind, t)
-            if offset is None:
-                row = sb.tile([P, S], F32, name=name, tag=reuse or name, align_bytes=64)
-            else:
-                row = shared.tile([P, S], F32, name=name, offset=offset)
-            if on_vector:
-                nc.vector.tensor_copy(row[:], accs[kind, t][:])
-            else:
-                nc.scalar.copy(row[:], accs[kind, t][:])
+        def evacuate(kind, t, tag=None, offset=None):
+            row = place([P, S], F32, "row_%s%d" % (kind, t), tag=tag, offset=offset)
+            nc.scalar.copy(row[:], sums[kind, t][:])
             rows[kind, t] = row
 
-        def gather_centres(t, reuse=None):
-            name = "got_y%d" % t
-            g_t = sb.tile([P, V], F32, name=name, tag=reuse or name, align_bytes=64)
-            nc.vector.tensor_copy(g_t[:], rows["y", t][:].indirect(cen_t[:]))
-            got["y", t, 0] = g_t[:]
+        def gather_centres(t):
+            got = place([P, V], F32, "centres%d" % t)
+            nc.vector.tensor_copy(got[:], rows["y", t][:].indirect(cen_list[:]))
+            centres[t] = got[:]
 
-        def gather_neighbours(t, ds, reuse=None):
-            name = "got_e%d%d" % (t, ds[0])
-            g_t = sb.tile([P, len(ds), V], F32, name=name, tag=reuse or name, align_bytes=64)
+        def gather_neighbours(t, ds, tag=None):
+            got = place([P, len(ds), V], F32, "neighbours%d%d" % (t, ds[0]), tag=tag)
             for i, d in enumerate(ds):
-                nc.vector.tensor_copy(g_t[:, i, :], rows["e", t][:].indirect(pos_t[d][:]))
-                got["e", t, d] = g_t[:, i, :]
+                nc.vector.tensor_copy(got[:, i, :], rows["e", t][:].indirect(pos_lists[d][:]))
+                neighbours[t, d] = got[:, i, :]
 
-        z_all = sb.tile([P, 2 * H], BF16, name="z_all")
+        def turn(dst, src, first, last):
+            nc.tensor.matmul(dst, src, ident[:], start=first, stop=last, is_transpose=True)
 
-        slots = [(half, dd) for dd in range(2) for half in range(2)]
+        def half_of(ap, half):
+            return ap[:, half * P : (half + 1) * P]
 
-        def turn(bank, half, dd, src, first, last):
-            nc.tensor.matmul(
-                bank[:, half, dd, :], src[:, half * P : (half + 1) * P], ident[:], start=first, stop=last, is_transpose=True
-            )
+        slots = [(half, i) for i in range(2) for half in range(2)]
 
-        def add_neighbours(t, pair, tag):
-            bank = ps.tile([P, 2, 2, P], F32, name="bank", tag=tag)
-            banks[t, pair] = bank
-            for i, (half, dd) in enumerate(slots):
-                turn(bank, half, dd, got["e", t, 2 * pair + dd], i == 0, False)
+        def turn_centres(t, pair, first):
+            for n, (half, i) in enumerate(slots):
+                turn(edges[t, pair][:, half, i, :], half_of(centres[t], half), first and n == 0, not first and n == 3)
 
-        def add_centres(t, pair):
-            for i, (half, dd) in enumerate(slots):
-                turn(banks[t, pair], half, dd, got["y", t, 0], False, i == 3)
+        def turn_neighbours(t, pair, first):
+            for n, (half, i) in enumerate(slots):
+                src = half_of(neighbours[t, 2 * pair + i], half)
+                turn(edges[t, pair][:, half, i, :], src, first and n == 0, not first and n == 3)
 
-        def edge_sums(t, pair, tag):
-            bank = ps.tile([P, 2, 2, P], F32, name="bank", tag=tag)
-            banks[t, pair] = bank
-            for i, (half, dd) in enumerate(slots):
-                turn(bank, half, dd, got["y", t, 0], i == 0, False)
-            for i, (half, dd) in enumerate(slots):
-                turn(bank, half, dd, got["e", t, 2 * pair + dd], False, i == 3)
+        def edge_sums(t, pair, number):
+            edges[t, pair] = bank([P, 2, 2, P], number)
+            turn_centres(t, pair, True)
+            turn_neighbours(t, pair, False)
 
-        def gelu(t, pair, act):
+        def gelu(dst, src):
             nc.scalar.activation(
-                act.rearrange("p (u q b) -> p u q b", u=2, b=2),
-                banks[t, pair][:].rearrange("p h d (q u b) -> p u (h d q) b", u=2, b=2),
-                GELU,
+                dst.rearrange("p (u q b) -> p u q b", u=2, b=2), src.rearrange("p (q u b) -> p u q b", u=2, b=2), GELU
             )
 
-        z_blocks = z_all[:].rearrange("p (h u t c) -> p u h t c", h=2, u=2, t=4)
+        def gelu_pair(t, pair, dst):
+            gelu(dst, edges[t, pair][:].rearrange("p h i c -> p (h i c)"))
+
+        def largest(dst, a, b):
+            nc.vector.tensor_tensor(dst, a, b, MAX)
+
+        z = sb.tile([P, 2 * H], BF16, name="z")
+        z_blocks = z[:].rearrange("p (h u t c) -> p u h t c", h=2, u=2, t=TILES)
+        z_words = z[:].bitcast(F32).rearrange("p (h u w) -> p h u w", h=2, u=2)
+
 
         for g in range(PASSES):
             round_weights("e", 0, g)
-            quantize_weights("e", 0, g)
-        product("e", 0, "bank0")
-        round_weights("y", 0, 0)
-        quantize_weights("y", 0, 0)
-        evacuate("e", 0, True, reuse="grp_y00")
-        round_weights("y", 0, 1)
-        quantize_weights("y", 0, 1)
-        gather_neighbours(0, (0, 1, 2, 3), "grp_y01")
-        product("y", 0, "bank1")
-        product("y", 1, "bank2")
-        product("e", 1, "bank0")
+            quantise_weights("e", 0, g)
+        product("e", 0, 0)
+        product("e", 1, 5)
+        for chunk, g in ((0, 0), (0, 1), (1, 0)):
+            round_weights("y", chunk, g)
+            quantise_weights("y", chunk, g)
+        evacuate("e", 0, tag="raw_y10")
+        gather_neighbours(0, (0, 1, 2, 3))
+        product("y", 0, 1)
+        product("y", 1, 2)
         for pair in range(2):
-            add_neighbours(0, pair, "bank%d" % (3 + pair))
-        round_weights("y", 1, 0)
+            edges[0, pair] = bank([P, 2, 2, P], 3 + pair)
+            turn_neighbours(0, pair, True)
         round_weights("y", 1, 1)
         evacuate("y", 0, offset=0)
         evacuate("y", 1, offset=ROW)
         evacuate("e", 1, offset=2 * ROW)
-        quantize_weights("y", 1, 0)
-        quantize_weights("y", 1, 1)
+        quantise_weights("y", 1, 1)
         gather_centres(0)
         gather_centres(1)
-        product("y", 2, "bank1")
-        product("y", 3, "bank2")
-        round_weights("e", 1, 0)
-        round_weights("e", 1, 1)
+        product("y", 2, 1)
+        product("y", 3, 2)
+        for g in range(PASSES):
+            round_weights("e", 1, g)
         for pair in range(2):
-            add_centres(0, pair)
+            turn_centres(0, pair, False)
         gather_neighbours(1, (0, 1))
-        quantize_weights("e", 1, 0)
-        quantize_weights("e", 1, 1)
-        gather_neighbours(1, (2, 3), "grp_e11")
+        for g in range(PASSES):
+            quantise_weights("e", 1, g)
+        gather_neighbours(1, (2, 3), tag="rounded_e11")
+
+
         evacuate("y", 2, offset=3 * ROW)
         evacuate("y", 3, offset=4 * ROW)
-        product("e", 2, "bank0")
-        product("e", 3, "bank5")
+        product("e", 2, 0)
+        product("e", 3, 5)
         for pair in range(2):
-            edge_sums(1, pair, "bank%d" % (2 - pair))
-        for t in range(2, 4):
-            gather_centres(t)
-        acts01 = shared.tile([P, 2, 2, 4 * P], BF16, name="acts01", offset=5 * ROW)
-        gelu(0, 0, acts01[:, 0, 0, :])
-        gelu(0, 1, acts01[:, 1, 0, :])
+            edge_sums(1, pair, 2 - pair)
+        gather_centres(2)
+        gather_centres(3)
+        acts = place([P, 2, TILES - 1, 4 * P], BF16, "acts", offset=5 * ROW)
+        for pair in range(2):
+            gelu_pair(0, pair, acts[:, pair, 0, :])
         evacuate("e", 2)
         evacuate("e", 3)
         gather_neighbours(2, (0, 1))
         gather_neighbours(2, (2, 3))
-        gelu(1, 0, acts01[:, 0, 1, :])
-        gelu(1, 1, acts01[:, 1, 1, :])
-        m01 = sb.tile([P, 2, 2, 2, 2, 64], BF16, name="m01")
-        nc.vector.tensor_tensor(
-            m01[:].rearrange("p t u h d c -> p (t u h d c)"),
-            acts01[:, 0, :, :].rearrange("p t c -> p (t c)"),
-            acts01[:, 1, :, :].rearrange("p t c -> p (t c)"),
-            MAX,
-        )
-        acts2 = [sb.tile([P, 4 * P], BF16, name="acts2%d" % pair, tag=("raw3", "acts21")[pair], align_bytes=64) for pair in range(2)]
         for pair in range(2):
-            edge_sums(2, pair, "bank%d" % (3 + pair))
-            gelu(2, pair, acts2[pair][:])
-        gather_neighbours(3, (0,))
-        for t in range(2):
-            nc.vector.tensor_tensor(z_blocks[:, :, :, t, :], m01[:, t, :, :, 0, :], m01[:, t, :, :, 1, :], MAX)
-        gather_neighbours(3, (1,))
-        w3_grouped = cast(raw3, "grp3", False)
-        edge_sums(3, 0, "bank6")
-        acts3 = sb.tile([P, 4, 2, 64], BF16, name="acts3")
-        gelu(3, 0, acts3[:].rearrange("p a d c -> p (a d c)"))
-        w3_codes, w3_scales = quantize(w3_grouped, "w3")
-        m2 = sb.tile([P, 2, 2, 2, 64], BF16, name="m2")
-        nc.vector.tensor_tensor(m2[:].rearrange("p u h d c -> p (u h d c)"), acts2[0][:], acts2[1][:], MAX)
-        gather_neighbours(3, (2,), "grp3")
-        nc.vector.tensor_tensor(z_blocks[:, :, :, 2, :], m2[:, :, :, 0, :], m2[:, :, :, 1, :], MAX)
-        bank = ps.tile([P, 2, P], F32, name="bank", tag="bank7")
+            gelu_pair(1, pair, acts[:, pair, 1, :])
+        round_weights("out", 0, 0, offset=4 * ROW)
+        for pair in range(2):
+            edge_sums(2, pair, 3 + pair)
+            gelu_pair(2, pair, acts[:, pair, 2, :])
+
+        last = TILES - 1
+        gather_neighbours(last, (0, 1))
+        edge_sums(last, 0, 6)
+        first_two = sb.tile([P, 4, 2, RUN], BF16, name="first_two")
+        gelu_pair(last, 0, first_two[:].rearrange("p a i c -> p (a i c)"))
+        gather_neighbours(last, (2,))
+        third_sums = bank([P, 2, P], 7)
         for half in range(2):
-            vs = slice(half * P, (half + 1) * P)
-            nc.tensor.matmul(bank[:, half, :], got["y", 3, 0][:, vs], ident[:], start=(half == 0), stop=False, is_transpose=True)
+            turn(third_sums[:, half, :], half_of(centres[last], half), half == 0, False)
         for half in range(2):
-            vs = slice(half * P, (half + 1) * P)
-            nc.tensor.matmul(bank[:, half, :], got["e", 3, 2][:, vs], ident[:], start=False, stop=(half == 1), is_transpose=True)
-        third = sb.tile([P, 4, 64], BF16, name="third")
-        nc.scalar.activation(
-            third[:].rearrange("p (u h) (q b) -> p u (h q) b", u=2, b=2),
-            bank[:].rearrange("p h (q u b) -> p u (h q) b", u=2, b=2),
-            GELU,
+            turn(third_sums[:, half, :], half_of(neighbours[last, 2], half), False, half == 1)
+        third = sb.tile([P, 4, RUN], BF16, name="third")
+        gelu(third[:].rearrange("p a c -> p (a c)"), third_sums[:].rearrange("p h c -> p (h c)"))
+
+        across_pairs = sb.tile([P, TILES - 1, 2, 2, 2, RUN], BF16, name="across_pairs")
+        largest(
+            across_pairs[:].rearrange("p t u h i c -> p (t u h i c)"),
+            acts[:, 0, :, :].rearrange("p t c -> p (t c)"),
+            acts[:, 1, :, :].rearrange("p t c -> p (t c)"),
         )
-        m3a = sb.tile([P, 4, 64], BF16, name="m3a")
-        nc.vector.tensor_tensor(m3a[:], acts3[:, :, 0, :], acts3[:, :, 1, :], MAX)
+        of_two = sb.tile([P, 4, RUN], BF16, name="of_two")
+        largest(of_two[:], first_two[:, :, 0, :], first_two[:, :, 1, :])
+
         fourth = []
         for half in range(2):
-            g_t = sb.tile([P, P], F32, name="got_last%d" % half, tag=("raw3", "acts21")[half], align_bytes=64)
-            nc.vector.tensor_copy(g_t[:], rows["e", 3][:].indirect(pos_t[3][:, 8 * half : 8 * half + 8]))
-            bank = ps.tile([P, P], F32, name="bank", tag=("bank0", "bank5")[half])
-            nc.tensor.matmul(bank[:], got["y", 3, 0][:, half * P : (half + 1) * P], ident[:], start=True, stop=False, is_transpose=True)
-            nc.tensor.matmul(bank[:], g_t[:], ident[:], start=False, stop=True, is_transpose=True)
-            act = sb.tile([P, 2, 64], BF16, name="fourth%d" % half)
-            nc.scalar.activation(
-                act[:].rearrange("p u (q b) -> p u q b", b=2), bank[:].rearrange("p (q u b) -> p u q b", u=2, b=2), GELU
-            )
+            got = place([P, P], F32, "neighbours_last%d" % half, offset=6 * ROW + half * 4 * P)
+            entries = pos_lists[3][:, half * (P // 16) : (half + 1) * (P // 16)]
+            nc.vector.tensor_copy(got[:], rows["e", last][:].indirect(entries))
+            fourth_sums = bank([P, P], (0, 5)[half])
+            turn(fourth_sums[:], half_of(centres[last], half), True, False)
+            turn(fourth_sums[:], got[:], False, True)
+            act = place([P, 2, RUN], BF16, "fourth%d" % half)
+            gelu(act[:].rearrange("p u c -> p (u c)"), fourth_sums[:])
             fourth.append(act)
-        m3b = sb.tile([P, 2, 2, 64], BF16, name="m3b")
-        nc.vector.tensor_tensor(m3b[:].rearrange("p u h c -> p (u h) c"), m3a[:], third[:], MAX)
 
-        z_words = z_all[:].bitcast(F32).rearrange("p (h u w) -> p h u w", h=2, u=2)
-        out_rows = out.rearrange("(m p) v -> p m v", p=P)
-        zgs = []
+        of_three = sb.tile([P, 2, 2, RUN], BF16, name="of_three")
+        largest(of_three[:].rearrange("p u h c -> p (u h) c"), of_two[:], third[:])
+        for t in range(last):
+            largest(z_blocks[:, :, :, t, :], across_pairs[:, t, :, :, 0, :], across_pairs[:, t, :, :, 1, :])
+
+
+        z_rounded = []
         for half in range(2):
-            nc.vector.tensor_tensor(z_blocks[:, :, half, 3, :], m3b[:, :, half, :], fourth[half][:], MAX)
-            zt = ps.tile([P, 2, P], F32, name="zt", tag="bank%d" % (1 + half))
+            largest(z_blocks[:, :, half, last, :], of_three[:, :, half, :], fourth[half][:])
+            turned = bank([P, 2, P], 1 + half)
             for u in range(2):
-                nc.tensor.transpose(zt[:, u, :], z_words[:, half, u, :], ident[:])
-            zg = sb.tile([P, P * PACK], BF16, name="zg%d" % half, align_bytes=64)
-            nc.scalar.copy(zg[:].bitcast(F32).rearrange("p (v u) -> p v u", u=2), zt[:].rearrange("p u v -> p v u"))
-            zgs.append(zg)
+                nc.tensor.transpose(turned[:, u, :], z_words[:, half, u, :], ident[:])
+            tile = place([P, P * PACK], BF16, "z_rounded%d" % half)
+            nc.scalar.copy(tile[:].bitcast(F32).rearrange("p (v u) -> p v u", u=2), turned[:].rearrange("p u v -> p v u"))
+            z_rounded.append(tile)
+
+        quantise_weights("out", 0, 0, tag="fourth1")
+        w3_codes, w3_plane = quantised["out", 0, 0]
+        out_rows = out.rearrange("(m p) v -> p m v", p=P)
         for half in range(2):
-            z_codes, z_scales = quantize(zgs[half], "z%d" % half)
-            res = sb.tile([P, 2, P], F32, name="res%d" % half)
-            for mt in range(N // P):
-                acc = ps.tile([P, P], F32, name="acc_out", tag=(("bank3", "bank4"), ("bank6", "bank7"))[half][mt])
-                cols = slice(mt * P, (mt + 1) * P)
+            z_codes, z_plane = quantise(z_rounded[half], "z%d" % half)
+            result = sb.tile([P, N // P, P], F32, name="result%d" % half)
+            for m in range(N // P):
+                acc = bank([P, P], ((3, 4), (6, 7))[half][m])
+                cols = slice(m * P, (m + 1) * P)
                 nc.tensor.matmul_mx(
                     out=acc[:],
                     lhsT=w3_codes[:, cols].bitcast(FP8X4),
-                    lhsT_scale=w3_scales[:, cols],
+                    lhsT_scale=w3_plane[:, cols],
                     rhs=z_codes[:].bitcast(FP8X4),
-                    rhs_scale=z_scales[:],
+                    rhs_scale=z_plane[:],
                     start=True,
                     stop=True,
                 )
-                if mt == 0:
-                    nc.vector.tensor_copy(res[:, mt, :], acc[:])
+                if m == 0:
+                    nc.vector.tensor_copy(result[:, m, :], acc[:])
                 else:
-                    nc.scalar.copy(res[:, mt, :], acc[:])
-            nc.sync.dma_start(out_rows[:, :, half * P : (half + 1) * P], res[:])
+                    nc.scalar.copy(result[:, m, :], acc[:])
+            nc.sync.dma_start(out_rows[:, :, half * P : (half + 1) * P], result[:])

@@ -26,6 +26,7 @@ CHUNK = 2 * P
 TILES = H // P
 RUN = P // 2
 ROW = 4 * S
+SHIFTED = 112
 
 
 def tile_picked_edgecv_gelu_p_kernel(
@@ -60,59 +61,66 @@ def tile_picked_edgecv_gelu_p_kernel(
             nc.sync.dma_start(tile[:], rows.rearrange("(p j) c -> p j c", j=PACK))
             raw[kind, chunk, g] = tile
 
-        x_scale_rows = sb.tile([P, PASSES, T], U8, name="x_scale_rows")
-        nc.gpsimd.memset(x_scale_rows[:].rearrange("p g c -> p (g c)").bitcast(I32), 0)
+        x_scale_rows = sb.tile([P, T], U8, name="x_scale_rows", align_bytes=64)
+        nc.gpsimd.memset(x_scale_rows[:, : T // 2].bitcast(I32), 0)
+        nc.vector.memset(x_scale_rows[:, T // 2 :].bitcast(I32), 0)
+        second_plane = sb.tile([P, S], U8, name="second_plane", align_bytes=64)
+        nc.gpsimd.memset(second_plane[:].bitcast(I32), 0)
 
+        offs_list = load_list(offs, "offs_list")
+        x_word_rows = [sb.tile([P, T], U16, name="x_word_rows%d" % g) for g in range(PASSES)]
+        nc.sync.dma_start(x_word_rows[0][:].bitcast(I32), x_words[0].bitcast(I32))
+        for q in range(P // QUADRANT):
+            (nc.sync, nc.scalar)[q % 2].dma_start(
+                x_scale_rows[QUADRANT * q : QUADRANT * q + 4 * PASSES, :].bitcast(I32),
+                x_scales[:, 4 * q : 4 * q + 4, :].bitcast(I32),
+            )
         warm_in = sb.tile([P, 1], F32, name="warm_in")
         nc.vector.memset(warm_in[:], 0.0)
         warm_out = sb.tile([P, 1], F32, name="warm_out")
         nc.scalar.activation(warm_out[:], warm_in[:], GELU)
-
-        x_word_rows = [sb.tile([P, T], U16, name="x_word_rows%d" % g) for g in range(PASSES)]
-        nc.sync.dma_start(x_word_rows[0][:].bitcast(I32), x_words[0].bitcast(I32))
-        offs_list = load_list(offs, "offs_list")
-        cen_list = load_list(cen, "cen_list")
-        pos_lists = [load_list(pos1, "pos1_list")]
         nc.sync.dma_start(x_word_rows[1][:].bitcast(I32), x_words[1].bitcast(I32))
         load_weights("e", 0, 0)
-        for q in range(P // QUADRANT):
-            nc.sync.dma_start(
-                x_scale_rows[QUADRANT * q : QUADRANT * q + 4, :, :].bitcast(I32),
-                x_scales[:, 4 * q : 4 * q + 4, :].rearrange("g r c -> r g c").bitcast(I32),
-            )
         load_weights("e", 0, 1)
         load_weights("y", 0, 0)
-        load_weights("y", 0, 1)
-        load_weights("y", 1, 0)
-        pos_lists.extend(load_list(src, "pos%d_list" % (d + 2)) for d, src in enumerate((pos2, pos3, pos4)))
-        load_weights("y", 1, 1, offset=ROW // 2)
+        pos_lists = [load_list(src, "pos%d_list" % (d + 1)) for d, src in enumerate((pos1, pos2, pos3, pos4))]
+
+        both_planes = sb.tile([P, S], U8, name="both_planes", align_bytes=64)
+        nc.vector.tensor_copy(both_planes[:], x_scale_rows[:].indirect(offs_list[:]))
+        nc.sync.dma_start(second_plane[0:SHIFTED, :].bitcast(I32), both_planes[4 : 4 + SHIFTED, :].bitcast(I32))
+        x_planes = [both_planes, second_plane]
+
+        load_weights("y", 0, 1, offset=0)
         load_weights("e", 1, 0)
-        load_weights("e", 1, 1, offset=3 * ROW + ROW // 2)
+        cen_list = load_list(cen, "cen_list")
+        load_weights("e", 1, 1, offset=2 * ROW)
+        load_weights("y", 1, 0)
+        load_weights("y", 1, 1, offset=5 * ROW - ROW // 4)
         load_weights("out", 0, 0)
 
         ident = sb.tile([P, P], F32, name="ident")
         make_identity(nc, ident[:])
 
-
-        x_codes, x_planes = [], []
+        x_codes = []
         for g in range(PASSES):
-            words = sb.tile([P, S], U16, name="x_codes%d" % g, align_bytes=64)
+            words = place([P, S], U16, "x_codes%d" % g, tag="x_scale_rows" if g == 0 else None)
             nc.vector.tensor_copy(words[:], x_word_rows[g][:].indirect(offs_list[:]))
             x_codes.append(words)
-            plane = sb.tile([P, S], U8, name="x_plane%d" % g, align_bytes=64)
-            nc.vector.tensor_copy(plane[:], x_scale_rows[:, g, :].indirect(offs_list[:]))
-            x_planes.append(plane)
 
 
-        rounded, quantised, sums, rows, centres, neighbours, edges = {}, {}, {}, {}, {}, {}, {}
+        rounded, quantised, sums, rows, centres, neighbours, edges, acts = {}, {}, {}, {}, {}, {}, {}, {}
 
-        def round_weights(kind, chunk, g, offset=None):
-            tile = place([P, CHUNK * PACK], BF16, "rounded_%s%d%d" % (kind, chunk, g), offset=offset)
-            nc.scalar.copy(
-                tile[:].rearrange("p (c i j) -> p c j i", i=4, j=PACK),
-                raw[kind, chunk, g][:].rearrange("p j (c i) -> p c j i", i=4),
-            )
-            rounded[kind, chunk, g] = tile
+        def round_weights(kind, chunk, g, shares, part=(0, 1), tag=None):
+            width = P * len(part)
+            tile = place([P, width * PACK], BF16, "rounded_%s%d%d%d" % (kind, chunk, g, part[0]), tag=tag)
+            step = width // len(shares)
+            for n, copy in enumerate(shares):
+                first = part[0] * P + n * step
+                copy(
+                    tile[:, n * step * PACK : (n + 1) * step * PACK].rearrange("p (c i j) -> p c j i", i=4, j=PACK),
+                    raw[kind, chunk, g][:, :, first : first + step].rearrange("p j (c i) -> p c j i", i=4),
+                )
+            rounded[kind, chunk, g, part] = tile
 
         def quantise(values, name, tag=None):
             width = values.shape[1] // PACK
@@ -121,22 +129,24 @@ def tile_picked_edgecv_gelu_p_kernel(
             nc.vector.quantize_mx(out=codes[:].bitcast(FP8X4), scales=plane[:], in_=values[:])
             return codes, plane
 
-        def quantise_weights(kind, chunk, g, tag=None):
-            quantised[kind, chunk, g] = quantise(rounded[kind, chunk, g], "%s%d%d" % (kind, chunk, g), tag)
+        def quantise_weights(kind, chunk, g, part=(0, 1), tag=None):
+            codes, plane = quantise(rounded[kind, chunk, g, part], "%s%d%d%d" % (kind, chunk, g, part[0]), tag)
+            for n, i in enumerate(part):
+                cols = slice(n * P, (n + 1) * P)
+                quantised[kind, 2 * chunk + i, g] = codes[:, cols], plane[:, cols]
 
-        def product(kind, t, number):
+        def product(kind, t, number, order=(0, 1)):
             acc = bank([P, S], number)
-            cols = slice((t % 2) * P, (t % 2 + 1) * P)
-            for g in range(PASSES):
-                codes, plane = quantised[kind, t // 2, g]
+            for g in order:
+                codes, plane = quantised[kind, t, g]
                 nc.tensor.matmul_mx(
                     out=acc[:],
-                    lhsT=codes[:, cols].bitcast(FP8X4),
-                    lhsT_scale=plane[:, cols],
+                    lhsT=codes.bitcast(FP8X4),
+                    lhsT_scale=plane,
                     rhs=x_codes[g][:].bitcast(FP4X4),
                     rhs_scale=x_planes[g][:],
-                    start=(g == 0),
-                    stop=(g == PASSES - 1),
+                    start=(g == order[0]),
+                    stop=(g == order[-1]),
                 )
             sums[kind, t] = acc
 
@@ -145,13 +155,13 @@ def tile_picked_edgecv_gelu_p_kernel(
             nc.scalar.copy(row[:], sums[kind, t][:])
             rows[kind, t] = row
 
-        def gather_centres(t):
-            got = place([P, V], F32, "centres%d" % t)
+        def gather_centres(t, offset=None):
+            got = place([P, V], F32, "centres%d" % t, offset=offset)
             nc.vector.tensor_copy(got[:], rows["y", t][:].indirect(cen_list[:]))
             centres[t] = got[:]
 
-        def gather_neighbours(t, ds, tag=None):
-            got = place([P, len(ds), V], F32, "neighbours%d%d" % (t, ds[0]), tag=tag)
+        def gather_neighbours(t, ds, tag=None, offset=None):
+            got = place([P, len(ds), V], F32, "neighbours%d%d" % (t, ds[0]), tag=tag, offset=offset)
             for i, d in enumerate(ds):
                 nc.vector.tensor_copy(got[:, i, :], rows["e", t][:].indirect(pos_lists[d][:]))
                 neighbours[t, d] = got[:, i, :]
@@ -162,139 +172,162 @@ def tile_picked_edgecv_gelu_p_kernel(
         def half_of(ap, half):
             return ap[:, half * P : (half + 1) * P]
 
-        slots = [(half, i) for i in range(2) for half in range(2)]
+        slots = [(i, half) for i in range(2) for half in range(2)]
 
         def turn_centres(t, pair, first):
-            for n, (half, i) in enumerate(slots):
-                turn(edges[t, pair][:, half, i, :], half_of(centres[t], half), first and n == 0, not first and n == 3)
+            for n, (i, half) in enumerate(slots):
+                turn(edges[t, pair][:, i, half, :], half_of(centres[t], half), first and n == 0, not first and n == 3)
 
         def turn_neighbours(t, pair, first):
-            for n, (half, i) in enumerate(slots):
+            for n, (i, half) in enumerate(slots):
                 src = half_of(neighbours[t, 2 * pair + i], half)
-                turn(edges[t, pair][:, half, i, :], src, first and n == 0, not first and n == 3)
+                turn(edges[t, pair][:, i, half, :], src, first and n == 0, not first and n == 3)
 
-        def edge_sums(t, pair, number):
+        def open_edges(t, pair, number):
             edges[t, pair] = bank([P, 2, 2, P], number)
-            turn_centres(t, pair, True)
-            turn_neighbours(t, pair, False)
+            turn_neighbours(t, pair, True)
 
         def gelu(dst, src):
             nc.scalar.activation(
-                dst.rearrange("p (u q b) -> p u q b", u=2, b=2), src.rearrange("p (q u b) -> p u q b", u=2, b=2), GELU
+                dst.rearrange("p a u (q b) -> p u a q b", b=2), src.rearrange("p a (q u b) -> p u a q b", u=2, b=2), GELU
             )
 
         def gelu_pair(t, pair, dst):
-            gelu(dst, edges[t, pair][:].rearrange("p h i c -> p (h i c)"))
+            gelu(dst, edges[t, pair][:].rearrange("p i h c -> p (i h) c"))
 
         def largest(dst, a, b):
             nc.vector.tensor_tensor(dst, a, b, MAX)
 
         z = sb.tile([P, 2 * H], BF16, name="z")
-        z_blocks = z[:].rearrange("p (h u t c) -> p u h t c", h=2, u=2, t=TILES)
+        z_blocks = z[:].rearrange("p (a t c) -> p a t c", a=4, t=TILES)
         z_words = z[:].bitcast(F32).rearrange("p (h u w) -> p h u w", h=2, u=2)
 
+        on_scalar, on_vector = [nc.scalar.copy], [nc.vector.tensor_copy]
 
-        for g in range(PASSES):
-            round_weights("e", 0, g)
-            quantise_weights("e", 0, g)
+
+        def act_tiles(first, count, offset=None):
+            acts[first] = [
+                place([P, 4, 2, count, RUN], BF16, "acts%d%d" % (first, pair), offset=offset and offset + pair * count * ROW // 2)
+                for pair in range(2)
+            ]
+
+        def activate(first, t):
+            for pair in range(2):
+                gelu_pair(t, pair, acts[first][pair][:, :, :, t - first, :])
+
+        def best_of_four(first, count):
+            across = sb.tile([P, 2, 4, count * RUN], BF16, name="across%d" % first)
+            flat = [acts[first][pair][:].rearrange("p a u t c -> p (a u t c)") for pair in range(2)]
+            largest(across[:].rearrange("p i a c -> p (i a c)"), flat[0], flat[1])
+            dst = z_blocks[:, :, first : first + count, :].rearrange("p a t c -> p a (t c)")
+            return lambda: largest(dst, across[:, 0], across[:, 1])
+
+        round_weights("e", 0, 0, on_scalar)
+        quantise_weights("e", 0, 0)
+        for i in range(2):
+            round_weights("e", 0, 1, on_scalar, (i,))
+            quantise_weights("e", 0, 1, (i,))
         product("e", 0, 0)
-        product("e", 1, 5)
-        for chunk, g in ((0, 0), (0, 1), (1, 0)):
-            round_weights("y", chunk, g)
-            quantise_weights("y", chunk, g)
-        evacuate("e", 0, tag="raw_y10")
-        gather_neighbours(0, (0, 1, 2, 3))
-        product("y", 0, 1)
-        product("y", 1, 2)
-        for pair in range(2):
-            edges[0, pair] = bank([P, 2, 2, P], 3 + pair)
-            turn_neighbours(0, pair, True)
-        round_weights("y", 1, 1)
-        evacuate("y", 0, offset=0)
-        evacuate("y", 1, offset=ROW)
-        evacuate("e", 1, offset=2 * ROW)
-        quantise_weights("y", 1, 1)
-        gather_centres(0)
-        gather_centres(1)
-        product("y", 2, 1)
-        product("y", 3, 2)
-        for g in range(PASSES):
-            round_weights("e", 1, g)
+        product("e", 1, 1, order=(1, 0))
+        round_weights("y", 0, 0, on_scalar + on_vector)
+        quantise_weights("y", 0, 0)
+        evacuate("e", 0)
+        round_weights("y", 0, 1, on_vector)
+        quantise_weights("y", 0, 1)
+        product("y", 0, 2, order=(1, 0))
+        product("y", 1, 3, order=(1, 0))
+        gather_neighbours(0, (0, 1), offset=0)
+        open_edges(0, 0, 4)
+        gather_neighbours(0, (2, 3), offset=ROW)
+        open_edges(0, 1, 5)
+        round_weights("e", 1, 0, on_scalar, tag="e010_codes")
+        quantise_weights("e", 1, 0)
+        evacuate("y", 0)
+        evacuate("e", 1, tag="raw_e10")
+        gather_neighbours(1, (0, 1))
+        round_weights("e", 1, 1, on_scalar, tag="e011_codes")
+        quantise_weights("e", 1, 1)
+        product("e", 2, 0)
+        product("e", 3, 1)
+        evacuate("y", 1)
+        gather_centres(0, offset=2 * ROW)
+        gather_neighbours(1, (2, 3), offset=3 * ROW)
+        open_edges(1, 0, 6)
         for pair in range(2):
             turn_centres(0, pair, False)
-        gather_neighbours(1, (0, 1))
+        open_edges(1, 1, 7)
+
+
         for g in range(PASSES):
-            quantise_weights("e", 1, g)
-        gather_neighbours(1, (2, 3), tag="rounded_e11")
-
-
-        evacuate("y", 2, offset=3 * ROW)
-        evacuate("y", 3, offset=4 * ROW)
-        product("e", 2, 0)
-        product("e", 3, 5)
+            round_weights("y", 1, g, on_scalar)
+            quantise_weights("y", 1, g)
+        product("y", 2, 2)
+        product("y", 3, 3)
+        gather_centres(1, offset=6 * ROW)
         for pair in range(2):
-            edge_sums(1, pair, 2 - pair)
-        gather_centres(2)
-        gather_centres(3)
-        acts = place([P, 2, TILES - 1, 4 * P], BF16, "acts", offset=5 * ROW)
-        for pair in range(2):
-            gelu_pair(0, pair, acts[:, pair, 0, :])
-        evacuate("e", 2)
-        evacuate("e", 3)
+            turn_centres(1, pair, False)
+        evacuate("e", 2, offset=4 * ROW)
+        act_tiles(0, 1, offset=5 * ROW)
+        activate(0, 0)
+        rest = best_of_four(0, 1)
         gather_neighbours(2, (0, 1))
         gather_neighbours(2, (2, 3))
-        for pair in range(2):
-            gelu_pair(1, pair, acts[:, pair, 1, :])
-        round_weights("out", 0, 0, offset=4 * ROW)
-        for pair in range(2):
-            edge_sums(2, pair, 3 + pair)
-            gelu_pair(2, pair, acts[:, pair, 2, :])
-
+        rest()
+        evacuate("y", 2)
+        evacuate("y", 3)
+        evacuate("e", 3, offset=7 * ROW - ROW // 2)
+        act_tiles(1, 2)
+        activate(1, 1)
+        open_edges(2, 0, 0)
+        open_edges(2, 1, 4)
         last = TILES - 1
+        gather_centres(2)
+        gather_centres(3)
         gather_neighbours(last, (0, 1))
-        edge_sums(last, 0, 6)
+        for pair in range(2):
+            turn_centres(2, pair, False)
+        round_weights("out", 0, 0, on_scalar)
+        activate(1, 2)
+
+        edges[last, 0] = bank([P, 2, 2, P], 5)
+        turn_centres(last, 0, True)
+        turn_neighbours(last, 0, False)
         first_two = sb.tile([P, 4, 2, RUN], BF16, name="first_two")
-        gelu_pair(last, 0, first_two[:].rearrange("p a i c -> p (a i c)"))
+        gelu_pair(last, 0, first_two[:])
         gather_neighbours(last, (2,))
-        third_sums = bank([P, 2, P], 7)
+        third_sums = bank([P, 2, P], 1)
         for half in range(2):
             turn(third_sums[:, half, :], half_of(centres[last], half), half == 0, False)
         for half in range(2):
             turn(third_sums[:, half, :], half_of(neighbours[last, 2], half), False, half == 1)
-        third = sb.tile([P, 4, RUN], BF16, name="third")
-        gelu(third[:].rearrange("p a c -> p (a c)"), third_sums[:].rearrange("p h c -> p (h c)"))
-
-        across_pairs = sb.tile([P, TILES - 1, 2, 2, 2, RUN], BF16, name="across_pairs")
-        largest(
-            across_pairs[:].rearrange("p t u h i c -> p (t u h i c)"),
-            acts[:, 0, :, :].rearrange("p t c -> p (t c)"),
-            acts[:, 1, :, :].rearrange("p t c -> p (t c)"),
-        )
-        of_two = sb.tile([P, 4, RUN], BF16, name="of_two")
-        largest(of_two[:], first_two[:, :, 0, :], first_two[:, :, 1, :])
+        third = sb.tile([P, 2, 2, RUN], BF16, name="third")
+        gelu(third[:], third_sums[:])
 
         fourth = []
         for half in range(2):
-            got = place([P, P], F32, "neighbours_last%d" % half, offset=6 * ROW + half * 4 * P)
+            got = place([P, P], F32, "neighbours_last%d" % half)
             entries = pos_lists[3][:, half * (P // 16) : (half + 1) * (P // 16)]
             nc.vector.tensor_copy(got[:], rows["e", last][:].indirect(entries))
-            fourth_sums = bank([P, P], (0, 5)[half])
-            turn(fourth_sums[:], half_of(centres[last], half), True, False)
-            turn(fourth_sums[:], got[:], False, True)
-            act = place([P, 2, RUN], BF16, "fourth%d" % half)
-            gelu(act[:].rearrange("p u c -> p (u c)"), fourth_sums[:])
+            fourth_sums = bank([P, 1, P], 2 + half)
+            turn(fourth_sums[:, 0, :], half_of(centres[last], half), True, False)
+            turn(fourth_sums[:, 0, :], got[:], False, True)
+            act = place([P, 1, 2, RUN], BF16, "fourth%d" % half)
+            gelu(act[:], fourth_sums[:])
             fourth.append(act)
 
+        rest = best_of_four(1, 2)
+        of_two = sb.tile([P, 4 * RUN], BF16, name="of_two")
+        pair_of = first_two[:].rearrange("p (i h) u c -> p i (h u c)", i=2)
+        largest(of_two[:], pair_of[:, 0, :], pair_of[:, 1, :])
+        rest()
         of_three = sb.tile([P, 2, 2, RUN], BF16, name="of_three")
-        largest(of_three[:].rearrange("p u h c -> p (u h) c"), of_two[:], third[:])
-        for t in range(last):
-            largest(z_blocks[:, :, :, t, :], across_pairs[:, t, :, :, 0, :], across_pairs[:, t, :, :, 1, :])
+        largest(of_three[:].rearrange("p h u c -> p (h u c)"), of_two[:], third[:].rearrange("p h u c -> p (h u c)"))
 
 
         z_rounded = []
         for half in range(2):
-            largest(z_blocks[:, :, half, last, :], of_three[:, :, half, :], fourth[half][:])
-            turned = bank([P, 2, P], 1 + half)
+            largest(z_blocks[:, 2 * half : 2 * half + 2, last, :], of_three[:, half], fourth[half][:, 0])
+            turned = bank([P, 2, P], 6 + half)
             for u in range(2):
                 nc.tensor.transpose(turned[:, u, :], z_words[:, half, u, :], ident[:])
             tile = place([P, P * PACK], BF16, "z_rounded%d" % half)
@@ -302,18 +335,17 @@ def tile_picked_edgecv_gelu_p_kernel(
             z_rounded.append(tile)
 
         quantise_weights("out", 0, 0, tag="fourth1")
-        w3_codes, w3_plane = quantised["out", 0, 0]
         out_rows = out.rearrange("(m p) v -> p m v", p=P)
         for half in range(2):
             z_codes, z_plane = quantise(z_rounded[half], "z%d" % half)
             result = sb.tile([P, N // P, P], F32, name="result%d" % half)
             for m in range(N // P):
-                acc = bank([P, P], ((3, 4), (6, 7))[half][m])
-                cols = slice(m * P, (m + 1) * P)
+                acc = bank([P, P], ((0, 4), (5, 1))[half][m])
+                w3_codes, w3_plane = quantised["out", m, 0]
                 nc.tensor.matmul_mx(
                     out=acc[:],
-                    lhsT=w3_codes[:, cols].bitcast(FP8X4),
-                    lhsT_scale=w3_plane[:, cols],
+                    lhsT=w3_codes.bitcast(FP8X4),
+                    lhsT_scale=w3_plane,
                     rhs=z_codes[:].bitcast(FP8X4),
                     rhs_scale=z_plane[:],
                     start=True,

@@ -70,10 +70,10 @@ def tile_picked_edgecv_gelu_p_kernel(
         offs_list = load_list(offs, "offs_list")
         x_word_rows = [sb.tile([P, T], U16, name="x_word_rows%d" % g) for g in range(PASSES)]
         nc.sync.dma_start(x_word_rows[0][:].bitcast(I32), x_words[0].bitcast(I32))
-        for q in range(P // QUADRANT):
-            (nc.sync, nc.scalar)[q % 2].dma_start(
-                x_scale_rows[QUADRANT * q : QUADRANT * q + 4 * PASSES, :].bitcast(I32),
-                x_scales[:, 4 * q : 4 * q + 4, :].bitcast(I32),
+        for r in range(4):
+            (nc.sync, nc.scalar)[r % 2].dma_start(
+                x_scale_rows[r : P : QUADRANT // 2, :].bitcast(I32),
+                x_scales[:, r : 16 : 4, :].rearrange("g q c -> q g c").bitcast(I32),
             )
         warm_in = sb.tile([P, 1], F32, name="warm_in")
         nc.vector.memset(warm_in[:], 0.0)
@@ -87,7 +87,7 @@ def tile_picked_edgecv_gelu_p_kernel(
 
         both_planes = sb.tile([P, S], U8, name="both_planes", align_bytes=64)
         nc.vector.tensor_copy(both_planes[:], x_scale_rows[:].indirect(offs_list[:]))
-        nc.sync.dma_start(second_plane[0:SHIFTED, :].bitcast(I32), both_planes[4 : 4 + SHIFTED, :].bitcast(I32))
+        nc.sync.dma_start(second_plane[0:SHIFTED, :].bitcast(I32), both_planes[P - SHIFTED :, :].bitcast(I32))
         x_planes = [both_planes, second_plane]
 
         load_weights("y", 0, 1, offset=0)
@@ -108,7 +108,7 @@ def tile_picked_edgecv_gelu_p_kernel(
             x_codes.append(words)
 
 
-        rounded, quantised, sums, rows, centres, neighbours, edges, acts = {}, {}, {}, {}, {}, {}, {}, {}
+        rounded, quantised, sums, rows, centres, neighbours, edges = {}, {}, {}, {}, {}, {}, {}
 
         def round_weights(kind, chunk, g, shares, part=(0, 1), tag=None):
             width = P * len(part)
@@ -172,16 +172,16 @@ def tile_picked_edgecv_gelu_p_kernel(
         def half_of(ap, half):
             return ap[:, half * P : (half + 1) * P]
 
-        slots = [(i, half) for i in range(2) for half in range(2)]
+        slots = [(half, i) for i in range(2) for half in range(2)]
 
         def turn_centres(t, pair, first):
-            for n, (i, half) in enumerate(slots):
-                turn(edges[t, pair][:, i, half, :], half_of(centres[t], half), first and n == 0, not first and n == 3)
+            for n, (half, i) in enumerate(slots):
+                turn(edges[t, pair][:, half, i, :], half_of(centres[t], half), first and n == 0, not first and n == 3)
 
         def turn_neighbours(t, pair, first):
-            for n, (i, half) in enumerate(slots):
+            for n, (half, i) in enumerate(slots):
                 src = half_of(neighbours[t, 2 * pair + i], half)
-                turn(edges[t, pair][:, i, half, :], src, first and n == 0, not first and n == 3)
+                turn(edges[t, pair][:, half, i, :], src, first and n == 0, not first and n == 3)
 
         def open_edges(t, pair, number):
             edges[t, pair] = bank([P, 2, 2, P], number)
@@ -193,34 +193,24 @@ def tile_picked_edgecv_gelu_p_kernel(
             )
 
         def gelu_pair(t, pair, dst):
-            gelu(dst, edges[t, pair][:].rearrange("p i h c -> p (i h) c"))
+            gelu(dst, edges[t, pair][:].rearrange("p h i c -> p (h i) c"))
 
         def largest(dst, a, b):
             nc.vector.tensor_tensor(dst, a, b, MAX)
 
-        z = sb.tile([P, 2 * H], BF16, name="z")
-        z_blocks = z[:].rearrange("p (a t c) -> p a t c", a=4, t=TILES)
-        z_words = z[:].bitcast(F32).rearrange("p (h u w) -> p h u w", h=2, u=2)
+        z = [sb.tile([P, H], BF16, name="z%d" % half) for half in range(2)]
+        z_blocks = [tile[:].rearrange("p (u t c) -> p u t c", u=2, t=TILES) for tile in z]
+        z_words = [tile[:].bitcast(F32).rearrange("p (u w) -> p u w", u=2) for tile in z]
 
         on_scalar, on_vector = [nc.scalar.copy], [nc.vector.tensor_copy]
 
 
-        def act_tiles(first, count, offset=None):
-            acts[first] = [
-                place([P, 4, 2, count, RUN], BF16, "acts%d%d" % (first, pair), offset=offset and offset + pair * count * ROW // 2)
-                for pair in range(2)
-            ]
+        last = TILES - 1
+        acts = []
 
-        def activate(first, t):
+        def activate(t):
             for pair in range(2):
-                gelu_pair(t, pair, acts[first][pair][:, :, :, t - first, :])
-
-        def best_of_four(first, count):
-            across = sb.tile([P, 2, 4, count * RUN], BF16, name="across%d" % first)
-            flat = [acts[first][pair][:].rearrange("p a u t c -> p (a u t c)") for pair in range(2)]
-            largest(across[:].rearrange("p i a c -> p (i a c)"), flat[0], flat[1])
-            dst = z_blocks[:, :, first : first + count, :].rearrange("p a t c -> p a (t c)")
-            return lambda: largest(dst, across[:, 0], across[:, 1])
+                gelu_pair(t, pair, acts[pair][:, :, :, t, :])
 
         round_weights("e", 0, 0, on_scalar)
         quantise_weights("e", 0, 0)
@@ -232,8 +222,10 @@ def tile_picked_edgecv_gelu_p_kernel(
         round_weights("y", 0, 0, on_scalar + on_vector)
         quantise_weights("y", 0, 0)
         evacuate("e", 0)
-        round_weights("y", 0, 1, on_vector)
-        quantise_weights("y", 0, 1)
+        for i in range(2):
+            round_weights("y", 0, 1, on_vector, (i,))
+        for i in range(2):
+            quantise_weights("y", 0, 1, (i,))
         product("y", 0, 2, order=(1, 0))
         product("y", 1, 3, order=(1, 0))
         gather_neighbours(0, (0, 1), offset=0)
@@ -263,36 +255,32 @@ def tile_picked_edgecv_gelu_p_kernel(
             quantise_weights("y", 1, g)
         product("y", 2, 2)
         product("y", 3, 3)
-        gather_centres(1, offset=6 * ROW)
+        gather_centres(1, offset=5 * ROW)
         for pair in range(2):
             turn_centres(1, pair, False)
         evacuate("e", 2, offset=4 * ROW)
-        act_tiles(0, 1, offset=5 * ROW)
-        activate(0, 0)
-        rest = best_of_four(0, 1)
+        both = place([P, 2, 4, 2, last, RUN], BF16, "acts", offset=6 * ROW + ROW // 2)
+        acts.extend(both[:, pair] for pair in range(2))
+        activate(0)
         gather_neighbours(2, (0, 1))
         gather_neighbours(2, (2, 3))
-        rest()
         evacuate("y", 2)
         evacuate("y", 3)
-        evacuate("e", 3, offset=7 * ROW - ROW // 2)
-        act_tiles(1, 2)
-        activate(1, 1)
+        evacuate("e", 3, offset=5 * ROW + ROW // 2)
+        activate(1)
         open_edges(2, 0, 0)
         open_edges(2, 1, 4)
-        last = TILES - 1
         gather_centres(2)
         gather_centres(3)
         gather_neighbours(last, (0, 1))
         for pair in range(2):
             turn_centres(2, pair, False)
-        round_weights("out", 0, 0, on_scalar)
-        activate(1, 2)
+        activate(2)
 
         edges[last, 0] = bank([P, 2, 2, P], 5)
         turn_centres(last, 0, True)
         turn_neighbours(last, 0, False)
-        first_two = sb.tile([P, 4, 2, RUN], BF16, name="first_two")
+        first_two = place([P, 4, 2, RUN], BF16, "first_two")
         gelu_pair(last, 0, first_two[:])
         gather_neighbours(last, (2,))
         third_sums = bank([P, 2, P], 1)
@@ -315,26 +303,40 @@ def tile_picked_edgecv_gelu_p_kernel(
             gelu(act[:], fourth_sums[:])
             fourth.append(act)
 
-        rest = best_of_four(1, 2)
-        of_two = sb.tile([P, 4 * RUN], BF16, name="of_two")
-        pair_of = first_two[:].rearrange("p (i h) u c -> p i (h u c)", i=2)
-        largest(of_two[:], pair_of[:, 0, :], pair_of[:, 1, :])
-        rest()
-        of_three = sb.tile([P, 2, 2, RUN], BF16, name="of_three")
-        largest(of_three[:].rearrange("p h u c -> p (h u c)"), of_two[:], third[:].rearrange("p h u c -> p (h u c)"))
+        across = [place([P, 2, 2, last * RUN], BF16, "across%d" % half) for half in range(2)]
+        late = [place([P, 2, RUN], BF16, "late%d" % half) for half in range(2)]
+        early = sb.tile([P, 2, 2 * RUN], BF16, name="early")
+
+        def across_banks(half):
+            flat = [acts[pair][:, 2 * half : 2 * half + 2].rearrange("p a u t c -> p (a u t c)") for pair in range(2)]
+            largest(across[half][:].rearrange("p i u c -> p (i u c)"), flat[0], flat[1])
+
+        def within_bank(half):
+            dst = z_blocks[half][:, :, :last, :].rearrange("p u t c -> p u (t c)")
+            largest(dst, across[half][:, 0], across[half][:, 1])
+
+        pair_of = first_two[:].rearrange("p (h i) u c -> p i h (u c)", i=2)
+        for half in range(2):
+            across_banks(half)
+        within_bank(0)
+        largest(early[:], pair_of[:, 0], pair_of[:, 1])
+        largest(late[0][:], third[:, 0], fourth[0][:, 0])
+        within_bank(1)
+        largest(late[1][:], third[:, 1], fourth[1][:, 0])
+        round_weights("out", 0, 0, on_scalar, tag="first_two")
 
 
         z_rounded = []
         for half in range(2):
-            largest(z_blocks[:, 2 * half : 2 * half + 2, last, :], of_three[:, half], fourth[half][:, 0])
+            largest(z_blocks[half][:, :, last, :], early[:, half].rearrange("p (u c) -> p u c", u=2), late[half][:])
             turned = bank([P, 2, P], 6 + half)
             for u in range(2):
-                nc.tensor.transpose(turned[:, u, :], z_words[:, half, u, :], ident[:])
+                nc.tensor.transpose(turned[:, u, :], z_words[half][:, u, :], ident[:])
             tile = place([P, P * PACK], BF16, "z_rounded%d" % half)
             nc.scalar.copy(tile[:].bitcast(F32).rearrange("p (v u) -> p v u", u=2), turned[:].rearrange("p u v -> p v u"))
             z_rounded.append(tile)
 
-        quantise_weights("out", 0, 0, tag="fourth1")
+        quantise_weights("out", 0, 0)
         out_rows = out.rearrange("(m p) v -> p m v", p=P)
         for half in range(2):
             z_codes, z_plane = quantise(z_rounded[half], "z%d" % half)

@@ -21,12 +21,17 @@ P = 128
 PACK = 4
 K_PASS = P * PACK
 PASSES = K // K_PASS
-QUADRANT = 32
+SCALE_ROWS = 4
+SHIFT = 16
 CHUNK = 2 * P
 TILES = H // P
+LAST = TILES - 1
 RUN = P // 2
 ROW = 4 * S
-SHIFTED = 112
+
+RAW_Y01, NEIGHBOURS_0 = 0, (0, ROW)
+RAW_E11, CENTRES_0, NEIGHBOURS_1 = 3 * ROW, 3 * ROW, 4 * ROW
+RAW_Y11, ROW_E2, ROW_Y1, ACTS = 6 * ROW, 5 * ROW + ROW // 2, 6 * ROW + ROW // 2, 7 * ROW + ROW // 2
 
 
 def tile_picked_edgecv_gelu_p_kernel(
@@ -61,51 +66,54 @@ def tile_picked_edgecv_gelu_p_kernel(
             nc.sync.dma_start(tile[:], rows.rearrange("(p j) c -> p j c", j=PACK))
             raw[kind, chunk, g] = tile
 
-        x_scale_rows = sb.tile([P, T], U8, name="x_scale_rows", align_bytes=64)
+        x_scale_rows = place([P, T], U8, "x_scale_rows")
         nc.gpsimd.memset(x_scale_rows[:, : T // 2].bitcast(I32), 0)
         nc.vector.memset(x_scale_rows[:, T // 2 :].bitcast(I32), 0)
-        second_plane = sb.tile([P, S], U8, name="second_plane", align_bytes=64)
-        nc.gpsimd.memset(second_plane[:].bitcast(I32), 0)
+        second_scales = place([P, S], U8, "second_scales")
+        nc.gpsimd.memset(second_scales[:].bitcast(I32), 0)
 
         offs_list = load_list(offs, "offs_list")
         x_word_rows = [sb.tile([P, T], U16, name="x_word_rows%d" % g) for g in range(PASSES)]
         nc.sync.dma_start(x_word_rows[0][:].bitcast(I32), x_words[0].bitcast(I32))
-        for r in range(4):
+        for r in range(SCALE_ROWS):
             (nc.sync, nc.scalar)[r % 2].dma_start(
-                x_scale_rows[r : P : QUADRANT // 2, :].bitcast(I32),
-                x_scales[:, r : 16 : 4, :].rearrange("g q c -> q g c").bitcast(I32),
+                x_scale_rows[r:P:SHIFT, :].bitcast(I32),
+                x_scales[:, r::SCALE_ROWS, :].rearrange("g q c -> q g c").bitcast(I32),
             )
         warm_in = sb.tile([P, 1], F32, name="warm_in")
         nc.vector.memset(warm_in[:], 0.0)
         warm_out = sb.tile([P, 1], F32, name="warm_out")
         nc.scalar.activation(warm_out[:], warm_in[:], GELU)
-        nc.sync.dma_start(x_word_rows[1][:].bitcast(I32), x_words[1].bitcast(I32))
         load_weights("e", 0, 0)
+        nc.sync.dma_start(x_word_rows[1][:].bitcast(I32), x_words[1].bitcast(I32))
         load_weights("e", 0, 1)
         load_weights("y", 0, 0)
         pos_lists = [load_list(src, "pos%d_list" % (d + 1)) for d, src in enumerate((pos1, pos2, pos3, pos4))]
 
-        both_planes = sb.tile([P, S], U8, name="both_planes", align_bytes=64)
-        nc.vector.tensor_copy(both_planes[:], x_scale_rows[:].indirect(offs_list[:]))
-        nc.sync.dma_start(second_plane[0:SHIFTED, :].bitcast(I32), both_planes[P - SHIFTED :, :].bitcast(I32))
-        x_planes = [both_planes, second_plane]
+        both_scales = place([P, S], U8, "both_scales")
+        nc.vector.tensor_copy(both_scales[:], x_scale_rows[:].indirect(offs_list[:]))
+        nc.sync.dma_start(second_scales[: P - SHIFT, :].bitcast(I32), both_scales[SHIFT:, :].bitcast(I32))
+        x_scale_bytes = [both_scales, second_scales]
 
-        load_weights("y", 0, 1, offset=0)
+        load_weights("y", 0, 1, offset=RAW_Y01)
         load_weights("e", 1, 0)
         cen_list = load_list(cen, "cen_list")
-        load_weights("e", 1, 1, offset=2 * ROW)
+        load_weights("e", 1, 1, offset=RAW_E11)
         load_weights("y", 1, 0)
-        load_weights("y", 1, 1, offset=5 * ROW - ROW // 4)
+        load_weights("y", 1, 1, offset=RAW_Y11)
         load_weights("out", 0, 0)
 
         ident = sb.tile([P, P], F32, name="ident")
         make_identity(nc, ident[:])
 
         x_codes = []
-        for g in range(PASSES):
-            words = place([P, S], U16, "x_codes%d" % g, tag="x_scale_rows" if g == 0 else None)
+
+        def gather_words(g, tag):
+            words = place([P, S], U16, "x_codes%d" % g, tag=tag)
             nc.vector.tensor_copy(words[:], x_word_rows[g][:].indirect(offs_list[:]))
             x_codes.append(words)
+
+        gather_words(0, "x_scale_rows")
 
 
         rounded, quantised, sums, rows, centres, neighbours, edges = {}, {}, {}, {}, {}, {}, {}
@@ -122,29 +130,29 @@ def tile_picked_edgecv_gelu_p_kernel(
                 )
             rounded[kind, chunk, g, part] = tile
 
-        def quantise(values, name, tag=None):
+        def quantise(values, name):
             width = values.shape[1] // PACK
-            codes = place([P, width], U32, name + "_codes", tag=tag)
-            plane = place([P, width], U8, name + "_plane")
-            nc.vector.quantize_mx(out=codes[:].bitcast(FP8X4), scales=plane[:], in_=values[:])
-            return codes, plane
+            codes = place([P, width], U32, name + "_codes")
+            scales = place([P, width], U8, name + "_scales")
+            nc.vector.quantize_mx(out=codes[:].bitcast(FP8X4), scales=scales[:], in_=values[:])
+            return codes, scales
 
-        def quantise_weights(kind, chunk, g, part=(0, 1), tag=None):
-            codes, plane = quantise(rounded[kind, chunk, g, part], "%s%d%d%d" % (kind, chunk, g, part[0]), tag)
+        def quantise_weights(kind, chunk, g, part=(0, 1)):
+            codes, scales = quantise(rounded[kind, chunk, g, part], "%s%d%d%d" % (kind, chunk, g, part[0]))
             for n, i in enumerate(part):
                 cols = slice(n * P, (n + 1) * P)
-                quantised[kind, 2 * chunk + i, g] = codes[:, cols], plane[:, cols]
+                quantised[kind, 2 * chunk + i, g] = codes[:, cols], scales[:, cols]
 
         def product(kind, t, number, order=(0, 1)):
             acc = bank([P, S], number)
             for g in order:
-                codes, plane = quantised[kind, t, g]
+                codes, scales = quantised[kind, t, g]
                 nc.tensor.matmul_mx(
                     out=acc[:],
                     lhsT=codes.bitcast(FP8X4),
-                    lhsT_scale=plane,
+                    lhsT_scale=scales,
                     rhs=x_codes[g][:].bitcast(FP4X4),
-                    rhs_scale=x_planes[g][:],
+                    rhs_scale=x_scale_bytes[g][:],
                     start=(g == order[0]),
                     stop=(g == order[-1]),
                 )
@@ -166,8 +174,8 @@ def tile_picked_edgecv_gelu_p_kernel(
                 nc.vector.tensor_copy(got[:, i, :], rows["e", t][:].indirect(pos_lists[d][:]))
                 neighbours[t, d] = got[:, i, :]
 
-        def turn(dst, src, first, last):
-            nc.tensor.matmul(dst, src, ident[:], start=first, stop=last, is_transpose=True)
+        def turn(dst, src, first, final):
+            nc.tensor.matmul(dst, src, ident[:], start=first, stop=final, is_transpose=True)
 
         def half_of(ap, half):
             return ap[:, half * P : (half + 1) * P]
@@ -205,45 +213,37 @@ def tile_picked_edgecv_gelu_p_kernel(
         on_scalar, on_vector = [nc.scalar.copy], [nc.vector.tensor_copy]
 
 
-        last = TILES - 1
-        acts = []
-
-        def activate(t):
-            for pair in range(2):
-                gelu_pair(t, pair, acts[pair][:, :, :, t, :])
-
         round_weights("e", 0, 0, on_scalar)
         quantise_weights("e", 0, 0)
+        gather_words(1, "raw_e00")
         for i in range(2):
             round_weights("e", 0, 1, on_scalar, (i,))
             quantise_weights("e", 0, 1, (i,))
         product("e", 0, 0)
-        product("e", 1, 1, order=(1, 0))
+        product("e", 1, 1)
         round_weights("y", 0, 0, on_scalar + on_vector)
         quantise_weights("y", 0, 0)
         evacuate("e", 0)
+        evacuate("e", 1)
         for i in range(2):
             round_weights("y", 0, 1, on_vector, (i,))
         for i in range(2):
             quantise_weights("y", 0, 1, (i,))
         product("y", 0, 2, order=(1, 0))
         product("y", 1, 3, order=(1, 0))
-        gather_neighbours(0, (0, 1), offset=0)
-        open_edges(0, 0, 4)
-        gather_neighbours(0, (2, 3), offset=ROW)
-        open_edges(0, 1, 5)
+        for pair in range(2):
+            gather_neighbours(0, (2 * pair, 2 * pair + 1), offset=NEIGHBOURS_0[pair])
+            open_edges(0, pair, 4 + pair)
         round_weights("e", 1, 0, on_scalar, tag="e010_codes")
         quantise_weights("e", 1, 0)
         evacuate("y", 0)
-        evacuate("e", 1, tag="raw_e10")
-        gather_neighbours(1, (0, 1))
+        gather_neighbours(1, (0, 1), tag="raw_e10")
         round_weights("e", 1, 1, on_scalar, tag="e011_codes")
         quantise_weights("e", 1, 1)
         product("e", 2, 0)
         product("e", 3, 1)
-        evacuate("y", 1)
-        gather_centres(0, offset=2 * ROW)
-        gather_neighbours(1, (2, 3), offset=3 * ROW)
+        gather_centres(0, offset=CENTRES_0)
+        gather_neighbours(1, (2, 3), offset=NEIGHBOURS_1)
         open_edges(1, 0, 6)
         for pair in range(2):
             turn_centres(0, pair, False)
@@ -254,40 +254,45 @@ def tile_picked_edgecv_gelu_p_kernel(
             round_weights("y", 1, g, on_scalar)
             quantise_weights("y", 1, g)
         product("y", 2, 2)
+        evacuate("y", 1, offset=ROW_Y1)
         product("y", 3, 3)
-        gather_centres(1, offset=5 * ROW)
+        evacuate("e", 2, offset=ROW_E2)
+        gather_centres(1)
         for pair in range(2):
             turn_centres(1, pair, False)
-        evacuate("e", 2, offset=4 * ROW)
-        both = place([P, 2, 4, 2, last, RUN], BF16, "acts", offset=6 * ROW + ROW // 2)
-        acts.extend(both[:, pair] for pair in range(2))
+        acts = place([P, 2, 4, 2, LAST, RUN], BF16, "acts", offset=ACTS)
+
+        def activate(t):
+            for pair in range(2):
+                gelu_pair(t, pair, acts[:, pair, :, :, t, :])
+
         activate(0)
         gather_neighbours(2, (0, 1))
         gather_neighbours(2, (2, 3))
         evacuate("y", 2)
         evacuate("y", 3)
-        evacuate("e", 3, offset=5 * ROW + ROW // 2)
+        evacuate("e", 3, tag="rounded_y110")
         activate(1)
         open_edges(2, 0, 0)
         open_edges(2, 1, 4)
         gather_centres(2)
         gather_centres(3)
-        gather_neighbours(last, (0, 1))
+        gather_neighbours(LAST, (0, 1))
         for pair in range(2):
             turn_centres(2, pair, False)
         activate(2)
 
-        edges[last, 0] = bank([P, 2, 2, P], 5)
-        turn_centres(last, 0, True)
-        turn_neighbours(last, 0, False)
+        edges[LAST, 0] = bank([P, 2, 2, P], 5)
+        turn_centres(LAST, 0, True)
+        turn_neighbours(LAST, 0, False)
         first_two = place([P, 4, 2, RUN], BF16, "first_two")
-        gelu_pair(last, 0, first_two[:])
-        gather_neighbours(last, (2,))
+        gelu_pair(LAST, 0, first_two[:])
+        gather_neighbours(LAST, (2,))
         third_sums = bank([P, 2, P], 1)
         for half in range(2):
-            turn(third_sums[:, half, :], half_of(centres[last], half), half == 0, False)
+            turn(third_sums[:, half, :], half_of(centres[LAST], half), half == 0, False)
         for half in range(2):
-            turn(third_sums[:, half, :], half_of(neighbours[last, 2], half), False, half == 1)
+            turn(third_sums[:, half, :], half_of(neighbours[LAST, 2], half), False, half == 1)
         third = sb.tile([P, 2, 2, RUN], BF16, name="third")
         gelu(third[:], third_sums[:])
 
@@ -295,24 +300,25 @@ def tile_picked_edgecv_gelu_p_kernel(
         for half in range(2):
             got = place([P, P], F32, "neighbours_last%d" % half)
             entries = pos_lists[3][:, half * (P // 16) : (half + 1) * (P // 16)]
-            nc.vector.tensor_copy(got[:], rows["e", last][:].indirect(entries))
+            nc.vector.tensor_copy(got[:], rows["e", LAST][:].indirect(entries))
             fourth_sums = bank([P, 1, P], 2 + half)
-            turn(fourth_sums[:, 0, :], half_of(centres[last], half), True, False)
+            turn(fourth_sums[:, 0, :], half_of(centres[LAST], half), True, False)
             turn(fourth_sums[:, 0, :], got[:], False, True)
             act = place([P, 1, 2, RUN], BF16, "fourth%d" % half)
             gelu(act[:], fourth_sums[:])
             fourth.append(act)
 
-        across = [place([P, 2, 2, last * RUN], BF16, "across%d" % half) for half in range(2)]
+
+        across = [place([P, 2, 2, LAST * RUN], BF16, "across%d" % half) for half in range(2)]
         late = [place([P, 2, RUN], BF16, "late%d" % half) for half in range(2)]
         early = sb.tile([P, 2, 2 * RUN], BF16, name="early")
 
         def across_banks(half):
-            flat = [acts[pair][:, 2 * half : 2 * half + 2].rearrange("p a u t c -> p (a u t c)") for pair in range(2)]
+            flat = [acts[:, pair, 2 * half : 2 * half + 2].rearrange("p a u t c -> p (a u t c)") for pair in range(2)]
             largest(across[half][:].rearrange("p i u c -> p (i u c)"), flat[0], flat[1])
 
         def within_bank(half):
-            dst = z_blocks[half][:, :, :last, :].rearrange("p u t c -> p u (t c)")
+            dst = z_blocks[half][:, :, :LAST, :].rearrange("p u t c -> p u (t c)")
             largest(dst, across[half][:, 0], across[half][:, 1])
 
         pair_of = first_two[:].rearrange("p (h i) u c -> p i h (u c)", i=2)
@@ -328,7 +334,7 @@ def tile_picked_edgecv_gelu_p_kernel(
 
         z_rounded = []
         for half in range(2):
-            largest(z_blocks[half][:, :, last, :], early[:, half].rearrange("p (u c) -> p u c", u=2), late[half][:])
+            largest(z_blocks[half][:, :, LAST, :], early[:, half].rearrange("p (u c) -> p u c", u=2), late[half][:])
             turned = bank([P, 2, P], 6 + half)
             for u in range(2):
                 nc.tensor.transpose(turned[:, u, :], z_words[half][:, u, :], ident[:])
@@ -339,17 +345,17 @@ def tile_picked_edgecv_gelu_p_kernel(
         quantise_weights("out", 0, 0)
         out_rows = out.rearrange("(m p) v -> p m v", p=P)
         for half in range(2):
-            z_codes, z_plane = quantise(z_rounded[half], "z%d" % half)
+            z_codes, z_scales = quantise(z_rounded[half], "z%d" % half)
             result = sb.tile([P, N // P, P], F32, name="result%d" % half)
             for m in range(N // P):
                 acc = bank([P, P], ((0, 4), (5, 1))[half][m])
-                w3_codes, w3_plane = quantised["out", m, 0]
+                w3_codes, w3_scales = quantised["out", m, 0]
                 nc.tensor.matmul_mx(
                     out=acc[:],
                     lhsT=w3_codes.bitcast(FP8X4),
-                    lhsT_scale=w3_plane,
+                    lhsT_scale=w3_scales,
                     rhs=z_codes[:].bitcast(FP8X4),
-                    rhs_scale=z_plane[:],
+                    rhs_scale=z_scales[:],
                     start=True,
                     stop=True,
                 )

@@ -84,8 +84,8 @@ def tile_picked_edgecv_gelu_p_kernel(
         nc.vector.memset(warm_in[:], 0.0)
         warm_out = sb.tile([P, 1], F32, name="warm_out")
         nc.scalar.activation(warm_out[:], warm_in[:], GELU)
-        load_weights("e", 0, 0)
         nc.sync.dma_start(x_word_rows[1][:].bitcast(I32), x_words[1].bitcast(I32))
+        load_weights("e", 0, 0)
         load_weights("e", 0, 1)
         load_weights("y", 0, 0)
         pos_lists = [load_list(src, "pos%d_list" % (d + 1)) for d, src in enumerate((pos1, pos2, pos3, pos4))]
@@ -97,8 +97,8 @@ def tile_picked_edgecv_gelu_p_kernel(
 
         load_weights("y", 0, 1, offset=RAW_Y01)
         load_weights("e", 1, 0)
-        cen_list = load_list(cen, "cen_list")
         load_weights("e", 1, 1, offset=RAW_E11)
+        cen_list = load_list(cen, "cen_list")
         load_weights("y", 1, 0)
         load_weights("y", 1, 1, offset=RAW_Y11)
         load_weights("out", 0, 0)
@@ -106,14 +106,9 @@ def tile_picked_edgecv_gelu_p_kernel(
         ident = sb.tile([P, P], F32, name="ident")
         make_identity(nc, ident[:])
 
-        x_codes = []
-
-        def gather_words(g, tag):
-            words = place([P, S], U16, "x_codes%d" % g, tag=tag)
-            nc.vector.tensor_copy(words[:], x_word_rows[g][:].indirect(offs_list[:]))
-            x_codes.append(words)
-
-        gather_words(0, "x_scale_rows")
+        x_codes = [place([P, S], U16, "x_codes0", tag="x_scale_rows"), place([P, S], U16, "x_codes1")]
+        for g in range(PASSES):
+            nc.vector.tensor_copy(x_codes[g][:], x_word_rows[g][:].indirect(offs_list[:]))
 
 
         rounded, quantised, sums, rows, centres, neighbours, edges = {}, {}, {}, {}, {}, {}, {}
@@ -215,12 +210,11 @@ def tile_picked_edgecv_gelu_p_kernel(
 
         round_weights("e", 0, 0, on_scalar)
         quantise_weights("e", 0, 0)
-        gather_words(1, "raw_e00")
         for i in range(2):
             round_weights("e", 0, 1, on_scalar, (i,))
             quantise_weights("e", 0, 1, (i,))
         product("e", 0, 0)
-        product("e", 1, 1)
+        product("e", 1, 1, order=(1, 0))
         round_weights("y", 0, 0, on_scalar + on_vector)
         quantise_weights("y", 0, 0)
         evacuate("e", 0)

@@ -23,15 +23,15 @@ K_PASS = P * PACK
 PASSES = K // K_PASS
 SCALE_ROWS = 4
 SHIFT = 16
-CHUNK = 2 * P
 TILES = H // P
 LAST = TILES - 1
 RUN = P // 2
 ROW = 4 * S
-
-RAW_Y01, NEIGHBOURS_0 = 0, (0, ROW)
-RAW_E11, CENTRES_0, NEIGHBOURS_1 = 3 * ROW, 3 * ROW, 4 * ROW
-RAW_Y11, ROW_E2, ROW_Y1, ACTS = 6 * ROW, 5 * ROW + ROW // 2, 6 * ROW + ROW // 2, 7 * ROW + ROW // 2
+MULT, ADD = mybir.AluOpType.mult, mybir.AluOpType.add
+CHUNK = 2 * P
+SHARE = 96
+QUARTER = 4 * V
+ROOM = 8 * QUARTER
 
 
 def tile_picked_edgecv_gelu_p_kernel(
@@ -48,6 +48,9 @@ def tile_picked_edgecv_gelu_p_kernel(
                 return sb.tile(shape, dtype, name=name, tag=tag or name, align_bytes=64)
             return shared.tile(shape, dtype, name=name, offset=offset, align_bytes=64)
 
+        def behind(kind, chunk, g, quarter):
+            return raw_offset[kind, chunk, g] + int(quarter * QUARTER)
+
         def bank(shape, number):
             return ps.tile(shape, F32, name="bank", tag="bank%d" % number)
 
@@ -57,20 +60,19 @@ def tile_picked_edgecv_gelu_p_kernel(
             nc.sync.dma_start(lst[:], src)
             return lst
 
-        raw = {}
+        raw, raw_offset = {}, {}
 
-        def load_weights(kind, chunk, g, offset=None):
+        def load_weights(kind, tiles, g):
             w = {"y": w1, "e": w2, "out": w3}[kind]
-            tile = place([P, PACK, CHUNK], F32, "raw_%s%d%d" % (kind, chunk, g), offset=offset)
-            rows = w[g * K_PASS : (g + 1) * K_PASS, chunk * CHUNK : (chunk + 1) * CHUNK]
+            raw_offset[kind, tiles[0], g] = offset = len(raw_offset) * ROOM + 2 * QUARTER
+            tile = place([P, PACK, P * len(tiles)], F32, "raw_%s%d%d" % (kind, tiles[0], g), offset=offset)
+            rows = w[g * K_PASS : (g + 1) * K_PASS, tiles[0] * P : (tiles[-1] + 1) * P]
             nc.sync.dma_start(tile[:], rows.rearrange("(p j) c -> p j c", j=PACK))
-            raw[kind, chunk, g] = tile
+            for n, t in enumerate(tiles):
+                raw[kind, t, g] = tile, n * P
 
         x_scale_rows = place([P, T], U8, "x_scale_rows")
-        nc.gpsimd.memset(x_scale_rows[:, : T // 2].bitcast(I32), 0)
-        nc.vector.memset(x_scale_rows[:, T // 2 :].bitcast(I32), 0)
-        second_scales = place([P, S], U8, "second_scales")
-        nc.gpsimd.memset(second_scales[:].bitcast(I32), 0)
+        nc.vector.memset(x_scale_rows[:].bitcast(I32), 0)
 
         offs_list = load_list(offs, "offs_list")
         x_word_rows = [sb.tile([P, T], U16, name="x_word_rows%d" % g) for g in range(PASSES)]
@@ -85,26 +87,29 @@ def tile_picked_edgecv_gelu_p_kernel(
         warm_out = sb.tile([P, 1], F32, name="warm_out")
         nc.scalar.activation(warm_out[:], warm_in[:], GELU)
         nc.sync.dma_start(x_word_rows[1][:].bitcast(I32), x_words[1].bitcast(I32))
-        load_weights("e", 0, 0)
-        load_weights("e", 0, 1)
-        load_weights("y", 0, 0)
+        second_scales = place([P, S], U8, "second_scales")
+        nc.vector.memset(second_scales[:].bitcast(I32), 0)
+        ident = sb.tile([P, P], F32, name="ident")
+        nc.vector.memset(ident[:], 0.0)
+        make_identity(nc, ident[:], nomemset=True)
+        load_weights("e", (0, 1), 0)
+        load_weights("e", (0, 1), 1)
         pos_lists = [load_list(src, "pos%d_list" % (d + 1)) for d, src in enumerate((pos1, pos2, pos3, pos4))]
+        cen_list = load_list(cen, "cen_list")
 
         both_scales = place([P, S], U8, "both_scales")
         nc.vector.tensor_copy(both_scales[:], x_scale_rows[:].indirect(offs_list[:]))
         nc.sync.dma_start(second_scales[: P - SHIFT, :].bitcast(I32), both_scales[SHIFT:, :].bitcast(I32))
         x_scale_bytes = [both_scales, second_scales]
 
-        load_weights("y", 0, 1, offset=RAW_Y01)
-        load_weights("e", 1, 0)
-        load_weights("e", 1, 1, offset=RAW_E11)
-        cen_list = load_list(cen, "cen_list")
-        load_weights("y", 1, 0)
-        load_weights("y", 1, 1, offset=RAW_Y11)
-        load_weights("out", 0, 0)
-
-        ident = sb.tile([P, P], F32, name="ident")
-        make_identity(nc, ident[:])
+        load_weights("y", (0, 1), 0)
+        load_weights("y", (0, 1), 1)
+        load_weights("y", (2, 3), 0)
+        load_weights("y", (2, 3), 1)
+        load_weights("e", (2, 3), 0)
+        load_weights("e", (2,), 1)
+        load_weights("e", (3,), 1)
+        load_weights("out", (0, 1), 0)
 
         x_codes = [place([P, S], U16, "x_codes0", tag="x_scale_rows"), place([P, S], U16, "x_codes1")]
         for g in range(PASSES):
@@ -112,62 +117,91 @@ def tile_picked_edgecv_gelu_p_kernel(
 
 
         rounded, quantised, sums, rows, centres, neighbours, edges = {}, {}, {}, {}, {}, {}, {}
+        on_scalar, on_vector = nc.scalar.copy, nc.vector.tensor_copy
+        WIDTH = P * PACK
 
-        def round_weights(kind, chunk, g, shares, part=(0, 1), tag=None):
-            width = P * len(part)
-            tile = place([P, width * PACK], BF16, "rounded_%s%d%d%d" % (kind, chunk, g, part[0]), tag=tag)
-            step = width // len(shares)
-            for n, copy in enumerate(shares):
-                first = part[0] * P + n * step
-                copy(
-                    tile[:, n * step * PACK : (n + 1) * step * PACK].rearrange("p (c i j) -> p c j i", i=4, j=PACK),
-                    raw[kind, chunk, g][:, :, first : first + step].rearrange("p j (c i) -> p c j i", i=4),
-                )
-            rounded[kind, chunk, g, part] = tile
+        def on_gpsimd(dst, src):
+            nc.gpsimd.tensor_scalar(
+                dst.rearrange("p c j i -> p c i j"), src.rearrange("p c j i -> p c i j"), 1.0, 0.0, MULT, ADD
+            )
 
-        def quantise(values, name):
+        def round_weights(kind, tiles, g, copy, key, slot=0, slots=None, tag=None):
+            if key not in rounded:
+                rounded[key] = place([P, (slots or len(tiles)) * WIDTH], BF16, "rounded_%s" % key, tag=tag), []
+            tile, parts = rounded[key]
+            source, first = raw[kind, tiles[0], g]
+            copy(
+                tile[:, slot * WIDTH : (slot + len(tiles)) * WIDTH].rearrange("p (c i j) -> p c j i", i=4, j=PACK),
+                source[:, :, first : first + P * len(tiles)].rearrange("p j (c i) -> p c j i", i=4),
+            )
+            parts.extend((slot + n, (kind, t, g)) for n, t in enumerate(tiles))
+
+        own = (CHUNK - SHARE) * PACK
+        ring = place([P, 2 * own + SHARE * PACK], BF16, "ring")
+
+        def interleave(copy, dst, kind, chunk, g, first, count):
+            copy(
+                dst.rearrange("p (c i j) -> p c j i", i=4, j=PACK),
+                raw[kind, chunk, g][0][:, :, first : first + count].rearrange("p j (c i) -> p c j i", i=4),
+            )
+
+        def share_rounding(kind, chunk, g, left):
+            start = 0 if left else own
+            rounded[kind, chunk, g] = ring[:, start : start + CHUNK * PACK], [(n, (kind, chunk + n, g)) for n in range(2)]
+            side = ring[:, :own] if left else ring[:, own + SHARE * PACK :]
+            interleave(on_scalar, side, kind, chunk, g, 0 if left else SHARE, CHUNK - SHARE)
+            interleave(on_gpsimd, ring[:, own : own + SHARE * PACK], kind, chunk, g, CHUNK - SHARE if left else 0, SHARE)
+
+        def quantise(values, name, tag=None):
             width = values.shape[1] // PACK
-            codes = place([P, width], U32, name + "_codes")
+            codes = place([P, width], U32, name + "_codes", tag=tag)
             scales = place([P, width], U8, name + "_scales")
             nc.vector.quantize_mx(out=codes[:].bitcast(FP8X4), scales=scales[:], in_=values[:])
             return codes, scales
 
-        def quantise_weights(kind, chunk, g, part=(0, 1)):
-            codes, scales = quantise(rounded[kind, chunk, g, part], "%s%d%d%d" % (kind, chunk, g, part[0]))
-            for n, i in enumerate(part):
-                cols = slice(n * P, (n + 1) * P)
-                quantised[kind, 2 * chunk + i, g] = codes[:, cols], scales[:, cols]
+        def quantise_weights(key, tag=None):
+            tile, parts = rounded[key]
+            codes, scales = quantise(tile, key if isinstance(key, str) else "%s%d%d" % key, tag)
+            for slot, which in parts:
+                cols = slice(slot * P, (slot + 1) * P)
+                quantised[which] = codes[:, cols], scales[:, cols]
 
-        def product(kind, t, number, order=(0, 1)):
-            acc = bank([P, S], number)
-            for g in order:
-                codes, scales = quantised[kind, t, g]
-                nc.tensor.matmul_mx(
-                    out=acc[:],
-                    lhsT=codes.bitcast(FP8X4),
-                    lhsT_scale=scales,
-                    rhs=x_codes[g][:].bitcast(FP4X4),
-                    rhs_scale=x_scale_bytes[g][:],
-                    start=(g == order[0]),
-                    stop=(g == order[-1]),
-                )
-            sums[kind, t] = acc
+        def one_pass(kind, t, g, number=None):
+            if number is not None:
+                sums[kind, t] = bank([P, S], number)
+            codes, scales = quantised[kind, t, g]
+            nc.tensor.matmul_mx(
+                out=sums[kind, t][:],
+                lhsT=codes.bitcast(FP8X4),
+                lhsT_scale=scales,
+                rhs=x_codes[g][:].bitcast(FP4X4),
+                rhs_scale=x_scale_bytes[g][:],
+                start=number is not None,
+                stop=number is None,
+            )
+
+        def open_sums(kind, chunk, numbers):
+            for n in range(2):
+                one_pass(kind, chunk + n, 0, numbers[n])
+
+        def close_sums(kind, chunk):
+            for n in range(2):
+                one_pass(kind, chunk + n, 1)
 
         def evacuate(kind, t, tag=None, offset=None):
             row = place([P, S], F32, "row_%s%d" % (kind, t), tag=tag, offset=offset)
             nc.scalar.copy(row[:], sums[kind, t][:])
             rows[kind, t] = row
 
-        def gather_centres(t, offset=None):
-            got = place([P, V], F32, "centres%d" % t, offset=offset)
+        def gather_centres(t, tag=None, offset=None):
+            got = place([P, V], F32, "centres%d" % t, tag=tag, offset=offset)
             nc.vector.tensor_copy(got[:], rows["y", t][:].indirect(cen_list[:]))
             centres[t] = got[:]
 
-        def gather_neighbours(t, ds, tag=None, offset=None):
-            got = place([P, len(ds), V], F32, "neighbours%d%d" % (t, ds[0]), tag=tag, offset=offset)
-            for i, d in enumerate(ds):
-                nc.vector.tensor_copy(got[:, i, :], rows["e", t][:].indirect(pos_lists[d][:]))
-                neighbours[t, d] = got[:, i, :]
+        def gather_neighbour(t, d, tag=None, offset=None):
+            got = place([P, V], F32, "neighbours%d%d" % (t, d), tag=tag, offset=offset)
+            nc.vector.tensor_copy(got[:], rows["e", t][:].indirect(pos_lists[d][:]))
+            neighbours[t, d] = got[:]
 
         def turn(dst, src, first, final):
             nc.tensor.matmul(dst, src, ident[:], start=first, stop=final, is_transpose=True)
@@ -188,7 +222,6 @@ def tile_picked_edgecv_gelu_p_kernel(
 
         def open_edges(t, pair, number):
             edges[t, pair] = bank([P, 2, 2, P], number)
-            turn_neighbours(t, pair, True)
 
         def gelu(dst, src):
             nc.scalar.activation(
@@ -205,86 +238,101 @@ def tile_picked_edgecv_gelu_p_kernel(
         z_blocks = [tile[:].rearrange("p (u t c) -> p u t c", u=2, t=TILES) for tile in z]
         z_words = [tile[:].bitcast(F32).rearrange("p (u w) -> p u w", u=2) for tile in z]
 
-        on_scalar, on_vector = [nc.scalar.copy], [nc.vector.tensor_copy]
-
-
-        round_weights("e", 0, 0, on_scalar)
-        quantise_weights("e", 0, 0)
-        for i in range(2):
-            round_weights("e", 0, 1, on_scalar, (i,))
-            quantise_weights("e", 0, 1, (i,))
-        product("e", 0, 0)
-        product("e", 1, 1, order=(1, 0))
-        round_weights("y", 0, 0, on_scalar + on_vector)
-        quantise_weights("y", 0, 0)
+        round_weights("e", (0, 1), 0, on_scalar, "e010")
+        quantise_weights("e010")
+        for t in range(2):
+            round_weights("e", (t,), 1, on_scalar, "e%d1" % t)
+            quantise_weights("e%d1" % t)
+        one_pass("e", 0, 0, 0)
+        one_pass("e", 0, 1)
+        one_pass("e", 1, 1, 1)
+        one_pass("e", 1, 0)
+        rounded["y", 0, 0] = ring[:, own:], [(n, ("y", n, 0)) for n in range(2)]
+        interleave(on_vector, ring[:, own:], "y", 0, 0, 0, CHUNK)
         evacuate("e", 0)
-        evacuate("e", 1)
-        for i in range(2):
-            round_weights("y", 0, 1, on_vector, (i,))
-        for i in range(2):
-            quantise_weights("y", 0, 1, (i,))
-        product("y", 0, 2, order=(1, 0))
-        product("y", 1, 3, order=(1, 0))
-        for pair in range(2):
-            gather_neighbours(0, (2 * pair, 2 * pair + 1), offset=NEIGHBOURS_0[pair])
-            open_edges(0, pair, 4 + pair)
-        round_weights("e", 1, 0, on_scalar, tag="e010_codes")
-        quantise_weights("e", 1, 0)
+        quantise_weights(("y", 0, 0))
+        open_sums("y", 0, (2, 3))
+        share_rounding("y", 0, 1, True)
+        evacuate("e", 1, offset=behind("y", 0, 1, 2))
+        gather_neighbour(0, 0, offset=behind("y", 0, 0, 0))
+        gather_neighbour(0, 1, offset=behind("y", 0, 0, 1))
+        quantise_weights(("y", 0, 1))
+        close_sums("y", 0)
+        open_edges(0, 0, 4)
+        turn_neighbours(0, 0, True)
+        share_rounding("y", 2, 0, False)
+        gather_neighbour(0, 2, offset=behind("y", 0, 1, 0))
+        gather_neighbour(0, 3, offset=behind("y", 0, 1, 1))
+        quantise_weights(("y", 2, 0))
+        open_sums("y", 2, (0, 1))
+        open_edges(0, 1, 5)
+        turn_neighbours(0, 1, True)
         evacuate("y", 0)
-        gather_neighbours(1, (0, 1), tag="raw_e10")
-        round_weights("e", 1, 1, on_scalar, tag="e011_codes")
-        quantise_weights("e", 1, 1)
-        product("e", 2, 0)
-        product("e", 3, 1)
-        gather_centres(0, offset=CENTRES_0)
-        gather_neighbours(1, (2, 3), offset=NEIGHBOURS_1)
+        share_rounding("y", 2, 1, True)
+        evacuate("y", 1)
+        gather_neighbour(1, 0, offset=behind("y", 2, 0, 0))
+        gather_neighbour(1, 1, offset=behind("y", 2, 0, 1))
+        quantise_weights(("y", 2, 1))
+        close_sums("y", 2)
         open_edges(1, 0, 6)
+        turn_neighbours(1, 0, True)
+        share_rounding("e", 2, 0, False)
+        gather_centres(0, offset=behind("y", 2, 1, 0))
+        gather_centres(1, offset=behind("y", 2, 1, 1))
+        quantise_weights(("e", 2, 0))
+        round_weights("e", (2,), 1, on_scalar, "e21")
+        round_weights("e", (3,), 1, on_scalar, "e31")
         for pair in range(2):
             turn_centres(0, pair, False)
+        open_sums("e", 2, (2, 3))
+        gather_neighbour(1, 2, offset=behind("e", 2, 0, 0))
+        quantise_weights("e21")
+        one_pass("e", 2, 1)
+        gather_neighbour(1, 3, offset=behind("e", 2, 1, 0.5))
+        turn_centres(1, 0, False)
+        quantise_weights("e31")
+        one_pass("e", 3, 1)
+        evacuate("y", 2, offset=behind("e", 2, 1, -1.5))
+        evacuate("y", 3, offset=behind("e", 2, 1, 1.5))
+        evacuate("e", 2)
         open_edges(1, 1, 7)
+        turn_centres(1, 1, True)
+        turn_neighbours(1, 1, False)
+        acts = place([P, 2, 4, 2, LAST, RUN], BF16, "acts", tag="rounded_e21")
 
-
-        for g in range(PASSES):
-            round_weights("y", 1, g, on_scalar)
-            quantise_weights("y", 1, g)
-        product("y", 2, 2)
-        evacuate("y", 1, offset=ROW_Y1)
-        product("y", 3, 3)
-        evacuate("e", 2, offset=ROW_E2)
-        gather_centres(1)
-        for pair in range(2):
-            turn_centres(1, pair, False)
-        acts = place([P, 2, 4, 2, LAST, RUN], BF16, "acts", offset=ACTS)
-
-        def activate(t):
-            for pair in range(2):
+        def activate(t, pairs=(0, 1)):
+            for pair in pairs:
                 gelu_pair(t, pair, acts[:, pair, :, :, t, :])
 
-        activate(0)
-        gather_neighbours(2, (0, 1))
-        gather_neighbours(2, (2, 3))
-        evacuate("y", 2)
-        evacuate("y", 3)
-        evacuate("e", 3, tag="rounded_y110")
-        activate(1)
-        open_edges(2, 0, 0)
-        open_edges(2, 1, 4)
         gather_centres(2)
         gather_centres(3)
-        gather_neighbours(LAST, (0, 1))
         for pair in range(2):
-            turn_centres(2, pair, False)
-        activate(2)
-
-        edges[LAST, 0] = bank([P, 2, 2, P], 5)
+            open_edges(2, pair, pair)
+            turn_centres(2, pair, True)
+        activate(0)
+        evacuate("e", 3)
+        gather_neighbour(2, 0)
+        gather_neighbour(2, 1)
+        turn_neighbours(2, 0, False)
+        activate(1)
+        open_edges(LAST, 0, 2)
         turn_centres(LAST, 0, True)
+        third_sums = bank([P, 2, P], 4)
+        for half in range(2):
+            turn(third_sums[:, half, :], half_of(centres[LAST], half), half == 0, False)
+        fourth_sums = [bank([P, 1, P], (5, 3)[half]) for half in range(2)]
+        for half in range(2):
+            turn(fourth_sums[half][:, 0, :], half_of(centres[LAST], half), True, False)
+        gather_neighbour(2, 2)
+        gather_neighbour(2, 3)
+        turn_neighbours(2, 1, False)
+        gather_neighbour(LAST, 0)
+        gather_neighbour(LAST, 1)
+        activate(2)
         turn_neighbours(LAST, 0, False)
         first_two = place([P, 4, 2, RUN], BF16, "first_two")
         gelu_pair(LAST, 0, first_two[:])
-        gather_neighbours(LAST, (2,))
-        third_sums = bank([P, 2, P], 1)
-        for half in range(2):
-            turn(third_sums[:, half, :], half_of(centres[LAST], half), half == 0, False)
+        gather_neighbour(LAST, 2)
         for half in range(2):
             turn(third_sums[:, half, :], half_of(neighbours[LAST, 2], half), False, half == 1)
         third = sb.tile([P, 2, 2, RUN], BF16, name="third")
@@ -295,17 +343,14 @@ def tile_picked_edgecv_gelu_p_kernel(
             got = place([P, P], F32, "neighbours_last%d" % half)
             entries = pos_lists[3][:, half * (P // 16) : (half + 1) * (P // 16)]
             nc.vector.tensor_copy(got[:], rows["e", LAST][:].indirect(entries))
-            fourth_sums = bank([P, 1, P], 2 + half)
-            turn(fourth_sums[:, 0, :], half_of(centres[LAST], half), True, False)
-            turn(fourth_sums[:, 0, :], got[:], False, True)
+            turn(fourth_sums[half][:, 0, :], got[:], False, True)
             act = place([P, 1, 2, RUN], BF16, "fourth%d" % half)
-            gelu(act[:], fourth_sums[:])
+            gelu(act[:], fourth_sums[half][:])
             fourth.append(act)
 
-
         across = [place([P, 2, 2, LAST * RUN], BF16, "across%d" % half) for half in range(2)]
-        late = [place([P, 2, RUN], BF16, "late%d" % half) for half in range(2)]
         early = sb.tile([P, 2, 2 * RUN], BF16, name="early")
+        late = [place([P, 2, RUN], BF16, "late%d" % half) for half in range(2)]
 
         def across_banks(half):
             flat = [acts[:, pair, 2 * half : 2 * half + 2].rearrange("p a u t c -> p (a u t c)") for pair in range(2)]
@@ -323,12 +368,13 @@ def tile_picked_edgecv_gelu_p_kernel(
         largest(late[0][:], third[:, 0], fourth[0][:, 0])
         within_bank(1)
         largest(late[1][:], third[:, 1], fourth[1][:, 0])
-        round_weights("out", 0, 0, on_scalar, tag="first_two")
-
-
-        z_rounded = []
         for half in range(2):
             largest(z_blocks[half][:, :, LAST, :], early[:, half].rearrange("p (u c) -> p u c", u=2), late[half][:])
+
+        rounded["out", 0, 0] = place([P, CHUNK * PACK], BF16, "rounded_w3", tag="first_two"), [(n, ("out", n, 0)) for n in range(2)]
+        interleave(on_scalar, rounded["out", 0, 0][0][:], "out", 0, 0, 0, CHUNK)
+        z_rounded = []
+        for half in range(2):
             turned = bank([P, 2, P], 6 + half)
             for u in range(2):
                 nc.tensor.transpose(turned[:, u, :], z_words[half][:, u, :], ident[:])
@@ -336,13 +382,14 @@ def tile_picked_edgecv_gelu_p_kernel(
             nc.scalar.copy(tile[:].bitcast(F32).rearrange("p (v u) -> p v u", u=2), turned[:].rearrange("p u v -> p v u"))
             z_rounded.append(tile)
 
-        quantise_weights("out", 0, 0)
+        quantise_weights(("out", 0, 0))
         out_rows = out.rearrange("(m p) v -> p m v", p=P)
+        z_quantised = [quantise(z_rounded[half], "z%d" % half) for half in range(2)]
         for half in range(2):
-            z_codes, z_scales = quantise(z_rounded[half], "z%d" % half)
+            z_codes, z_scales = z_quantised[half]
             result = sb.tile([P, N // P, P], F32, name="result%d" % half)
             for m in range(N // P):
-                acc = bank([P, P], ((0, 4), (5, 1))[half][m])
+                acc = bank([P, P], ((0, 1), (2, 4))[half][m])
                 w3_codes, w3_scales = quantised["out", m, 0]
                 nc.tensor.matmul_mx(
                     out=acc[:],

@@ -29,7 +29,7 @@ RUN = P // 2
 ROW = 4 * S
 MULT, ADD = mybir.AluOpType.mult, mybir.AluOpType.add
 CHUNK = 2 * P
-SHARE = 96
+SHARE = 64
 QUARTER = 4 * V
 ROOM = 8 * QUARTER
 
@@ -253,7 +253,7 @@ def tile_picked_edgecv_gelu_p_kernel(
         quantise_weights(("y", 0, 0))
         open_sums("y", 0, (2, 3))
         share_rounding("y", 0, 1, True)
-        evacuate("e", 1, offset=behind("y", 0, 1, 2))
+        evacuate("e", 1, tag="y00_codes")
         gather_neighbour(0, 0, offset=behind("y", 0, 0, 0))
         gather_neighbour(0, 1, offset=behind("y", 0, 0, 1))
         quantise_weights(("y", 0, 1))
@@ -298,6 +298,8 @@ def tile_picked_edgecv_gelu_p_kernel(
         open_edges(1, 1, 7)
         turn_centres(1, 1, True)
         turn_neighbours(1, 1, False)
+        rounded["out", 0, 0] = place([P, CHUNK * PACK], BF16, "rounded_w3", tag="rounded_e31"), [(n, ("out", n, 0)) for n in range(2)]
+        interleave(on_gpsimd, rounded["out", 0, 0][0][:], "out", 0, 0, 0, CHUNK)
         acts = place([P, 2, 4, 2, LAST, RUN], BF16, "acts", tag="rounded_e21")
 
         def activate(t, pairs=(0, 1)):
@@ -371,8 +373,6 @@ def tile_picked_edgecv_gelu_p_kernel(
         for half in range(2):
             largest(z_blocks[half][:, :, LAST, :], early[:, half].rearrange("p (u c) -> p u c", u=2), late[half][:])
 
-        rounded["out", 0, 0] = place([P, CHUNK * PACK], BF16, "rounded_w3", tag="first_two"), [(n, ("out", n, 0)) for n in range(2)]
-        interleave(on_scalar, rounded["out", 0, 0][0][:], "out", 0, 0, 0, CHUNK)
         z_rounded = []
         for half in range(2):
             turned = bank([P, 2, P], 6 + half)
@@ -382,7 +382,7 @@ def tile_picked_edgecv_gelu_p_kernel(
             nc.scalar.copy(tile[:].bitcast(F32).rearrange("p (v u) -> p v u", u=2), turned[:].rearrange("p u v -> p v u"))
             z_rounded.append(tile)
 
-        quantise_weights(("out", 0, 0))
+        quantise_weights(("out", 0, 0), tag="late0")
         out_rows = out.rearrange("(m p) v -> p m v", p=P)
         z_quantised = [quantise(z_rounded[half], "z%d" % half) for half in range(2)]
         for half in range(2):

@@ -94,18 +94,18 @@ def tile_picked_edgecv_gelu_p_kernel(
         make_identity(nc, ident[:], nomemset=True)
         load_weights("e", (0, 1), 0)
         load_weights("e", (0, 1), 1)
+        load_weights("y", (0, 1), 0)
         pos_lists = [load_list(src, "pos%d_list" % (d + 1)) for d, src in enumerate((pos1, pos2, pos3, pos4))]
-        cen_list = load_list(cen, "cen_list")
 
         both_scales = place([P, S], U8, "both_scales")
         nc.vector.tensor_copy(both_scales[:], x_scale_rows[:].indirect(offs_list[:]))
         nc.sync.dma_start(second_scales[: P - SHIFT, :].bitcast(I32), both_scales[SHIFT:, :].bitcast(I32))
         x_scale_bytes = [both_scales, second_scales]
 
-        load_weights("y", (0, 1), 0)
         load_weights("y", (0, 1), 1)
         load_weights("y", (2, 3), 0)
         load_weights("y", (2, 3), 1)
+        cen_list = load_list(cen, "cen_list")
         load_weights("e", (2, 3), 0)
         load_weights("e", (2,), 1)
         load_weights("e", (3,), 1)
@@ -228,15 +228,8 @@ def tile_picked_edgecv_gelu_p_kernel(
                 dst.rearrange("p a u (q b) -> p u a q b", b=2), src.rearrange("p a (q u b) -> p u a q b", u=2, b=2), GELU
             )
 
-        def gelu_pair(t, pair, dst):
-            gelu(dst, edges[t, pair][:].rearrange("p h i c -> p (h i) c"))
-
         def largest(dst, a, b):
             nc.vector.tensor_tensor(dst, a, b, MAX)
-
-        z = [sb.tile([P, H], BF16, name="z%d" % half) for half in range(2)]
-        z_blocks = [tile[:].rearrange("p (u t c) -> p u t c", u=2, t=TILES) for tile in z]
-        z_words = [tile[:].bitcast(F32).rearrange("p (u w) -> p u w", u=2) for tile in z]
 
         round_weights("e", (0, 1), 0, on_scalar, "e010")
         quantise_weights("e010")
@@ -247,51 +240,55 @@ def tile_picked_edgecv_gelu_p_kernel(
         one_pass("e", 0, 1)
         one_pass("e", 1, 1, 1)
         one_pass("e", 1, 0)
-        rounded["y", 0, 0] = ring[:, own:], [(n, ("y", n, 0)) for n in range(2)]
-        interleave(on_vector, ring[:, own:], "y", 0, 0, 0, CHUNK)
+        round_weights("y", (0,), 0, on_scalar, "y010", 0, 2)
+        round_weights("y", (1,), 0, on_vector, "y010", 1, 2)
+        quantise_weights("y010")
         evacuate("e", 0)
-        quantise_weights(("y", 0, 0))
-        open_sums("y", 0, (2, 3))
-        share_rounding("y", 0, 1, True)
-        evacuate("e", 1, tag="y00_codes")
-        gather_neighbour(0, 0, offset=behind("y", 0, 0, 0))
-        gather_neighbour(0, 1, offset=behind("y", 0, 0, 1))
-        quantise_weights(("y", 0, 1))
-        close_sums("y", 0)
+        evacuate("e", 1)
+        round_weights("y", (0,), 1, on_vector, "y01")
+        rounded["y11"] = ring[:, own : own + WIDTH], [(0, ("y", 1, 1))]
+        interleave(on_vector, ring[:, own : own + WIDTH], "y", 0, 1, P, P)
+        quantise_weights("y01")
+        quantise_weights("y11")
+        for t in range(2):
+            one_pass("y", t, 1, 2 + t)
+            one_pass("y", t, 0)
+        share_rounding("y", 2, 0, True)
+        gather_neighbour(0, 0, offset=behind("y", 0, 1, 0))
+        gather_neighbour(0, 1, offset=behind("y", 0, 1, 1))
+        gather_neighbour(0, 2, offset=behind("y", 0, 1, 2))
         open_edges(0, 0, 4)
         turn_neighbours(0, 0, True)
-        share_rounding("y", 2, 0, False)
-        gather_neighbour(0, 2, offset=behind("y", 0, 1, 0))
-        gather_neighbour(0, 3, offset=behind("y", 0, 1, 1))
         quantise_weights(("y", 2, 0))
         open_sums("y", 2, (0, 1))
-        open_edges(0, 1, 5)
-        turn_neighbours(0, 1, True)
         evacuate("y", 0)
-        share_rounding("y", 2, 1, True)
+        share_rounding("y", 2, 1, False)
         evacuate("y", 1)
-        gather_neighbour(1, 0, offset=behind("y", 2, 0, 0))
-        gather_neighbour(1, 1, offset=behind("y", 2, 0, 1))
+        gather_neighbour(0, 3, offset=behind("y", 2, 0, 0))
+        gather_neighbour(1, 0, offset=behind("y", 2, 0, 1))
         quantise_weights(("y", 2, 1))
         close_sums("y", 2)
-        open_edges(1, 0, 6)
-        turn_neighbours(1, 0, True)
-        share_rounding("e", 2, 0, False)
+        open_edges(0, 1, 5)
+        turn_neighbours(0, 1, True)
+        share_rounding("e", 2, 0, True)
         gather_centres(0, offset=behind("y", 2, 1, 0))
-        gather_centres(1, offset=behind("y", 2, 1, 1))
+        gather_neighbour(1, 1, offset=behind("y", 2, 1, 1))
         quantise_weights(("e", 2, 0))
         round_weights("e", (2,), 1, on_scalar, "e21")
         round_weights("e", (3,), 1, on_scalar, "e31")
         for pair in range(2):
             turn_centres(0, pair, False)
         open_sums("e", 2, (2, 3))
-        gather_neighbour(1, 2, offset=behind("e", 2, 0, 0))
+        open_edges(1, 0, 6)
+        turn_neighbours(1, 0, True)
+        gather_centres(1, offset=behind("e", 2, 0, 0))
         quantise_weights("e21")
         one_pass("e", 2, 1)
-        gather_neighbour(1, 3, offset=behind("e", 2, 1, 0.5))
+        gather_neighbour(1, 2, offset=behind("e", 2, 1, 0.5))
         turn_centres(1, 0, False)
         quantise_weights("e31")
         one_pass("e", 3, 1)
+        gather_neighbour(1, 3, offset=behind("e", 3, 1, 0))
         evacuate("y", 2, offset=behind("e", 2, 1, -1.5))
         evacuate("y", 3, offset=behind("e", 2, 1, 1.5))
         evacuate("e", 2)
@@ -300,23 +297,31 @@ def tile_picked_edgecv_gelu_p_kernel(
         turn_neighbours(1, 1, False)
         rounded["out", 0, 0] = place([P, CHUNK * PACK], BF16, "rounded_w3", tag="rounded_e31"), [(n, ("out", n, 0)) for n in range(2)]
         interleave(on_gpsimd, rounded["out", 0, 0][0][:], "out", 0, 0, 0, CHUNK)
-        acts = place([P, 2, 4, 2, LAST, RUN], BF16, "acts", tag="rounded_e21")
+        firsts = place([P, 4, 2, LAST, RUN], BF16, "firsts", tag="rounded_e21")
+        lasts = [
+            place([P, 2, 2, TILES, RUN], BF16, "lasts%d" % half, tag=("e21_codes", "e21_scales")[half]) for half in range(2)
+        ]
 
-        def activate(t, pairs=(0, 1)):
-            for pair in pairs:
-                gelu_pair(t, pair, acts[:, pair, :, :, t, :])
+        def activate_firsts(t):
+            gelu(firsts[:, :, :, t, :], edges[t, 0][:].rearrange("p h i c -> p (h i) c"))
+
+        def activate_lasts(t):
+            for half in range(2):
+                gelu(lasts[half][:, :, :, t, :], edges[t, 1][:, half])
 
         gather_centres(2)
         gather_centres(3)
         for pair in range(2):
             open_edges(2, pair, pair)
             turn_centres(2, pair, True)
-        activate(0)
+        activate_firsts(0)
+        activate_lasts(0)
         evacuate("e", 3)
-        gather_neighbour(2, 0)
-        gather_neighbour(2, 1)
-        turn_neighbours(2, 0, False)
-        activate(1)
+        gather_neighbour(2, 2)
+        gather_neighbour(2, 3)
+        turn_neighbours(2, 1, False)
+        activate_firsts(1)
+        activate_lasts(1)
         open_edges(LAST, 0, 2)
         turn_centres(LAST, 0, True)
         third_sums = bank([P, 2, P], 4)
@@ -325,21 +330,22 @@ def tile_picked_edgecv_gelu_p_kernel(
         fourth_sums = [bank([P, 1, P], (5, 3)[half]) for half in range(2)]
         for half in range(2):
             turn(fourth_sums[half][:, 0, :], half_of(centres[LAST], half), True, False)
-        gather_neighbour(2, 2)
-        gather_neighbour(2, 3)
-        turn_neighbours(2, 1, False)
+        gather_neighbour(2, 0)
+        gather_neighbour(2, 1)
+        turn_neighbours(2, 0, False)
+        activate_lasts(2)
+        activate_firsts(2)
+
         gather_neighbour(LAST, 0)
         gather_neighbour(LAST, 1)
-        activate(2)
         turn_neighbours(LAST, 0, False)
         first_two = place([P, 4, 2, RUN], BF16, "first_two")
-        gelu_pair(LAST, 0, first_two[:])
+        gelu(first_two[:], edges[LAST, 0][:].rearrange("p h i c -> p (h i) c"))
         gather_neighbour(LAST, 2)
         for half in range(2):
             turn(third_sums[:, half, :], half_of(neighbours[LAST, 2], half), False, half == 1)
-        third = sb.tile([P, 2, 2, RUN], BF16, name="third")
-        gelu(third[:], third_sums[:])
-
+        for half in range(2):
+            gelu(lasts[half][:, :1, :, LAST, :], third_sums[:, half : half + 1, :])
         fourth = []
         for half in range(2):
             got = place([P, P], F32, "neighbours_last%d" % half)
@@ -350,46 +356,60 @@ def tile_picked_edgecv_gelu_p_kernel(
             gelu(act[:], fourth_sums[half][:])
             fourth.append(act)
 
-        across = [place([P, 2, 2, LAST * RUN], BF16, "across%d" % half) for half in range(2)]
-        early = sb.tile([P, 2, 2 * RUN], BF16, name="early")
-        late = [place([P, 2, RUN], BF16, "late%d" % half) for half in range(2)]
+        def turn_back(values, number):
+            words = values.rearrange("p u t c -> p (u t c)").bitcast(F32).rearrange("p (u w) -> p u w", u=2)
+            turned = bank([P, 2, P], number)
+            for u in range(2):
+                nc.tensor.transpose(turned[:, u, :], words[:, u, :], ident[:])
+            return turned
 
-        def across_banks(half):
-            flat = [acts[:, pair, 2 * half : 2 * half + 2].rearrange("p a u t c -> p (a u t c)") for pair in range(2)]
-            largest(across[half][:].rearrange("p i u c -> p (i u c)"), flat[0], flat[1])
+        third_turned = [turn_back(lasts[half][:, 0], 6 + half) for half in range(2)]
 
-        def within_bank(half):
-            dst = z_blocks[half][:, :, :LAST, :].rearrange("p u t c -> p u (t c)")
-            largest(dst, across[half][:, 0], across[half][:, 1])
+
+        of_two = [place([P, 2, LAST * RUN], BF16, "of_two%d" % half) for half in range(2)]
+        early = place([P, 2, 2 * RUN], BF16, "early")
+        of_three = [place([P, 2, TILES, RUN], BF16, "of_three%d" % half) for half in range(2)]
+
+        def first_tiles(ap):
+            return ap[:, :, :LAST, :].rearrange("p u t c -> p u (t c)")
 
         pair_of = first_two[:].rearrange("p (h i) u c -> p i h (u c)", i=2)
         for half in range(2):
-            across_banks(half)
-        within_bank(0)
+            largest(of_two[half][:], first_tiles(firsts[:, 2 * half]), first_tiles(firsts[:, 2 * half + 1]))
+        largest(first_tiles(of_three[0][:]), of_two[0][:], first_tiles(lasts[0][:, 1]))
         largest(early[:], pair_of[:, 0], pair_of[:, 1])
-        largest(late[0][:], third[:, 0], fourth[0][:, 0])
-        within_bank(1)
-        largest(late[1][:], third[:, 1], fourth[1][:, 0])
+        largest(first_tiles(of_three[1][:]), of_two[1][:], first_tiles(lasts[1][:, 1]))
         for half in range(2):
-            largest(z_blocks[half][:, :, LAST, :], early[:, half].rearrange("p (u c) -> p u c", u=2), late[half][:])
+            largest(of_three[half][:, :, LAST, :], early[:, half].rearrange("p (u c) -> p u c", u=2), fourth[half][:, 0])
+        quantise_weights(("out", 0, 0), tag="early")
+
+        third = []
+        for half in range(2):
+            tile = place([P, P * PACK], BF16, "third%d" % half)
+            nc.scalar.copy(
+                tile[:].bitcast(F32).rearrange("p (v u) -> p v u", u=2), third_turned[half][:].rearrange("p u v -> p v u")
+            )
+            third.append(tile)
+
 
         z_rounded = []
         for half in range(2):
-            turned = bank([P, 2, P], 6 + half)
-            for u in range(2):
-                nc.tensor.transpose(turned[:, u, :], z_words[half][:, u, :], ident[:])
+            turned = turn_back(of_three[half][:], (0, 1)[half])
             tile = place([P, P * PACK], BF16, "z_rounded%d" % half)
-            nc.scalar.copy(tile[:].bitcast(F32).rearrange("p (v u) -> p v u", u=2), turned[:].rearrange("p u v -> p v u"))
+            largest(
+                tile[:].rearrange("p (v u b) -> p v u b", u=2, b=2),
+                turned[:].bitcast(BF16).rearrange("p u (v b) -> p v u b", b=2),
+                third[half][:].rearrange("p (v u b) -> p v u b", u=2, b=2),
+            )
             z_rounded.append(tile)
 
-        quantise_weights(("out", 0, 0), tag="late0")
         out_rows = out.rearrange("(m p) v -> p m v", p=P)
         z_quantised = [quantise(z_rounded[half], "z%d" % half) for half in range(2)]
         for half in range(2):
             z_codes, z_scales = z_quantised[half]
             result = sb.tile([P, N // P, P], F32, name="result%d" % half)
             for m in range(N // P):
-                acc = bank([P, P], ((0, 1), (2, 4))[half][m])
+                acc = bank([P, P], ((2, 4), (5, 3))[half][m])
                 w3_codes, w3_scales = quantised["out", m, 0]
                 nc.tensor.matmul_mx(
                     out=acc[:],

@@ -111,9 +111,13 @@ def tile_picked_edgecv_gelu_p_kernel(
         load_weights("e", (3,), 1)
         load_weights("out", (0, 1), 0)
 
-        x_codes = [place([P, S], U16, "x_codes0", tag="x_scale_rows"), place([P, S], U16, "x_codes1")]
-        for g in range(PASSES):
+        x_codes = {}
+
+        def gather_words(g, tag=None, offset=None):
+            x_codes[g] = place([P, S], U16, "x_codes%d" % g, tag=tag, offset=offset)
             nc.vector.tensor_copy(x_codes[g][:], x_word_rows[g][:].indirect(offs_list[:]))
+
+        gather_words(0, tag="x_scale_rows")
 
 
         rounded, quantised, sums, rows, centres, neighbours, edges = {}, {}, {}, {}, {}, {}, {}
@@ -180,6 +184,26 @@ def tile_picked_edgecv_gelu_p_kernel(
                 stop=number is None,
             )
 
+        def first_row(g):
+            codes, scales = quantised["e", 0, g]
+            for n in range(S // P):
+                if g == 0:
+                    sums["e", 0, n] = bank([P, P], (2, 3, 6, 7)[n])
+                nc.tensor.matmul_mx(
+                    out=sums["e", 0, n][:],
+                    lhsT=codes.bitcast(FP8X4),
+                    lhsT_scale=scales,
+                    rhs=x_codes[g][:, n * P : (n + 1) * P].bitcast(FP4X4),
+                    rhs_scale=x_scale_bytes[g][:, n * P : (n + 1) * P],
+                    start=g == 0,
+                    stop=g == 1,
+                )
+
+        def evacuate_first_row():
+            rows["e", 0] = place([P, S], F32, "row_e0", offset=behind("y", 0, 0, 0))
+            for n in range(S // P):
+                nc.scalar.copy(rows["e", 0][:, n * P : (n + 1) * P], sums["e", 0, n][:])
+
         def open_sums(kind, chunk, numbers):
             for n in range(2):
                 one_pass(kind, chunk + n, 0, numbers[n])
@@ -231,64 +255,64 @@ def tile_picked_edgecv_gelu_p_kernel(
         def largest(dst, a, b):
             nc.vector.tensor_tensor(dst, a, b, MAX)
 
-        round_weights("e", (0, 1), 0, on_scalar, "e010")
-        quantise_weights("e010")
-        for t in range(2):
-            round_weights("e", (t,), 1, on_scalar, "e%d1" % t)
-            quantise_weights("e%d1" % t)
-        one_pass("e", 0, 0, 0)
-        one_pass("e", 0, 1)
+        round_weights("e", (0,), 0, on_scalar, "e00")
+        round_weights("e", (1,), 0, on_scalar, "e1", 0, 2)
+        quantise_weights("e00")
+        gather_words(1, offset=behind("e", 0, 0, 0))
+        round_weights("e", (0,), 1, on_scalar, "e01")
+        round_weights("e", (1,), 1, on_scalar, "e1", 1, 2)
+        quantise_weights("e01")
+        quantise_weights("e1")
+        first_row(0)
+        first_row(1)
         one_pass("e", 1, 1, 1)
         one_pass("e", 1, 0)
-        round_weights("y", (0,), 0, on_scalar, "y010", 0, 2)
-        round_weights("y", (1,), 0, on_vector, "y010", 1, 2)
-        quantise_weights("y010")
-        evacuate("e", 0)
-        evacuate("e", 1)
-        round_weights("y", (0,), 1, on_vector, "y01")
-        rounded["y11"] = ring[:, own : own + WIDTH], [(0, ("y", 1, 1))]
-        interleave(on_vector, ring[:, own : own + WIDTH], "y", 0, 1, P, P)
-        quantise_weights("y01")
-        quantise_weights("y11")
-        for t in range(2):
-            one_pass("y", t, 1, 2 + t)
-            one_pass("y", t, 0)
-        share_rounding("y", 2, 0, True)
-        gather_neighbour(0, 0, offset=behind("y", 0, 1, 0))
-        gather_neighbour(0, 1, offset=behind("y", 0, 1, 1))
-        gather_neighbour(0, 2, offset=behind("y", 0, 1, 2))
+        rounded["y", 0, 0] = ring[:, own:], [(n, ("y", n, 0)) for n in range(2)]
+        interleave(on_scalar, ring[:, own : own + WIDTH], "y", 0, 0, 0, P)
+        interleave(on_vector, ring[:, own + WIDTH :], "y", 0, 0, P, P)
+        quantise_weights(("y", 0, 0))
+        evacuate_first_row()
+        open_sums("y", 0, (2, 3))
+        share_rounding("y", 0, 1, True)
+        evacuate("e", 1, offset=behind("y", 0, 1, 2))
+        gather_neighbour(0, 0)
+        gather_neighbour(0, 1)
+        quantise_weights(("y", 0, 1))
+        close_sums("y", 0)
         open_edges(0, 0, 4)
         turn_neighbours(0, 0, True)
+        share_rounding("y", 2, 0, False)
+        gather_neighbour(0, 2, offset=behind("y", 0, 1, 0))
+        gather_neighbour(0, 3, offset=behind("y", 0, 1, 1))
         quantise_weights(("y", 2, 0))
         open_sums("y", 2, (0, 1))
-        evacuate("y", 0)
-        share_rounding("y", 2, 1, False)
-        evacuate("y", 1)
-        gather_neighbour(0, 3, offset=behind("y", 2, 0, 0))
-        gather_neighbour(1, 0, offset=behind("y", 2, 0, 1))
-        quantise_weights(("y", 2, 1))
-        close_sums("y", 2)
         open_edges(0, 1, 5)
         turn_neighbours(0, 1, True)
-        share_rounding("e", 2, 0, True)
-        gather_centres(0, offset=behind("y", 2, 1, 0))
-        gather_neighbour(1, 1, offset=behind("y", 2, 1, 1))
+        evacuate("y", 0)
+        share_rounding("y", 2, 1, True)
+        evacuate("y", 1)
+        gather_neighbour(1, 0, offset=behind("y", 2, 0, 0))
+        gather_centres(0, offset=behind("y", 2, 0, 1))
+        quantise_weights(("y", 2, 1))
+        close_sums("y", 2)
+        for pair in range(2):
+            turn_centres(0, pair, False)
+        share_rounding("e", 2, 0, False)
+        gather_neighbour(1, 1, offset=behind("y", 2, 1, 0))
+        gather_centres(1, offset=behind("y", 2, 1, 1))
         quantise_weights(("e", 2, 0))
         round_weights("e", (2,), 1, on_scalar, "e21")
         round_weights("e", (3,), 1, on_scalar, "e31")
-        for pair in range(2):
-            turn_centres(0, pair, False)
         open_sums("e", 2, (2, 3))
         open_edges(1, 0, 6)
         turn_neighbours(1, 0, True)
-        gather_centres(1, offset=behind("e", 2, 0, 0))
+        gather_neighbour(1, 2, offset=behind("e", 2, 0, 0))
         quantise_weights("e21")
         one_pass("e", 2, 1)
-        gather_neighbour(1, 2, offset=behind("e", 2, 1, 0.5))
+        gather_neighbour(1, 3, offset=behind("e", 2, 1, 0.5))
         turn_centres(1, 0, False)
         quantise_weights("e31")
         one_pass("e", 3, 1)
-        gather_neighbour(1, 3, offset=behind("e", 3, 1, 0))
         evacuate("y", 2, offset=behind("e", 2, 1, -1.5))
         evacuate("y", 3, offset=behind("e", 2, 1, 1.5))
         evacuate("e", 2)
@@ -314,6 +338,8 @@ def tile_picked_edgecv_gelu_p_kernel(
         for pair in range(2):
             open_edges(2, pair, pair)
             turn_centres(2, pair, True)
+        open_edges(LAST, 0, 2)
+        turn_centres(LAST, 0, True)
         activate_firsts(0)
         activate_lasts(0)
         evacuate("e", 3)
@@ -322,8 +348,6 @@ def tile_picked_edgecv_gelu_p_kernel(
         turn_neighbours(2, 1, False)
         activate_firsts(1)
         activate_lasts(1)
-        open_edges(LAST, 0, 2)
-        turn_centres(LAST, 0, True)
         third_sums = bank([P, 2, P], 4)
         for half in range(2):
             turn(third_sums[:, half, :], half_of(centres[LAST], half), half == 0, False)

@@ -15,6 +15,7 @@ U8 = mybir.dt.uint8
 FP8X4 = mybir.dt.float8_e4m3fn_x4
 FP4X4 = mybir.dt.float4_e2m1fn_x4
 GELU = mybir.ActivationFunctionType.Gelu_apprx_tanh
+COPY = mybir.ActivationFunctionType.Copy
 MAX = mybir.AluOpType.max
 
 P = 128
@@ -222,9 +223,12 @@ def tile_picked_edgecv_gelu_p_kernel(
             nc.vector.tensor_copy(got[:], rows["y", t][:].indirect(cen_list[:]))
             centres[t] = got[:]
 
-        def gather_neighbour(t, d, tag=None, offset=None):
+        def gather_neighbour(t, d, tag=None, offset=None, scalar=False):
             got = place([P, V], F32, "neighbours%d%d" % (t, d), tag=tag, offset=offset)
-            nc.vector.tensor_copy(got[:], rows["e", t][:].indirect(pos_lists[d][:]))
+            if scalar:
+                nc.scalar.activation(got[:], rows["e", t][:].indirect(pos_lists[d][:]), COPY)
+            else:
+                nc.vector.tensor_copy(got[:], rows["e", t][:].indirect(pos_lists[d][:]))
             neighbours[t, d] = got[:]
 
         def turn(dst, src, first, final):
@@ -358,10 +362,10 @@ def tile_picked_edgecv_gelu_p_kernel(
         gather_neighbour(2, 1)
         turn_neighbours(2, 0, False)
         activate_lasts(2)
+        gather_neighbour(LAST, 1, scalar=True)
         activate_firsts(2)
 
         gather_neighbour(LAST, 0)
-        gather_neighbour(LAST, 1)
         turn_neighbours(LAST, 0, False)
         first_two = place([P, 4, 2, RUN], BF16, "first_two")
         gelu(first_two[:], edges[LAST, 0][:].rearrange("p h i c -> p (h i) c"))

@@ -73,7 +73,7 @@ def tile_picked_edgecv_gelu_p_kernel(
                 raw[kind, t, g] = tile, n * P
 
         x_scale_rows = place([P, T], U8, "x_scale_rows")
-        nc.vector.memset(x_scale_rows[:].bitcast(I32), 0)
+        nc.gpsimd.memset(x_scale_rows[:].bitcast(I32), 0)
 
         offs_list = load_list(offs, "offs_list")
         x_word_rows = [sb.tile([P, T], U16, name="x_word_rows%d" % g) for g in range(PASSES)]

from contextlib import ExitStack

import concourse.mybir as mybir
from concourse.masks import make_identity

K, T, S, V, H, N = 1024, 1024, 512, 256, 512, 256
FLOPS = 2 * (2 * K * H * S + H * N * V)

F32 = mybir.dt.float32
BF16 = mybir.dt.bfloat16
I32 = mybir.dt.int32
U32 = mybir.dt.uint32
U16 = mybir.dt.uint16
U8 = mybir.dt.uint8
FP8X4 = mybir.dt.float8_e4m3fn_x4
FP4X4 = mybir.dt.float4_e2m1fn_x4
GELU = mybir.ActivationFunctionType.Gelu_apprx_tanh
COPY = mybir.ActivationFunctionType.Copy
MAX = mybir.AluOpType.max

P = 128
PACK = 4
K_PASS = P * PACK
PASSES = K // K_PASS
SCALE_ROWS = 4
SHIFT = 16
TILES = H // P
LAST = TILES - 1
RUN = P // 2
ROW = 4 * S
MULT, ADD = mybir.AluOpType.mult, mybir.AluOpType.add
CHUNK = 2 * P
SHARE = 64
QUARTER = 4 * V
ROOM = 8 * QUARTER


def tile_picked_edgecv_gelu_p_kernel(
    tc, x_words, x_scales, w1, w2, w3, offs, cen, pos1, pos2, pos3, pos4, out
):
    nc = tc.nc
    with ExitStack() as ctx:
        sb = ctx.enter_context(tc.tile_pool(name="sb", bufs=1))
        shared = ctx.enter_context(tc.tile_pool(name="shared", bufs=1))
        ps = ctx.enter_context(tc.psum_pool(name="ps", bufs=1))

        def place(shape, dtype, name, tag=None, offset=None):
            if offset is None:
                return sb.tile(shape, dtype, name=name, tag=tag or name, align_bytes=64)
            return shared.tile(shape, dtype, name=name, offset=offset, align_bytes=64)

        def behind(kind, chunk, g, quarter):
            return raw_offset[kind, chunk, g] + int(quarter * QUARTER)

        def bank(shape, number):
            return ps.tile(shape, F32, name="bank", tag="bank%d" % number)


        def load_list(src, name):
            lst = sb.tile(list(src.shape), U16, name=name)
            nc.sync.dma_start(lst[:], src)
            return lst

        raw, raw_offset = {}, {}

        def load_weights(kind, tiles, g):
            w = {"y": w1, "e": w2, "out": w3}[kind]
            raw_offset[kind, tiles[0], g] = offset = len(raw_offset) * ROOM + 2 * QUARTER
            tile = place([P, PACK, P * len(tiles)], F32, "raw_%s%d%d" % (kind, tiles[0], g), offset=offset)
            rows = w[g * K_PASS : (g + 1) * K_PASS, tiles[0] * P : (tiles[-1] + 1) * P]
            nc.sync.dma_start(tile[:], rows.rearrange("(p j) c -> p j c", j=PACK))
            for n, t in enumerate(tiles):
                raw[kind, t, g] = tile, n * P

        x_scale_rows = place([P, T], U8, "x_scale_rows")
        nc.gpsimd.memset(x_scale_rows[:].bitcast(I32), 0)

        offs_list = load_list(offs, "offs_list")
        x_word_rows = [sb.tile([P, T], U16, name="x_word_rows%d" % g) for g in range(PASSES)]
        nc.sync.dma_start(x_word_rows[0][:].bitcast(I32), x_words[0].bitcast(I32))
        for r in range(SCALE_ROWS):
            (nc.sync, nc.scalar)[r % 2].dma_start(
                x_scale_rows[r:P:SHIFT, :].bitcast(I32),
                x_scales[:, r::SCALE_ROWS, :].rearrange("g q c -> q g c").bitcast(I32),
            )
        warm_in = sb.tile([P, 1], F32, name="warm_in")
        nc.vector.memset(warm_in[:], 0.0)
        warm_out = sb.tile([P, 1], F32, name="warm_out")
        nc.scalar.activation(warm_out[:], warm_in[:], GELU)
        nc.sync.dma_start(x_word_rows[1][:].bitcast(I32), x_words[1].bitcast(I32))
        second_scales = place([P, S], U8, "second_scales")
        nc.vector.memset(second_scales[:].bitcast(I32), 0)
        ident = sb.tile([P, P], F32, name="ident")
        nc.vector.memset(ident[:], 0.0)
        make_identity(nc, ident[:], nomemset=True)
        load_weights("e", (0, 1), 0)
        load_weights("e", (0, 1), 1)
        load_weights("y", (0, 1), 0)
        pos_lists = [load_list(src, "pos%d_list" % (d + 1)) for d, src in enumerate((pos1, pos2, pos3, pos4))]

        both_scales = place([P, S], U8, "both_scales")
        nc.vector.tensor_copy(both_scales[:], x_scale_rows[:].indirect(offs_list[:]))
        nc.sync.dma_start(second_scales[: P - SHIFT, :].bitcast(I32), both_scales[SHIFT:, :].bitcast(I32))
        x_scale_bytes = [both_scales, second_scales]

        load_weights("y", (0, 1), 1)
        load_weights("y", (2, 3), 0)
        load_weights("y", (2, 3), 1)
        cen_list = load_list(cen, "cen_list")
        load_weights("e", (2, 3), 0)
        load_weights("e", (2,), 1)
        load_weights("e", (3,), 1)
        load_weights("out", (0, 1), 0)

        x_codes = {}

        def gather_words(g, tag=None, offset=None):
            x_codes[g] = place([P, S], U16, "x_codes%d" % g, tag=tag, offset=offset)
            nc.vector.tensor_copy(x_codes[g][:], x_word_rows[g][:].indirect(offs_list[:]))

        gather_words(0, tag="x_scale_rows")


        rounded, quantised, sums, rows, centres, neighbours, edges = {}, {}, {}, {}, {}, {}, {}
        on_scalar, on_vector = nc.scalar.copy, nc.vector.tensor_copy
        WIDTH = P * PACK

        def on_gpsimd(dst, src):
            nc.gpsimd.tensor_scalar(
                dst.rearrange("p c j i -> p c i j"), src.rearrange("p c j i -> p c i j"), 1.0, 0.0, MULT, ADD
            )

        def round_weights(kind, tiles, g, copy, key, slot=0, slots=None, tag=None):
            if key not in rounded:
                rounded[key] = place([P, (slots or len(tiles)) * WIDTH], BF16, "rounded_%s" % key, tag=tag), []
            tile, parts = rounded[key]
            source, first = raw[kind, tiles[0], g]
            copy(
                tile[:, slot * WIDTH : (slot + len(tiles)) * WIDTH].rearrange("p (c i j) -> p c j i", i=4, j=PACK),
                source[:, :, first : first + P * len(tiles)].rearrange("p j (c i) -> p c j i", i=4),
            )
            parts.extend((slot + n, (kind, t, g)) for n, t in enumerate(tiles))

        own = (CHUNK - SHARE) * PACK
        ring = place([P, 2 * own + SHARE * PACK], BF16, "ring")

        def interleave(copy, dst, kind, chunk, g, first, count):
            copy(
                dst.rearrange("p (c i j) -> p c j i", i=4, j=PACK),
                raw[kind, chunk, g][0][:, :, first : first + count].rearrange("p j (c i) -> p c j i", i=4),
            )

        def share_rounding(kind, chunk, g, left):
            start = 0 if left else own
            rounded[kind, chunk, g] = ring[:, start : start + CHUNK * PACK], [(n, (kind, chunk + n, g)) for n in range(2)]
            side = ring[:, :own] if left else ring[:, own + SHARE * PACK :]
            interleave(on_scalar, side, kind, chunk, g, 0 if left else SHARE, CHUNK - SHARE)
            interleave(on_gpsimd, ring[:, own : own + SHARE * PACK], kind, chunk, g, CHUNK - SHARE if left else 0, SHARE)

        def quantise(values, name, tag=None):
            width = values.shape[1] // PACK
            codes = place([P, width], U32, name + "_codes", tag=tag)
            scales = place([P, width], U8, name + "_scales")
            nc.vector.quantize_mx(out=codes[:].bitcast(FP8X4), scales=scales[:], in_=values[:])
            return codes, scales

        def quantise_weights(key, tag=None):
            tile, parts = rounded[key]
            codes, scales = quantise(tile, key if isinstance(key, str) else "%s%d%d" % key, tag)
            for slot, which in parts:
                cols = slice(slot * P, (slot + 1) * P)
                quantised[which] = codes[:, cols], scales[:, cols]

        def one_pass(kind, t, g, number=None):
            if number is not None:
                sums[kind, t] = bank([P, S], number)
            codes, scales = quantised[kind, t, g]
            nc.tensor.matmul_mx(
                out=sums[kind, t][:],
                lhsT=codes.bitcast(FP8X4),
                lhsT_scale=scales,
                rhs=x_codes[g][:].bitcast(FP4X4),
                rhs_scale=x_scale_bytes[g][:],
                start=number is not None,
                stop=number is None,
            )

        def first_row(g):
            codes, scales = quantised["e", 0, g]
            for n in range(S // P):
                if g == 0:
                    sums["e", 0, n] = bank([P, P], (2, 3, 6, 7)[n])
                nc.tensor.matmul_mx(
                    out=sums["e", 0, n][:],
                    lhsT=codes.bitcast(FP8X4),
                    lhsT_scale=scales,
                    rhs=x_codes[g][:, n * P : (n + 1) * P].bitcast(FP4X4),
                    rhs_scale=x_scale_bytes[g][:, n * P : (n + 1) * P],
                    start=g == 0,
                    stop=g == 1,
                )

        def evacuate_first_row():
            rows["e", 0] = place([P, S], F32, "row_e0", offset=behind("y", 0, 0, 0))
            for n in range(S // P):
                nc.scalar.copy(rows["e", 0][:, n * P : (n + 1) * P], sums["e", 0, n][:])

        def open_sums(kind, chunk, numbers):
            for n in range(2):
                one_pass(kind, chunk + n, 0, numbers[n])

        def close_sums(kind, chunk):
            for n in range(2):
                one_pass(kind, chunk + n, 1)

        def evacuate(kind, t, tag=None, offset=None):
            row = place([P, S], F32, "row_%s%d" % (kind, t), tag=tag, offset=offset)
            nc.scalar.copy(row[:], sums[kind, t][:])
            rows[kind, t] = row

        def gather_centres(t, tag=None, offset=None):
            got = place([P, V], F32, "centres%d" % t, tag=tag, offset=offset)
            nc.vector.tensor_copy(got[:], rows["y", t][:].indirect(cen_list[:]))
            centres[t] = got[:]

        def gather_neighbour(t, d, tag=None, offset=None, scalar=False):
            got = place([P, V], F32, "neighbours%d%d" % (t, d), tag=tag, offset=offset)
            if scalar:
                nc.scalar.activation(got[:], rows["e", t][:].indirect(pos_lists[d][:]), COPY)
            else:
                nc.vector.tensor_copy(got[:], rows["e", t][:].indirect(pos_lists[d][:]))
            neighbours[t, d] = got[:]

        def turn(dst, src, first, final):
            nc.tensor.matmul(dst, src, ident[:], start=first, stop=final, is_transpose=True)

        def half_of(ap, half):
            return ap[:, half * P : (half + 1) * P]

        slots = [(half, i) for i in range(2) for half in range(2)]

        def turn_centres(t, pair, first):
            for n, (half, i) in enumerate(slots):
                turn(edges[t, pair][:, half, i, :], half_of(centres[t], half), first and n == 0, not first and n == 3)

        def turn_neighbours(t, pair, first):
            for n, (half, i) in enumerate(slots):
                src = half_of(neighbours[t, 2 * pair + i], half)
                turn(edges[t, pair][:, half, i, :], src, first and n == 0, not first and n == 3)

        def open_edges(t, pair, number):
            edges[t, pair] = bank([P, 2, 2, P], number)

        def gelu(dst, src):
            nc.scalar.activation(
                dst.rearrange("p a u (q b) -> p u a q b", b=2), src.rearrange("p a (q u b) -> p u a q b", u=2, b=2), GELU
            )

        def largest(dst, a, b):
            nc.vector.tensor_tensor(dst, a, b, MAX)

        round_weights("e", (0,), 0, on_scalar, "e00")
        round_weights("e", (1,), 0, on_scalar, "e1", 0, 2)
        quantise_weights("e00")
        gather_words(1, offset=behind("e", 0, 0, 0))
        round_weights("e", (0,), 1, on_scalar, "e01")
        round_weights("e", (1,), 1, on_scalar, "e1", 1, 2)
        quantise_weights("e01")
        quantise_weights("e1")
        first_row(0)
        first_row(1)
        one_pass("e", 1, 1, 1)
        one_pass("e", 1, 0)
        rounded["y", 0, 0] = ring[:, own:], [(n, ("y", n, 0)) for n in range(2)]
        interleave(on_scalar, ring[:, own : own + WIDTH], "y", 0, 0, 0, P)
        interleave(on_vector, ring[:, own + WIDTH :], "y", 0, 0, P, P)
        quantise_weights(("y", 0, 0))
        evacuate_first_row()
        open_sums("y", 0, (2, 3))
        share_rounding("y", 0, 1, True)
        evacuate("e", 1, offset=behind("y", 0, 1, 2))
        gather_neighbour(0, 0)
        gather_neighbour(0, 1)
        quantise_weights(("y", 0, 1))
        close_sums("y", 0)
        open_edges(0, 0, 4)
        turn_neighbours(0, 0, True)
        share_rounding("y", 2, 0, False)
        gather_neighbour(0, 2, offset=behind("y", 0, 1, 0))
        gather_neighbour(0, 3, offset=behind("y", 0, 1, 1))
        quantise_weights(("y", 2, 0))
        open_sums("y", 2, (0, 1))
        open_edges(0, 1, 5)
        turn_neighbours(0, 1, True)
        evacuate("y", 0)
        share_rounding("y", 2, 1, True)
        evacuate("y", 1)
        gather_neighbour(1, 0, offset=behind("y", 2, 0, 0))
        gather_centres(0, offset=behind("y", 2, 0, 1))
        quantise_weights(("y", 2, 1))
        close_sums("y", 2)
        for pair in range(2):
            turn_centres(0, pair, False)
        share_rounding("e", 2, 0, False)
        gather_neighbour(1, 1, offset=behind("y", 2, 1, 0))
        gather_centres(1, offset=behind("y", 2, 1, 1))
        quantise_weights(("e", 2, 0))
        round_weights("e", (2,), 1, on_scalar, "e21")
        round_weights("e", (3,), 1, on_scalar, "e31")
        open_sums("e", 2, (2, 3))
        open_edges(1, 0, 6)
        turn_neighbours(1, 0, True)
        gather_neighbour(1, 2, offset=behind("e", 2, 0, 0))
        quantise_weights("e21")
        one_pass("e", 2, 1)
        gather_neighbour(1, 3, offset=behind("e", 2, 1, 0.5))
        turn_centres(1, 0, False)
        quantise_weights("e31")
        one_pass("e", 3, 1)
        evacuate("y", 2, offset=behind("e", 2, 1, -1.5))
        evacuate("y", 3, offset=behind("e", 2, 1, 1.5))
        evacuate("e", 2)
        open_edges(1, 1, 7)
        turn_centres(1, 1, True)
        turn_neighbours(1, 1, False)
        rounded["out", 0, 0] = place([P, CHUNK * PACK], BF16, "rounded_w3", tag="rounded_e31"), [(n, ("out", n, 0)) for n in range(2)]
        interleave(on_gpsimd, rounded["out", 0, 0][0][:], "out", 0, 0, 0, CHUNK)
        firsts = place([P, 4, 2, LAST, RUN], BF16, "firsts", tag="rounded_e21")
        lasts = [
            place([P, 2, 2, TILES, RUN], BF16, "lasts%d" % half, tag=("e21_codes", "e21_scales")[half]) for half in range(2)
        ]

        def activate_firsts(t):
            gelu(firsts[:, :, :, t, :], edges[t, 0][:].rearrange("p h i c -> p (h i) c"))

        def activate_lasts(t):
            for half in range(2):
                gelu(lasts[half][:, :, :, t, :], edges[t, 1][:, half])

        gather_centres(2)
        gather_centres(3)
        for pair in range(2):
            open_edges(2, pair, pair)
            turn_centres(2, pair, True)
        open_edges(LAST, 0, 2)
        turn_centres(LAST, 0, True)
        activate_firsts(0)
        activate_lasts(0)
        evacuate("e", 3)
        gather_neighbour(2, 2)
        gather_neighbour(2, 3)
        turn_neighbours(2, 1, False)
        activate_firsts(1)
        activate_lasts(1)
        third_sums = bank([P, 2, P], 4)
        for half in range(2):
            turn(third_sums[:, half, :], half_of(centres[LAST], half), half == 0, False)
        fourth_sums = [bank([P, 1, P], (5, 3)[half]) for half in range(2)]
        for half in range(2):
            turn(fourth_sums[half][:, 0, :], half_of(centres[LAST], half), True, False)
        gather_neighbour(2, 0)
        gather_neighbour(2, 1)
        turn_neighbours(2, 0, False)
        activate_lasts(2)
        gather_neighbour(LAST, 1, scalar=True)
        activate_firsts(2)

        gather_neighbour(LAST, 0)
        turn_neighbours(LAST, 0, False)
        first_two = place([P, 4, 2, RUN], BF16, "first_two")
        gelu(first_two[:], edges[LAST, 0][:].rearrange("p h i c -> p (h i) c"))
        gather_neighbour(LAST, 2)
        for half in range(2):
            turn(third_sums[:, half, :], half_of(neighbours[LAST, 2], half), False, half == 1)
        for half in range(2):
            gelu(lasts[half][:, :1, :, LAST, :], third_sums[:, half : half + 1, :])
        fourth = []
        for half in range(2):
            got = place([P, P], F32, "neighbours_last%d" % half)
            entries = pos_lists[3][:, half * (P // 16) : (half + 1) * (P // 16)]
            nc.vector.tensor_copy(got[:], rows["e", LAST][:].indirect(entries))
            turn(fourth_sums[half][:, 0, :], got[:], False, True)
            act = place([P, 1, 2, RUN], BF16, "fourth%d" % half)
            gelu(act[:], fourth_sums[half][:])
            fourth.append(act)

        def turn_back(values, number):
            words = values.rearrange("p u t c -> p (u t c)").bitcast(F32).rearrange("p (u w) -> p u w", u=2)
            turned = bank([P, 2, P], number)
            for u in range(2):
                nc.tensor.transpose(turned[:, u, :], words[:, u, :], ident[:])
            return turned

        third_turned = [turn_back(lasts[half][:, 0], 6 + half) for half in range(2)]


        of_two = [place([P, 2, LAST * RUN], BF16, "of_two%d" % half) for half in range(2)]
        early = place([P, 2, 2 * RUN], BF16, "early")
        of_three = [place([P, 2, TILES, RUN], BF16, "of_three%d" % half) for half in range(2)]

        def first_tiles(ap):
            return ap[:, :, :LAST, :].rearrange("p u t c -> p u (t c)")

        pair_of = first_two[:].rearrange("p (h i) u c -> p i h (u c)", i=2)
        for half in range(2):
            largest(of_two[half][:], first_tiles(firsts[:, 2 * half]), first_tiles(firsts[:, 2 * half + 1]))
        largest(first_tiles(of_three[0][:]), of_two[0][:], first_tiles(lasts[0][:, 1]))
        largest(early[:], pair_of[:, 0], pair_of[:, 1])
        largest(first_tiles(of_three[1][:]), of_two[1][:], first_tiles(lasts[1][:, 1]))
        for half in range(2):
            largest(of_three[half][:, :, LAST, :], early[:, half].rearrange("p (u c) -> p u c", u=2), fourth[half][:, 0])
        quantise_weights(("out", 0, 0), tag="early")

        third = []
        for half in range(2):
            tile = place([P, P * PACK], BF16, "third%d" % half)
            nc.scalar.copy(
                tile[:].bitcast(F32).rearrange("p (v u) -> p v u", u=2), third_turned[half][:].rearrange("p u v -> p v u")
            )
            third.append(tile)


        z_rounded = []
        for half in range(2):
            turned = turn_back(of_three[half][:], (0, 1)[half])
            tile = place([P, P * PACK], BF16, "z_rounded%d" % half)
            largest(
                tile[:].rearrange("p (v u b) -> p v u b", u=2, b=2),
                turned[:].bitcast(BF16).rearrange("p u (v b) -> p v u b", b=2),
                third[half][:].rearrange("p (v u b) -> p v u b", u=2, b=2),
            )
            z_rounded.append(tile)

        out_rows = out.rearrange("(m p) v -> p m v", p=P)
        z_quantised = [quantise(z_rounded[half], "z%d" % half) for half in range(2)]
        for half in range(2):
            z_codes, z_scales = z_quantised[half]
            result = sb.tile([P, N // P, P], F32, name="result%d" % half)
            for m in range(N // P):
                acc = bank([P, P], ((2, 4), (5, 3))[half][m])
                w3_codes, w3_scales = quantised["out", m, 0]
                nc.tensor.matmul_mx(
                    out=acc[:],
                    lhsT=w3_codes.bitcast(FP8X4),
                    lhsT_scale=w3_scales,
                    rhs=z_codes[:].bitcast(FP8X4),
                    rhs_scale=z_scales[:],
                    start=True,
                    stop=True,
                )
                if m == 0:
                    nc.vector.tensor_copy(result[:, m, :], acc[:])
                else:
                    nc.scalar.copy(result[:, m, :], acc[:])
            nc.sync.dma_start(out_rows[:, :, half * P : (half + 1) * P], result[:])
